import numpy as np
import ml_dtypes


def mxq(x, axis, fmt="e4m3"):
    dtype, down = {"e4m3": (ml_dtypes.float8_e4m3fn, 7), "e5m2": (ml_dtypes.float8_e5m2, 14)}[fmt]
    v = np.moveaxis(np.asarray(x, np.float32).astype(ml_dtypes.bfloat16).astype(np.float64), axis, -1)
    blocks = v.reshape(v.shape[:-1] + (-1, 32))
    amax = np.abs(blocks).max(-1, keepdims=True)
    byte = np.maximum(np.where(amax > 0, np.frexp(amax)[1] - 1 + 127, 0) - down, 1)
    scale = np.exp2(byte - 127.0)
    codes = (blocks / scale).astype(np.float32).astype(dtype).astype(np.float64)
    return np.moveaxis((codes * scale).reshape(v.shape), -1, axis)


WIDE = False


def mx_kscale(k):
    if not WIDE:
        return np.ones(k)
    levels = np.array([10, -10, 5, -5, 0])
    if k % 512:
        return np.exp2(np.random.permutation(np.resize(levels, k // 32))).repeat(32)
    a = np.empty((k // 512, 16))
    for p in range(k // 512):
        a[p, :8] = np.random.permutation(np.resize(levels, 8))
        for g in range(8):
            far = levels[np.abs(levels - a[p, g]) >= 10]
            a[p, g + 8] = far[np.random.randint(len(far))]
    return np.exp2(a.ravel()).repeat(32)


def f64(x):
    return np.asarray(x).astype(np.float64)


def striped(idx):
    return np.tile(idx.reshape(-1, 16).T, (8, 1)).astype(np.uint16)


def unstriped(offs):
    return offs[:16].T.reshape(-1).astype(np.int64)


E2M1 = np.array([0.0, 0.5, 1.0, 1.5, 2.0, 3.0, 4.0, 6.0, -0.0, -0.5, -1.0, -1.5, -2.0, -3.0, -4.0, -6.0])


def pack_weight(w, fmt):
    k, n = w.shape
    w = f64(np.asarray(w, np.float32).astype(ml_dtypes.bfloat16)).reshape(k // 32, 32, n)
    amax = np.abs(w).max(1)
    if fmt == "e4m3":
        byte = np.frexp(amax)[1] - 1 + 127 - 7
    else:
        mant, ex = np.frexp(amax / 6.0)
        byte = np.where(mant > 0.5, ex, ex - 1) + 127
    byte = np.clip(np.where(amax > 0, byte, 1), 1, 254)
    scaled = (w * np.exp2(127.0 - byte)[:, None, :]).reshape(k, n).astype(np.float32)
    by_word = np.ascontiguousarray(scaled.reshape(k // 512, 128, 4, n).transpose(0, 1, 3, 2))
    if fmt == "e4m3":
        words = by_word.astype(ml_dtypes.float8_e4m3fn).view(np.uint8)
    else:
        c = by_word.astype(ml_dtypes.float4_e2m1fn).view(np.uint8) & 0xF
        words = (c[..., 0::2] | (c[..., 1::2] << 4)).reshape(k // 512, 128, 2 * n)
    return np.ascontiguousarray(words), np.ascontiguousarray(byte.astype(np.uint8).reshape(k // 512, 16, n))


def unpack_weight(words, scales, fmt):
    g, _, n = scales.shape
    words = np.ascontiguousarray(words).reshape(g, 128, n, -1)
    if fmt == "e4m3":
        vals = words.view(ml_dtypes.float8_e4m3fn).astype(np.float64)
    else:
        nib = np.empty((g, 128, n, 4), np.uint8)
        nib[..., 0::2] = words & 0xF
        nib[..., 1::2] = words >> 4
        vals = E2M1[nib]
    vals = vals * np.repeat(np.exp2(scales.astype(np.float64) - 127.0), 8, axis=1)[..., None]
    return vals.transpose(0, 1, 3, 2).reshape(g * 512, n)


def gelu(v):
    return 0.5 * v * (1.0 + np.tanh(np.sqrt(2.0 / np.pi) * (v + 0.044715 * v**3)))


K, K2, T, T2, S, P, H, N = 1024, 512, 2048, 2048, 1024, 1024, 1024, 512

def setup_inputs():
    n = np.random.standard_normal
    s = mx_kscale(K)[:, None]
    s2 = mx_kscale(K2)[:, None]
    u = mx_kscale(H)[:, None]
    tab_words, tab_scales = pack_weight(n((K, T)) * s, "e4m3")
    w2_words, w2_scales = pack_weight(n((K, H)) * 0.8 / np.sqrt(K) / s * u.T, "e2m1")
    w3_words, w3_scales = pack_weight(n((H, N)) * 0.7 / np.sqrt(H) / u, "e4m3")
    return {
        "tab_words": tab_words, "tab_scales": tab_scales,
        "offs": striped(np.random.permutation(T)[:P]),
        "offs2": striped(np.random.permutation(T2)[:S]),
        "offs3": striped(np.random.permutation(T2)[:P]),
        "base": (n((K2, T2)) * s2).astype(np.float32),
        "xs": (np.round(16 * n((K2, S))) / 16 * s2).astype(np.float32),
        "w1": (n((K2, H)) * 0.6 / np.sqrt(K2) / s2 / u.T).astype(np.float32),
        "w2_words": w2_words, "w2_scales": w2_scales,
        "w3_words": w3_words, "w3_scales": w3_scales,
        "trim": (0.5 * n(N)).astype(np.float32),
    }

def reference(tab_words, tab_scales, offs, offs2, offs3, base, xs, w1, w2_words, w2_scales, w3_words, w3_scales, trim):
    page = f64(base).copy()
    page[:, unstriped(offs2)] = f64(xs)
    a = mxq(f64(w1), 0, "e4m3").T @ mxq(page, 0, "e4m3")
    ad = a[:, unstriped(offs3)]
    v = unpack_weight(tab_words, tab_scales, "e4m3")[:, unstriped(offs)]
    b = unpack_weight(w2_words, w2_scales, "e2m1").T @ v
    z = b * (2.0 - ad * b)
    y = unpack_weight(w3_words, w3_scales, "e4m3").T @ mxq(z, 0, "e4m3")
    return y + f64(trim)[:, None]

@@ -1,0 +1,303 @@
+from contextlib import ExitStack
+
+import concourse.mybir as mybir
+
+F32 = mybir.dt.float32
+BF16 = mybir.dt.bfloat16
+I32 = mybir.dt.int32
+U32 = mybir.dt.uint32
+U16 = mybir.dt.uint16
+U8 = mybir.dt.uint8
+FP8X4 = mybir.dt.float8_e4m3fn_x4
+FP4X4 = mybir.dt.float4_e2m1fn_x4
+ALU = mybir.AluOpType
+ACT = mybir.ActivationFunctionType
+
+P = 128
+PACK = 4
+T = 2048
+S = 1024
+H = 1024
+N = 512
+BANK = 512
+GROUP = 16
+FLOPS = 2 * (512 * H * T + 1024 * H * S + H * N * S)
+
+
+def tile_list_newton_clock_step_kernel(
+    tc, tab_words, tab_scales, offs, offs2, offs3, base, xs, w1, w2_words, w2_scales, w3_words, w3_scales, trim, out
+):
+    nc = tc.nc
+    with ExitStack() as ctx:
+        lists = ctx.enter_context(tc.tile_pool(name="lists", bufs=1))
+        held = ctx.enter_context(tc.tile_pool(name="held", bufs=1))
+        psum = ctx.enter_context(tc.psum_pool(name="psum", bufs=1))
+
+        def sb(shape, dtype, tag, bufs=1):
+            return held.tile(shape, dtype, name=tag, tag=tag, bufs=bufs, align_bytes=64)
+
+        banks_taken = []
+
+        def bank():
+            tag = "bank%d" % (len(banks_taken) % 8)
+            banks_taken.append(tag)
+            return psum.tile([P, BANK], F32, name=tag, tag=tag)
+
+        def words(ap):
+            return ap.bitcast(I32)
+
+        idx = lists.tile([P, S // GROUP], U16, name="idx")
+        idx2 = lists.tile([P, S // GROUP], U16, name="idx2")
+        idx3 = lists.tile([P, S // GROUP], U16, name="idx3")
+
+        tab_sc = sb([P, T], U8, "tab_sc")
+        w2_sc_raw = sb([P, 2 * H], U8, "w2_sc_raw")
+        w3_sc = sb([P, 2 * N], U8, "w3_sc")
+        v_sc1 = sb([P, S], U8, "v_sc1")
+        for plane in (w2_sc_raw, tab_sc, w3_sc, v_sc1):
+            nc.vector.memset(words(plane[:]), 0)
+
+        page = [sb([P, T], F32, "wide%d" % t) for t in range(PACK)]
+        w1_raw = [sb([P, PACK * BANK], F32, "wide%d" % (4 + g)) for g in range(2)]
+        tab = [sb([P, T], U32, "wide%d" % (6 + a)) for a in range(2)]
+        w2_raw = sb([P, 2 * 2 * H], U8, "w2_raw")
+        w3 = sb([P, 2 * N], U32, "w3")
+        trim_sb = sb([P, N // P], F32, "trim")
+        page_pairs = [sb([P, PACK * BANK], BF16, "pairs%d" % c) for c in range(4)]
+        page_quads = [sb([P, PACK * BANK], BF16, "quads%d" % c) for c in range(4)]
+        w1_quads = [sb([P, PACK * BANK], BF16, "w1_quads%d" % g) for g in range(2)]
+
+        w2 = sb([P, 2 * 2 * H], U8, "w2")
+        w2_sc = sb([P, 2 * H], U8, "w2_sc")
+        v_sc = sb([P, S], U8, "v_sc")
+        v_early = [sb([P, BANK], U32, "v_early%d" % a) for a in range(2)]
+        b_pairs = [sb([P, 2 * S], F32, "b%d" % k) for k in range(4)]
+
+        def pick_words(picked_words, a, h):
+            at = h * BANK // GROUP
+            nc.vector.tensor_copy(picked_words[:], tab[a][:].indirect(idx[:, at : at + BANK // GROUP]))
+
+        def estimate(v, s, h):
+            cols = slice(h * BANK, (h + 1) * BANK)
+            acc = bank()
+            for a in range(2):
+                lo = a * H + s * P
+                nc.tensor.matmul_mx(
+                    acc[:], lhsT=w2[:, 2 * lo : 2 * (lo + P)].bitcast(FP4X4), lhsT_scale=w2_sc[:, lo : lo + P],
+                    rhs=v[a][:].bitcast(FP8X4), rhs_scale=(v_sc, v_sc1)[a][:, cols], start=a == 0, stop=a == 1,
+                )
+            lo = (s % 2) * S + h * BANK
+            nc.scalar.copy(b_pairs[s // 2][:, lo : lo + BANK], acc[:])
+
+        base_planes = base.rearrange("(p t) c -> t p c", t=PACK)
+        xs_planes = xs.rearrange("(p t) j -> t p j", t=PACK)
+        w1_rows = w1.rearrange("(p t) r -> p t r", t=PACK)
+
+        with tc.tile_pool(name="arrivals", bufs=1) as arrivals:
+            blocks = [arrivals.tile([P, S], F32, name="xs%d" % t, align_bytes=64) for t in range(PACK)]
+
+            def load_plane(t):
+                nc.sync.dma_start(page[t][:], base_planes[t])
+                nc.sync.dma_start(blocks[t][:], xs_planes[t])
+
+            def load_table(a):
+                nc.sync.dma_start(words(tab[a][:]), words(tab_words[a].rearrange("p t i -> p (t i)")))
+
+            def load_w1(g):
+                nc.sync.dma_start(
+                    w1_raw[g][:].rearrange("p (t r) -> p t r", t=PACK), w1_rows[:, :, g * BANK : (g + 1) * BANK]
+                )
+
+            def place(t):
+                nc.vector.tensor_copy(page[t][:].indirect(idx2[:]), blocks[t][:])
+                for c in range(4):
+                    nc.scalar.copy(
+                        page_pairs[c][:].rearrange("p (u c e) -> p u c e", u=2, e=2)[:, t // 2, :, t % 2],
+                        page[t][:, c * BANK : (c + 1) * BANK],
+                    )
+
+            def round_w1(g):
+                nc.scalar.activation(
+                    w1_quads[g][:].rearrange("p (t m j) -> p m t j", t=PACK, j=PACK),
+                    w1_raw[g][:].rearrange("p (j m t) -> p m t j", j=PACK, t=PACK),
+                    ACT.Copy,
+                )
+
+            nc.sync.dma_start(
+                words(w2_raw[:]).rearrange("p (a c) -> p a c", a=2), words(w2_words).rearrange("a p c -> p a c")
+            )
+            for q in range(4):
+                nc.sync.dma_start(
+                    words(w2_sc_raw[32 * q : 32 * q + 4, :]).rearrange("r (a c) -> r a c", a=2),
+                    words(w2_scales[:, 4 * q : 4 * q + 4, :]).rearrange("a r c -> r a c"),
+                )
+            nc.sync.dma_start(idx2[:], offs2)
+            load_plane(0)
+            load_w1(0)
+            load_plane(1)
+            load_w1(1)
+            nc.sync.dma_start(idx[:], offs)
+            for q in range(4):
+                nc.sync.dma_start(words(tab_sc[32 * q : 32 * q + 8, :]), words(tab_scales[:, 4 * q : 4 * q + 4, :]))
+            load_table(0)
+            load_table(1)
+            load_plane(2)
+            load_plane(3)
+            nc.sync.dma_start(idx3[:], offs3)
+            nc.sync.dma_start(
+                words(w3[:]).rearrange("p (a c) -> p a c", a=2),
+                words(w3_words.rearrange("a p c i -> a p (c i)")).rearrange("a p c -> p a c"),
+            )
+            for q in range(4):
+                nc.sync.dma_start(
+                    words(w3_sc[32 * q : 32 * q + 4, :]).rearrange("r (a c) -> r a c", a=2),
+                    words(w3_scales[:, 4 * q : 4 * q + 4, :]).rearrange("a r c -> r a c"),
+                )
+            with nc.allow_non_contiguous_dma(reason="one trim value a partition"):
+                nc.sync.dma_start(trim_sb[:], trim.rearrange("(c p) -> p c", p=P))
+
+            nc.vector.tensor_copy(
+                w2[:].bitcast(U16).rearrange("p (x t m) -> p x t m", t=PACK, m=P),
+                w2_raw[:].bitcast(U16).rearrange("p (x m t) -> p x t m", t=PACK, m=P),
+            )
+            nc.vector.tensor_copy(
+                w2_sc[:].rearrange("p (x t m) -> p x t m", t=PACK, m=P),
+                w2_sc_raw[:].rearrange("p (x m t) -> p x t m", t=PACK, m=P),
+            )
+            place(0)
+            round_w1(0)
+            place(1)
+            round_w1(1)
+            nc.vector.tensor_copy(v_sc[:], tab_sc[:].indirect(idx[:]))
+            for q in range(4):
+                nc.sync.dma_start(words(v_sc1[32 * q : 32 * q + 4, :]), words(v_sc[32 * q + 4 : 32 * q + 8, :]))
+            for a in range(2):
+                pick_words(v_early[a], a, 0)
+            for s in range(8):
+                estimate(v_early, s, 0)
+            place(2)
+            place(3)
+
+        picked = ctx.enter_context(tc.tile_pool(name="picked", bufs=1))
+        v_late = [picked.tile([P, BANK], U32, name="v_late%d" % a, align_bytes=64) for a in range(2)]
+        w1_codes = picked.tile([P, H], U32, name="w1_codes", align_bytes=64)
+        w1_sc = sb([P, H], U8, "w1_sc")
+        page_codes = sb([P, T], U32, "page_codes")
+        page_sc = sb([P, T], U8, "page_sc")
+
+        def weave_page(c):
+            nc.vector.tensor_copy(
+                page_quads[c][:].bitcast(F32).rearrange("p (c u) -> p c u", u=2),
+                page_pairs[c][:].bitcast(F32).rearrange("p (u c) -> p c u", u=2),
+            )
+
+        def quantise_page(c):
+            cols = slice(c * BANK, (c + 1) * BANK)
+            nc.vector.quantize_mx(page_codes[:, cols].bitcast(FP8X4), page_sc[:, cols], page_quads[c][:])
+
+        def quantise_w1(g):
+            cols = slice(g * BANK, (g + 1) * BANK)
+            nc.vector.quantize_mx(w1_codes[:, cols].bitcast(FP8X4), w1_sc[:, cols], w1_quads[g][:])
+
+        quantise_w1(0)
+        weave_page(0)
+        quantise_w1(1)
+        for c in range(1, 4):
+            weave_page(c)
+            quantise_page(c - 1)
+        quantise_page(3)
+        for a in range(2):
+            pick_words(v_late[a], a, 1)
+
+        neg_a = []
+        for s in range(8):
+            rows = slice(s * P, (s + 1) * P)
+            neg_a.append(sb([P, T], F32, "wide%d" % s))
+            for c in range(4):
+                cols = slice(c * BANK, (c + 1) * BANK)
+                acc = bank()
+                nc.tensor.matmul_mx(
+                    acc[:], lhsT=w1_codes[:, rows].bitcast(FP8X4), lhsT_scale=w1_sc[:, rows],
+                    rhs=page_codes[:, cols].bitcast(FP8X4), rhs_scale=page_sc[:, cols], start=True, stop=True,
+                )
+                nc.scalar.activation(neg_a[s][:, cols], acc[:], ACT.Copy, scale=-1.0)
+            estimate(v_late, s, 1)
+
+        z_codes = [sb([P, S], U32, "z_codes%d" % g) for g in range(2)]
+        z_sc = [sb([P, S], U8, "z_sc%d" % g) for g in range(2)]
+        out_rows = out.rearrange("(c p) j -> p c j", p=P)
+
+        def pick_product(prod, s, lo, hi):
+            at = (s % 2) * S
+            nc.vector.tensor_tensor(
+                prod[:, at + lo : at + hi],
+                neg_a[s][:].indirect(idx3[:, lo // GROUP : hi // GROUP]),
+                b_pairs[s // 2][:, at + lo : at + hi],
+                ALU.mult,
+            )
+
+        def newton(z_pairs, prod, k, lo, hi):
+            nc.vector.scalar_tensor_tensor(
+                z_pairs[:].rearrange("p (u j e) -> p u j e", u=2, e=2)[:, k % 2],
+                prod[:].rearrange("p (e j) -> p j e", e=2)[:, lo:hi, :],
+                2.0,
+                b_pairs[k][:].rearrange("p (e j) -> p j e", e=2)[:, lo:hi, :],
+                ALU.add,
+                ALU.mult,
+            )
+
+        def quantise_z(z_pairs, tag, g, lo, hi, weave):
+            quads = sb([P, PACK * (hi - lo)], BF16, tag)
+            weave(
+                quads[:].bitcast(F32).rearrange("p (j u) -> p j u", u=2),
+                z_pairs[:].bitcast(F32).rearrange("p (u j) -> p j u", u=2),
+            )
+            nc.vector.quantize_mx(z_codes[g][:, lo:hi].bitcast(FP8X4), z_sc[g][:, lo:hi], quads[:])
+
+        def project(acc, g, c, lo, hi):
+            at = g * N + c * P
+            nc.tensor.matmul_mx(
+                acc[:, : hi - lo], lhsT=w3[:, at : at + P].bitcast(FP8X4), lhsT_scale=w3_sc[:, at : at + P],
+                rhs=z_codes[g][:, lo:hi].bitcast(FP8X4), rhs_scale=z_sc[g][:, lo:hi], start=g == 0, stop=g == 1,
+            )
+
+        halves = [(0, BANK), (BANK, S)]
+        pieces = [(0, 512), (512, 768), (768, 1024)]
+
+        z_first = [sb([P, PACK * BANK], BF16, "pairs%d" % h) for h in range(2)]
+        for k in range(2):
+            prod = sb([P, 2 * S], F32, "prod", bufs=2)
+            for s in (2 * k, 2 * k + 1):
+                for lo, hi in halves if s == 0 else [(0, S)]:
+                    pick_product(prod, s, lo, hi)
+            for h, (lo, hi) in enumerate(halves):
+                newton(z_first[h], prod, k, lo, hi)
+        for h, (lo, hi) in enumerate(halves):
+            quantise_z(z_first[h], "quads%d" % h, 0, lo, hi, nc.scalar.copy)
+
+        z_second = [sb([P, PACK * (hi - lo)], BF16, ("pairs2", "pairs3", "w1_quads0")[i]) for i, (lo, hi) in enumerate(pieces)]
+        prod = sb([P, 2 * S], F32, "prod", bufs=2)
+        for s in (4, 5):
+            pick_product(prod, s, 0, S)
+        for i, (lo, hi) in enumerate(pieces):
+            newton(z_second[i], prod, 2, lo, hi)
+        prod = sb([P, 2 * S], F32, "prod", bufs=2)
+        for i, (lo, hi) in enumerate(pieces):
+            last = i == len(pieces) - 1
+            accs = [bank() for c in range(4)]
+            for c in range(4):
+                project(accs[c], 0, c, lo, hi)
+            for s in (6, 7):
+                pick_product(prod, s, lo, hi)
+            newton(z_second[i], prod, 3, lo, hi)
+            quantise_z(z_second[i], ("quads2", "quads3", "w1_quads1")[i], 1, lo, hi, nc.vector.tensor_copy if last else nc.scalar.copy)
+            staged = sb([P, 4 * (hi - lo)], F32, "staged%d" % i)
+            rows = staged[:].rearrange("p (c j) -> p c j", c=4)
+            for c in range(4):
+                project(accs[c], 1, c, lo, hi)
+                if last and c % 2 == 1:
+                    nc.vector.tensor_scalar(rows[:, c, :], accs[c][:, : hi - lo], trim_sb[:, c : c + 1], None, ALU.add)
+                else:
+                    nc.scalar.activation(rows[:, c, :], accs[c][:, : hi - lo], ACT.Identity, bias=trim_sb[:, c : c + 1])
+            for half in range(2):
+                nc.sync.dma_start(out_rows[:, 2 * half : 2 * half + 2, lo:hi], rows[:, 2 * half : 2 * half + 2, :])

@@ -51,10 +51,11 @@ def tile_list_newton_clock_step_kernel(
         idx3 = lists.tile([P, S // GROUP], U16, name="idx3")
 
         tab_sc = sb([P, T], U8, "tab_sc")
-        w2_sc_raw = sb([P, 2 * H], U8, "w2_sc_raw")
+        w2_sc_raw = sb([P, H], U8, "w2_sc_raw")
+        w2_sc1 = sb([P, H], U8, "w2_sc1")
         w3_sc = sb([P, 2 * N], U8, "w3_sc")
         v_sc1 = sb([P, S], U8, "v_sc1")
-        for plane in (w2_sc_raw, tab_sc, w3_sc, v_sc1):
+        for plane in (tab_sc, w2_sc_raw, v_sc1, w2_sc1, w3_sc):
             nc.vector.memset(words(plane[:]), 0)
 
         page = [sb([P, T], F32, "wide%d" % t) for t in range(PACK)]
@@ -68,7 +69,7 @@ def tile_list_newton_clock_step_kernel(
         w1_quads = [sb([P, PACK * BANK], BF16, "w1_quads%d" % g) for g in range(2)]
 
         w2 = sb([P, 2 * 2 * H], U8, "w2")
-        w2_sc = sb([P, 2 * H], U8, "w2_sc")
+        w2_sc = sb([P, H], U8, "w2_sc")
         v_sc = sb([P, S], U8, "v_sc")
         v_early = [sb([P, BANK], U32, "v_early%d" % a) for a in range(2)]
         b_pairs = [sb([P, 2 * S], F32, "b%d" % k) for k in range(4)]
@@ -83,7 +84,7 @@ def tile_list_newton_clock_step_kernel(
             for a in range(2):
                 lo = a * H + s * P
                 nc.tensor.matmul_mx(
-                    acc[:], lhsT=w2[:, 2 * lo : 2 * (lo + P)].bitcast(FP4X4), lhsT_scale=w2_sc[:, lo : lo + P],
+                    acc[:], lhsT=w2[:, 2 * lo : 2 * (lo + P)].bitcast(FP4X4), lhsT_scale=(w2_sc, w2_sc1)[a][:, s * P : (s + 1) * P],
                     rhs=v[a][:].bitcast(FP8X4), rhs_scale=(v_sc, v_sc1)[a][:, cols], start=a == 0, stop=a == 1,
                 )
             lo = (s % 2) * S + h * BANK
@@ -127,18 +128,15 @@ def tile_list_newton_clock_step_kernel(
                 words(w2_raw[:]).rearrange("p (a c) -> p a c", a=2), words(w2_words).rearrange("a p c -> p a c")
             )
             for q in range(4):
-                nc.sync.dma_start(
-                    words(w2_sc_raw[32 * q : 32 * q + 4, :]).rearrange("r (a c) -> r a c", a=2),
-                    words(w2_scales[:, 4 * q : 4 * q + 4, :]).rearrange("a r c -> r a c"),
-                )
-            nc.sync.dma_start(idx2[:], offs2)
+                nc.sync.dma_start(words(tab_sc[32 * q : 32 * q + 8, :]), words(tab_scales[:, 4 * q : 4 * q + 4, :]))
+            nc.sync.dma_start(idx[:], offs)
             load_plane(0)
+            for q in range(4):
+                nc.sync.dma_start(words(w2_sc_raw[32 * q : 32 * q + 8, :]), words(w2_scales[:, 4 * q : 4 * q + 4, :]))
+            nc.sync.dma_start(idx2[:], offs2)
             load_w1(0)
             load_plane(1)
             load_w1(1)
-            nc.sync.dma_start(idx[:], offs)
-            for q in range(4):
-                nc.sync.dma_start(words(tab_sc[32 * q : 32 * q + 8, :]), words(tab_scales[:, 4 * q : 4 * q + 4, :]))
             load_table(0)
             load_table(1)
             load_plane(2)
@@ -160,6 +158,7 @@ def tile_list_newton_clock_step_kernel(
                 w2[:].bitcast(U16).rearrange("p (x t m) -> p x t m", t=PACK, m=P),
                 w2_raw[:].bitcast(U16).rearrange("p (x m t) -> p x t m", t=PACK, m=P),
             )
+            nc.vector.tensor_copy(v_sc[:], tab_sc[:].indirect(idx[:]))
             nc.vector.tensor_copy(
                 w2_sc[:].rearrange("p (x t m) -> p x t m", t=PACK, m=P),
                 w2_sc_raw[:].rearrange("p (x m t) -> p x t m", t=PACK, m=P),
@@ -168,9 +167,9 @@ def tile_list_newton_clock_step_kernel(
             round_w1(0)
             place(1)
             round_w1(1)
-            nc.vector.tensor_copy(v_sc[:], tab_sc[:].indirect(idx[:]))
-            for q in range(4):
-                nc.sync.dma_start(words(v_sc1[32 * q : 32 * q + 4, :]), words(v_sc[32 * q + 4 : 32 * q + 8, :]))
+            for packed, second in ((v_sc, v_sc1), (w2_sc, w2_sc1)):
+                for q in range(4):
+                    nc.sync.dma_start(words(second[32 * q : 32 * q + 4, :]), words(packed[32 * q + 4 : 32 * q + 8, :]))
             for a in range(2):
                 pick_words(v_early[a], a, 0)
             for s in range(8):
@@ -185,8 +184,8 @@ def tile_list_newton_clock_step_kernel(
         page_codes = sb([P, T], U32, "page_codes")
         page_sc = sb([P, T], U8, "page_sc")
 
-        def weave_page(c):
-            nc.vector.tensor_copy(
+        def weave_page(c, weave):
+            weave(
                 page_quads[c][:].bitcast(F32).rearrange("p (c u) -> p c u", u=2),
                 page_pairs[c][:].bitcast(F32).rearrange("p (u c) -> p c u", u=2),
             )
@@ -200,28 +199,32 @@ def tile_list_newton_clock_step_kernel(
             nc.vector.quantize_mx(w1_codes[:, cols].bitcast(FP8X4), w1_sc[:, cols], w1_quads[g][:])
 
         quantise_w1(0)
-        weave_page(0)
+        weave_page(0, nc.vector.tensor_copy)
         quantise_w1(1)
         for c in range(1, 4):
-            weave_page(c)
+            weave_page(c, nc.vector.tensor_copy)
             quantise_page(c - 1)
         quantise_page(3)
         for a in range(2):
             pick_words(v_late[a], a, 1)
 
-        neg_a = []
-        for s in range(8):
+        neg_a = [sb([P, T], F32, "wide%d" % s) for s in range(8)]
+
+        def gain(s, c):
             rows = slice(s * P, (s + 1) * P)
-            neg_a.append(sb([P, T], F32, "wide%d" % s))
+            cols = slice(c * BANK, (c + 1) * BANK)
+            acc = bank()
+            nc.tensor.matmul_mx(
+                acc[:], lhsT=w1_codes[:, rows].bitcast(FP8X4), lhsT_scale=w1_sc[:, rows],
+                rhs=page_codes[:, cols].bitcast(FP8X4), rhs_scale=page_sc[:, cols], start=True, stop=True,
+            )
+            nc.scalar.activation(neg_a[s][:, cols], acc[:], ACT.Copy, scale=-1.0)
+
+        for s in range(8):
             for c in range(4):
-                cols = slice(c * BANK, (c + 1) * BANK)
-                acc = bank()
-                nc.tensor.matmul_mx(
-                    acc[:], lhsT=w1_codes[:, rows].bitcast(FP8X4), lhsT_scale=w1_sc[:, rows],
-                    rhs=page_codes[:, cols].bitcast(FP8X4), rhs_scale=page_sc[:, cols], start=True, stop=True,
-                )
-                nc.scalar.activation(neg_a[s][:, cols], acc[:], ACT.Copy, scale=-1.0)
-            estimate(v_late, s, 1)
+                gain(s, c)
+            if s < 4:
+                estimate(v_late, s, 1)
 
         z_codes = [sb([P, S], U32, "z_codes%d" % g) for g in range(2)]
         z_sc = [sb([P, S], U8, "z_sc%d" % g) for g in range(2)]
@@ -236,9 +239,9 @@ def tile_list_newton_clock_step_kernel(
                 ALU.mult,
             )
 
-        def newton(z_pairs, prod, k, lo, hi):
+        def newton(z_pairs, first, prod, k, lo, hi):
             nc.vector.scalar_tensor_tensor(
-                z_pairs[:].rearrange("p (u j e) -> p u j e", u=2, e=2)[:, k % 2],
+                z_pairs[:].rearrange("p (u j e) -> p u j e", u=2, e=2)[:, k % 2, lo - first : hi - first, :],
                 prod[:].rearrange("p (e j) -> p j e", e=2)[:, lo:hi, :],
                 2.0,
                 b_pairs[k][:].rearrange("p (e j) -> p j e", e=2)[:, lo:hi, :],
@@ -246,11 +249,11 @@ def tile_list_newton_clock_step_kernel(
                 ALU.mult,
             )
 
-        def quantise_z(z_pairs, tag, g, lo, hi, weave):
+        def quantise_z(z_pairs, first, tag, g, lo, hi, weave):
             quads = sb([P, PACK * (hi - lo)], BF16, tag)
             weave(
                 quads[:].bitcast(F32).rearrange("p (j u) -> p j u", u=2),
-                z_pairs[:].bitcast(F32).rearrange("p (u j) -> p j u", u=2),
+                z_pairs[:].bitcast(F32).rearrange("p (u j) -> p j u", u=2)[:, lo - first : hi - first, :],
             )
             nc.vector.quantize_mx(z_codes[g][:, lo:hi].bitcast(FP8X4), z_sc[g][:, lo:hi], quads[:])
 
@@ -264,34 +267,25 @@ def tile_list_newton_clock_step_kernel(
         halves = [(0, BANK), (BANK, S)]
         pieces = [(0, 512), (512, 768), (768, 1024)]
 
-        z_first = [sb([P, PACK * BANK], BF16, "pairs%d" % h) for h in range(2)]
+        z_first = sb([P, PACK * S], BF16, "wide0")
         for k in range(2):
             prod = sb([P, 2 * S], F32, "prod", bufs=2)
             for s in (2 * k, 2 * k + 1):
                 for lo, hi in halves if s == 0 else [(0, S)]:
                     pick_product(prod, s, lo, hi)
-            for h, (lo, hi) in enumerate(halves):
-                newton(z_first[h], prod, k, lo, hi)
-        for h, (lo, hi) in enumerate(halves):
-            quantise_z(z_first[h], "quads%d" % h, 0, lo, hi, nc.scalar.copy)
+            newton(z_first, 0, prod, k, 0, S)
+        quantise_z(z_first, 0, "page_codes", 0, 0, S, nc.scalar.copy)
 
-        z_second = [sb([P, PACK * (hi - lo)], BF16, ("pairs2", "pairs3", "w1_quads0")[i]) for i, (lo, hi) in enumerate(pieces)]
-        prod = sb([P, 2 * S], F32, "prod", bufs=2)
-        for s in (4, 5):
-            pick_product(prod, s, 0, S)
-        for i, (lo, hi) in enumerate(pieces):
-            newton(z_second[i], prod, 2, lo, hi)
-        prod = sb([P, 2 * S], F32, "prod", bufs=2)
-        for i, (lo, hi) in enumerate(pieces):
+        z_second = [sb([P, PACK * BANK], BF16, "pairs%d" % h) for h in range(2)]
+        prods = [sb([P, 2 * S], F32, "prod", bufs=2) for k in range(2)]
+
+        def finish(i):
+            lo, hi = pieces[i]
             last = i == len(pieces) - 1
             accs = [bank() for c in range(4)]
             for c in range(4):
                 project(accs[c], 0, c, lo, hi)
-            for s in (6, 7):
-                pick_product(prod, s, lo, hi)
-            newton(z_second[i], prod, 3, lo, hi)
-            quantise_z(z_second[i], ("quads2", "quads3", "w1_quads1")[i], 1, lo, hi, nc.vector.tensor_copy if last else nc.scalar.copy)
-            staged = sb([P, 4 * (hi - lo)], F32, "staged%d" % i)
+            staged = sb([P, 4 * (hi - lo)], F32, "wide%d" % (2 + i))
             rows = staged[:].rearrange("p (c j) -> p c j", c=4)
             for c in range(4):
                 project(accs[c], 1, c, lo, hi)
@@ -299,5 +293,24 @@ def tile_list_newton_clock_step_kernel(
                     nc.vector.tensor_scalar(rows[:, c, :], accs[c][:, : hi - lo], trim_sb[:, c : c + 1], None, ALU.add)
                 else:
                     nc.scalar.activation(rows[:, c, :], accs[c][:, : hi - lo], ACT.Identity, bias=trim_sb[:, c : c + 1])
-            for half in range(2):
-                nc.sync.dma_start(out_rows[:, 2 * half : 2 * half + 2, lo:hi], rows[:, 2 * half : 2 * half + 2, :])
+            nc.sync.dma_start(out_rows[:, :, lo:hi], rows)
+
+        for k in (2, 3):
+            for s in (2 * k, 2 * k + 1):
+                pick_product(prods[k - 2], s, 0, BANK)
+            newton(z_second[0], 0, prods[k - 2], k, 0, BANK)
+        for s in (4, 5):
+            estimate(v_late, s, 1)
+        quantise_z(z_second[0], 0, "quads0", 1, 0, BANK, nc.scalar.copy)
+        for s in (6, 7):
+            estimate(v_late, s, 1)
+        finish(0)
+        for s in (4, 5):
+            pick_product(prods[0], s, BANK, S)
+        newton(z_second[1], BANK, prods[0], 2, BANK, S)
+        for i in (1, 2):
+            for s in (6, 7):
+                pick_product(prods[1], s, *pieces[i])
+            newton(z_second[1], BANK, prods[1], 3, *pieces[i])
+            quantise_z(z_second[1], BANK, "quads%d" % i, 1, *pieces[i], nc.vector.tensor_copy if i == 2 else nc.scalar.copy)
+            finish(i)

@@ -51,11 +51,10 @@ def tile_list_newton_clock_step_kernel(
         idx3 = lists.tile([P, S // GROUP], U16, name="idx3")
 
         tab_sc = sb([P, T], U8, "tab_sc")
-        w2_sc_raw = sb([P, H], U8, "w2_sc_raw")
-        w2_sc1 = sb([P, H], U8, "w2_sc1")
+        w2_sc_raw = sb([P, 2 * H], U8, "w2_sc_raw")
         w3_sc = sb([P, 2 * N], U8, "w3_sc")
         v_sc1 = sb([P, S], U8, "v_sc1")
-        for plane in (tab_sc, w2_sc_raw, v_sc1, w2_sc1, w3_sc):
+        for plane in (tab_sc, w2_sc_raw, v_sc1, w3_sc):
             nc.vector.memset(words(plane[:]), 0)
 
         page = [sb([P, T], F32, "wide%d" % t) for t in range(PACK)]
@@ -69,7 +68,7 @@ def tile_list_newton_clock_step_kernel(
         w1_quads = [sb([P, PACK * BANK], BF16, "w1_quads%d" % g) for g in range(2)]
 
         w2 = sb([P, 2 * 2 * H], U8, "w2")
-        w2_sc = sb([P, H], U8, "w2_sc")
+        w2_sc = sb([P, 2 * H], U8, "w2_sc")
         v_sc = sb([P, S], U8, "v_sc")
         v_early = [sb([P, BANK], U32, "v_early%d" % a) for a in range(2)]
         b_pairs = [sb([P, 2 * S], F32, "b%d" % k) for k in range(4)]
@@ -84,7 +83,7 @@ def tile_list_newton_clock_step_kernel(
             for a in range(2):
                 lo = a * H + s * P
                 nc.tensor.matmul_mx(
-                    acc[:], lhsT=w2[:, 2 * lo : 2 * (lo + P)].bitcast(FP4X4), lhsT_scale=(w2_sc, w2_sc1)[a][:, s * P : (s + 1) * P],
+                    acc[:], lhsT=w2[:, 2 * lo : 2 * (lo + P)].bitcast(FP4X4), lhsT_scale=w2_sc[:, lo : lo + P],
                     rhs=v[a][:].bitcast(FP8X4), rhs_scale=(v_sc, v_sc1)[a][:, cols], start=a == 0, stop=a == 1,
                 )
             lo = (s % 2) * S + h * BANK
@@ -132,13 +131,29 @@ def tile_list_newton_clock_step_kernel(
             nc.sync.dma_start(idx[:], offs)
             load_plane(0)
             for q in range(4):
-                nc.sync.dma_start(words(w2_sc_raw[32 * q : 32 * q + 8, :]), words(w2_scales[:, 4 * q : 4 * q + 4, :]))
+                nc.sync.dma_start(
+                    words(w2_sc_raw[32 * q : 32 * q + 4, :]).rearrange("r (a c) -> r a c", a=2),
+                    words(w2_scales[:, 4 * q : 4 * q + 4, :]).rearrange("a r c -> r a c"),
+                )
             nc.sync.dma_start(idx2[:], offs2)
             load_w1(0)
             load_plane(1)
             load_w1(1)
             load_table(0)
             load_table(1)
+
+            nc.vector.tensor_copy(
+                w2[:].bitcast(U16).rearrange("p (x t m) -> p x t m", t=PACK, m=P),
+                w2_raw[:].bitcast(U16).rearrange("p (x m t) -> p x t m", t=PACK, m=P),
+            )
+            nc.vector.tensor_copy(v_sc[:], tab_sc[:].indirect(idx[:]))
+            nc.vector.tensor_copy(
+                w2_sc[:].rearrange("p (x t m) -> p x t m", t=PACK, m=P),
+                w2_sc_raw[:].rearrange("p (x m t) -> p x t m", t=PACK, m=P),
+            )
+            for q in range(4):
+                nc.sync.dma_start(words(v_sc1[32 * q : 32 * q + 4, :]), words(v_sc[32 * q + 4 : 32 * q + 8, :]))
+
             load_plane(2)
             load_plane(3)
             nc.sync.dma_start(idx3[:], offs3)
@@ -154,22 +169,10 @@ def tile_list_newton_clock_step_kernel(
             with nc.allow_non_contiguous_dma(reason="one trim value a partition"):
                 nc.sync.dma_start(trim_sb[:], trim.rearrange("(c p) -> p c", p=P))
 
-            nc.vector.tensor_copy(
-                w2[:].bitcast(U16).rearrange("p (x t m) -> p x t m", t=PACK, m=P),
-                w2_raw[:].bitcast(U16).rearrange("p (x m t) -> p x t m", t=PACK, m=P),
-            )
-            nc.vector.tensor_copy(v_sc[:], tab_sc[:].indirect(idx[:]))
-            nc.vector.tensor_copy(
-                w2_sc[:].rearrange("p (x t m) -> p x t m", t=PACK, m=P),
-                w2_sc_raw[:].rearrange("p (x m t) -> p x t m", t=PACK, m=P),
-            )
             place(0)
             round_w1(0)
             place(1)
             round_w1(1)
-            for packed, second in ((v_sc, v_sc1), (w2_sc, w2_sc1)):
-                for q in range(4):
-                    nc.sync.dma_start(words(second[32 * q : 32 * q + 4, :]), words(packed[32 * q + 4 : 32 * q + 8, :]))
             for a in range(2):
                 pick_words(v_early[a], a, 0)
             for s in range(8):
@@ -287,13 +290,17 @@ def tile_list_newton_clock_step_kernel(
                 project(accs[c], 0, c, lo, hi)
             staged = sb([P, 4 * (hi - lo)], F32, "wide%d" % (2 + i))
             rows = staged[:].rearrange("p (c j) -> p c j", c=4)
-            for c in range(4):
+            for c in (0, 2, 1, 3):
                 project(accs[c], 1, c, lo, hi)
-                if last and c % 2 == 1:
+                if last and c >= 2:
                     nc.vector.tensor_scalar(rows[:, c, :], accs[c][:, : hi - lo], trim_sb[:, c : c + 1], None, ALU.add)
                 else:
                     nc.scalar.activation(rows[:, c, :], accs[c][:, : hi - lo], ACT.Identity, bias=trim_sb[:, c : c + 1])
-            nc.sync.dma_start(out_rows[:, :, lo:hi], rows)
+            if last:
+                nc.scalar.dma_start(out_rows[:, :2, lo:hi], rows[:, :2, :])
+                nc.sync.dma_start(out_rows[:, 2:, lo:hi], rows[:, 2:, :])
+            else:
+                nc.sync.dma_start(out_rows[:, :, lo:hi], rows)
 
         for k in (2, 3):
             for s in (2 * k, 2 * k + 1):

@@ -129,16 +129,16 @@ def tile_list_newton_clock_step_kernel(
             for q in range(4):
                 nc.sync.dma_start(words(tab_sc[32 * q : 32 * q + 8, :]), words(tab_scales[:, 4 * q : 4 * q + 4, :]))
             nc.sync.dma_start(idx[:], offs)
+            nc.sync.dma_start(idx2[:], offs2)
             load_plane(0)
+            load_w1(0)
+            load_plane(1)
+            load_w1(1)
             for q in range(4):
                 nc.sync.dma_start(
                     words(w2_sc_raw[32 * q : 32 * q + 4, :]).rearrange("r (a c) -> r a c", a=2),
                     words(w2_scales[:, 4 * q : 4 * q + 4, :]).rearrange("a r c -> r a c"),
                 )
-            nc.sync.dma_start(idx2[:], offs2)
-            load_w1(0)
-            load_plane(1)
-            load_w1(1)
             load_table(0)
             load_table(1)
 
@@ -147,10 +147,6 @@ def tile_list_newton_clock_step_kernel(
                 w2_raw[:].bitcast(U16).rearrange("p (x m t) -> p x t m", t=PACK, m=P),
             )
             nc.vector.tensor_copy(v_sc[:], tab_sc[:].indirect(idx[:]))
-            nc.vector.tensor_copy(
-                w2_sc[:].rearrange("p (x t m) -> p x t m", t=PACK, m=P),
-                w2_sc_raw[:].rearrange("p (x m t) -> p x t m", t=PACK, m=P),
-            )
             for q in range(4):
                 nc.sync.dma_start(words(v_sc1[32 * q : 32 * q + 4, :]), words(v_sc[32 * q + 4 : 32 * q + 8, :]))
 
@@ -173,6 +169,10 @@ def tile_list_newton_clock_step_kernel(
             round_w1(0)
             place(1)
             round_w1(1)
+            nc.vector.tensor_copy(
+                w2_sc[:].rearrange("p (x t m) -> p x t m", t=PACK, m=P),
+                w2_sc_raw[:].rearrange("p (x m t) -> p x t m", t=PACK, m=P),
+            )
             for a in range(2):
                 pick_words(v_early[a], a, 0)
             for s in range(8):
@@ -181,7 +181,6 @@ def tile_list_newton_clock_step_kernel(
             place(3)
 
         picked = ctx.enter_context(tc.tile_pool(name="picked", bufs=1))
-        v_late = [picked.tile([P, BANK], U32, name="v_late%d" % a, align_bytes=64) for a in range(2)]
         w1_codes = picked.tile([P, H], U32, name="w1_codes", align_bytes=64)
         w1_sc = sb([P, H], U8, "w1_sc")
         page_codes = sb([P, T], U32, "page_codes")
@@ -201,13 +200,16 @@ def tile_list_newton_clock_step_kernel(
             cols = slice(g * BANK, (g + 1) * BANK)
             nc.vector.quantize_mx(w1_codes[:, cols].bitcast(FP8X4), w1_sc[:, cols], w1_quads[g][:])
 
+        weave_page(3, nc.scalar.copy)
         quantise_w1(0)
         weave_page(0, nc.vector.tensor_copy)
         quantise_w1(1)
-        for c in range(1, 4):
+        for c in range(1, 3):
             weave_page(c, nc.vector.tensor_copy)
             quantise_page(c - 1)
+        quantise_page(2)
         quantise_page(3)
+        v_late = [sb([P, BANK], U32, "quads%d" % (2 + a)) for a in range(2)]
         for a in range(2):
             pick_words(v_late[a], a, 1)
 

@@ -54,7 +54,8 @@ def tile_list_newton_clock_step_kernel(
         w2_sc_raw = sb([P, 2 * H], U8, "w2_sc_raw")
         w3_sc = sb([P, 2 * N], U8, "w3_sc")
         v_sc1 = sb([P, S], U8, "v_sc1")
-        for plane in (tab_sc, w2_sc_raw, v_sc1, w3_sc):
+        nc.gpsimd.memset(words(tab_sc[:]), 0)
+        for plane in (w2_sc_raw, v_sc1, w3_sc):
             nc.vector.memset(words(plane[:]), 0)
 
         page = [sb([P, T], F32, "wide%d" % t) for t in range(PACK)]
@@ -123,34 +124,39 @@ def tile_list_newton_clock_step_kernel(
                     ACT.Copy,
                 )
 
+            nc.sync.dma_start(idx[:], offs)
+            for q in range(4):
+                nc.sync.dma_start(words(tab_sc[32 * q : 32 * q + 8, :]), words(tab_scales[:, 4 * q : 4 * q + 4, :]))
+            nc.sync.dma_start(idx2[:], offs2)
+            load_plane(0)
             nc.sync.dma_start(
                 words(w2_raw[:]).rearrange("p (a c) -> p a c", a=2), words(w2_words).rearrange("a p c -> p a c")
             )
-            for q in range(4):
-                nc.sync.dma_start(words(tab_sc[32 * q : 32 * q + 8, :]), words(tab_scales[:, 4 * q : 4 * q + 4, :]))
-            nc.sync.dma_start(idx[:], offs)
-            nc.sync.dma_start(idx2[:], offs2)
-            load_plane(0)
-            load_w1(0)
-            load_plane(1)
-            load_w1(1)
             for q in range(4):
                 nc.sync.dma_start(
                     words(w2_sc_raw[32 * q : 32 * q + 4, :]).rearrange("r (a c) -> r a c", a=2),
                     words(w2_scales[:, 4 * q : 4 * q + 4, :]).rearrange("a r c -> r a c"),
                 )
-            load_table(0)
-            load_table(1)
+            load_plane(1)
+            load_w1(0)
 
-            nc.vector.tensor_copy(
-                w2[:].bitcast(U16).rearrange("p (x t m) -> p x t m", t=PACK, m=P),
-                w2_raw[:].bitcast(U16).rearrange("p (x m t) -> p x t m", t=PACK, m=P),
-            )
             nc.vector.tensor_copy(v_sc[:], tab_sc[:].indirect(idx[:]))
             for q in range(4):
                 nc.sync.dma_start(words(v_sc1[32 * q : 32 * q + 4, :]), words(v_sc[32 * q + 4 : 32 * q + 8, :]))
+            load_table(0)
+            load_table(1)
+            for x in range(4):
+                nc.gpsimd.tensor_copy(
+                    w2[:, x * H : (x + 1) * H].rearrange("p (t m e) -> p t m e", t=PACK, e=2),
+                    w2_raw[:, x * H : (x + 1) * H].rearrange("p (m t e) -> p t m e", t=PACK, e=2),
+                )
+            nc.gpsimd.tensor_copy(
+                w2_sc[:].rearrange("p (x t m) -> p x t m", t=PACK, m=P),
+                w2_sc_raw[:].rearrange("p (x m t) -> p x t m", t=PACK, m=P),
+            )
 
             load_plane(2)
+            load_w1(1)
             load_plane(3)
             nc.sync.dma_start(idx3[:], offs3)
             nc.sync.dma_start(
@@ -168,16 +174,12 @@ def tile_list_newton_clock_step_kernel(
             place(0)
             round_w1(0)
             place(1)
-            round_w1(1)
-            nc.vector.tensor_copy(
-                w2_sc[:].rearrange("p (x t m) -> p x t m", t=PACK, m=P),
-                w2_sc_raw[:].rearrange("p (x m t) -> p x t m", t=PACK, m=P),
-            )
             for a in range(2):
                 pick_words(v_early[a], a, 0)
             for s in range(8):
                 estimate(v_early, s, 0)
             place(2)
+            round_w1(1)
             place(3)
 
         picked = ctx.enter_context(tc.tile_pool(name="picked", bufs=1))

@@ -230,38 +230,46 @@ def tile_list_newton_clock_step_kernel(
         for s in range(8):
             for c in range(4):
                 gain(s, c)
-            if s < 4:
+            if s < 6:
                 estimate(v_late, s, 1)
+        for s in (6, 7):
+            estimate(v_late, s, 1)
 
         z_codes = [sb([P, S], U32, "z_codes%d" % g) for g in range(2)]
         z_sc = [sb([P, S], U8, "z_sc%d" % g) for g in range(2)]
         out_rows = out.rearrange("(c p) j -> p c j", p=P)
 
+        def product_tile(lo, hi, tag="prod", bufs=4):
+            return sb([P, 2 * (hi - lo)], F32, tag, bufs=bufs)
+
         def pick_product(prod, s, lo, hi):
             at = (s % 2) * S
             nc.vector.tensor_tensor(
-                prod[:, at + lo : at + hi],
+                prod[:, (s % 2) * (hi - lo) : (s % 2 + 1) * (hi - lo)],
                 neg_a[s][:].indirect(idx3[:, lo // GROUP : hi // GROUP]),
                 b_pairs[s // 2][:, at + lo : at + hi],
                 ALU.mult,
             )
 
-        def newton(z_pairs, first, prod, k, lo, hi):
+        def newton(z_pairs, z_first_col, prod, prod_first_col, k, lo, hi):
             nc.vector.scalar_tensor_tensor(
-                z_pairs[:].rearrange("p (u j e) -> p u j e", u=2, e=2)[:, k % 2, lo - first : hi - first, :],
-                prod[:].rearrange("p (e j) -> p j e", e=2)[:, lo:hi, :],
+                z_pairs[:].rearrange("p (u j e) -> p u j e", u=2, e=2)[:, k % 2, lo - z_first_col : hi - z_first_col, :],
+                prod[:].rearrange("p (e j) -> p j e", e=2)[:, lo - prod_first_col : hi - prod_first_col, :],
                 2.0,
                 b_pairs[k][:].rearrange("p (e j) -> p j e", e=2)[:, lo:hi, :],
                 ALU.add,
                 ALU.mult,
             )
 
-        def quantise_z(z_pairs, first, tag, g, lo, hi, weave):
-            quads = sb([P, PACK * (hi - lo)], BF16, tag)
+        def weave_z(z_pairs, tag, weave):
+            quads = sb(list(z_pairs.shape), BF16, tag)
             weave(
                 quads[:].bitcast(F32).rearrange("p (j u) -> p j u", u=2),
-                z_pairs[:].bitcast(F32).rearrange("p (u j) -> p j u", u=2)[:, lo - first : hi - first, :],
+                z_pairs[:].bitcast(F32).rearrange("p (u j) -> p j u", u=2),
             )
+            return quads
+
+        def quantise_z(quads, g, lo, hi):
             nc.vector.quantize_mx(z_codes[g][:, lo:hi].bitcast(FP8X4), z_sc[g][:, lo:hi], quads[:])
 
         def project(acc, g, c, lo, hi):
@@ -272,56 +280,90 @@ def tile_list_newton_clock_step_kernel(
             )
 
         halves = [(0, BANK), (BANK, S)]
-        pieces = [(0, 512), (512, 768), (768, 1024)]
+        pieces = [(lo, lo + 256) for lo in range(0, S, 256)]
+
+        def pick_pair(k):
+            prods = [product_tile(lo, hi) for lo, hi in halves]
+            for s in (2 * k, 2 * k + 1):
+                for prod, (lo, hi) in zip(prods, halves):
+                    pick_product(prod, s, lo, hi)
+            return prods
 
         z_first = sb([P, PACK * S], BF16, "wide0")
         for k in range(2):
-            prod = sb([P, 2 * S], F32, "prod", bufs=2)
-            for s in (2 * k, 2 * k + 1):
-                for lo, hi in halves if s == 0 else [(0, S)]:
-                    pick_product(prod, s, lo, hi)
-            newton(z_first, 0, prod, k, 0, S)
-        quantise_z(z_first, 0, "page_codes", 0, 0, S, nc.scalar.copy)
+            for prod, (lo, hi) in zip(pick_pair(k), halves):
+                newton(z_first, 0, prod, lo, k, lo, hi)
+        quads_first = weave_z(z_first, "page_codes", nc.scalar.copy)
 
-        z_second = [sb([P, PACK * BANK], BF16, "pairs%d" % h) for h in range(2)]
-        prods = [sb([P, 2 * S], F32, "prod", bufs=2) for k in range(2)]
+        z_second = [sb([P, PACK * (hi - lo)], BF16, "pairs%d" % i) for i, (lo, hi) in enumerate(pieces)]
+        prods = pick_pair(2)
+        for z_pairs, (lo, hi) in zip(z_second, pieces):
+            newton(z_pairs, lo, prods[lo // BANK], lo // BANK * BANK, 2, lo, hi)
 
-        def finish(i):
-            lo, hi = pieces[i]
-            last = i == len(pieces) - 1
+        def open_sums(i):
             accs = [bank() for c in range(4)]
             for c in range(4):
-                project(accs[c], 0, c, lo, hi)
-            staged = sb([P, 4 * (hi - lo)], F32, "wide%d" % (2 + i))
-            rows = staged[:].rearrange("p (c j) -> p c j", c=4)
-            for c in (0, 2, 1, 3):
-                project(accs[c], 1, c, lo, hi)
-                if last and c >= 2:
-                    nc.vector.tensor_scalar(rows[:, c, :], accs[c][:, : hi - lo], trim_sb[:, c : c + 1], None, ALU.add)
-                else:
-                    nc.scalar.activation(rows[:, c, :], accs[c][:, : hi - lo], ACT.Identity, bias=trim_sb[:, c : c + 1])
-            if last:
-                nc.scalar.dma_start(out_rows[:, :2, lo:hi], rows[:, :2, :])
-                nc.sync.dma_start(out_rows[:, 2:, lo:hi], rows[:, 2:, :])
-            else:
-                nc.sync.dma_start(out_rows[:, :, lo:hi], rows)
+                project(accs[c], 0, c, *pieces[i])
+            return accs
 
-        for k in (2, 3):
-            for s in (2 * k, 2 * k + 1):
-                pick_product(prods[k - 2], s, 0, BANK)
-            newton(z_second[0], 0, prods[k - 2], k, 0, BANK)
-        for s in (4, 5):
-            estimate(v_late, s, 1)
-        quantise_z(z_second[0], 0, "quads0", 1, 0, BANK, nc.scalar.copy)
+        def close_sums(accs, i):
+            for c in (0, 2, 1, 3):
+                project(accs[c], 1, c, *pieces[i])
+
+        def staging(i):
+            lo, hi = pieces[i]
+            staged = sb([P, 4 * (hi - lo)], F32, "wide%d" % (2 + i))
+            return staged[:].rearrange("p (c j) -> p c j", c=4)
+
+        def add_trim(rows, accs, i, c, on_vector):
+            lo, hi = pieces[i]
+            if on_vector:
+                nc.vector.tensor_scalar(rows[:, c, :], accs[c][:, : hi - lo], trim_sb[:, c : c + 1], None, ALU.add)
+            else:
+                nc.scalar.activation(rows[:, c, :], accs[c][:, : hi - lo], ACT.Identity, bias=trim_sb[:, c : c + 1])
+
+        def store(queue, rows, i, c0, c1):
+            lo, hi = pieces[i]
+            queue.dma_start(out_rows[:, c0:c1, lo:hi], rows[:, c0:c1, :])
+
+        def multiply(quads, i):
+            accs = open_sums(i)
+            quantise_z(quads, 1, *pieces[i])
+            close_sums(accs, i)
+            return accs
+
+        def finish(accs, i):
+            rows = staging(i)
+            for c in (0, 2, 1, 3):
+                add_trim(rows, accs, i, c, i >= 2 and c >= 2)
+            if i == len(pieces) - 1:
+                store(nc.scalar, rows, i, 0, 2)
+                store(nc.sync, rows, i, 2, 4)
+            else:
+                store(nc.sync, rows, i, 0, 4)
+
+        def last_step(prod, i, weave):
+            lo, hi = pieces[i]
+            newton(z_second[i], lo, prod, lo, 3, lo, hi)
+            return weave_z(z_second[i], "quads%d" % (i + 1 if i >= 2 else i), weave)
+
+        prods = [product_tile(*pieces[i]) for i in range(2)]
         for s in (6, 7):
-            estimate(v_late, s, 1)
-        finish(0)
-        for s in (4, 5):
-            pick_product(prods[0], s, BANK, S)
-        newton(z_second[1], BANK, prods[0], 2, BANK, S)
-        for i in (1, 2):
-            for s in (6, 7):
-                pick_product(prods[1], s, *pieces[i])
-            newton(z_second[1], BANK, prods[1], 3, *pieces[i])
-            quantise_z(z_second[1], BANK, "quads%d" % i, 1, *pieces[i], nc.vector.tensor_copy if i == 2 else nc.scalar.copy)
-            finish(i)
+            for i in range(2):
+                pick_product(prods[i], s, *pieces[i])
+        quads = [last_step(prods[i], i, nc.scalar.copy) for i in range(2)]
+        quantise_z(quads_first, 0, 0, S)
+        sums = [multiply(quads[i], i) for i in range(2)]
+        prods = [product_tile(*pieces[2], "page_codes", 1), product_tile(*pieces[3], "quads0", 1)]
+        pick_product(prods[0], 6, *pieces[2])
+        pick_product(prods[0], 7, *pieces[2])
+        pick_product(prods[1], 6, *pieces[3])
+        finish(sums[0], 0)
+        quads2 = last_step(prods[0], 2, nc.scalar.copy)
+        finish(sums[1], 1)
+        pick_product(prods[1], 7, *pieces[3])
+        sums2 = multiply(quads2, 2)
+        quads3 = last_step(prods[1], 3, nc.vector.tensor_copy)
+        sums3 = multiply(quads3, 3)
+        finish(sums2, 2)
+        finish(sums3, 3)

@@ -51,7 +51,7 @@ def tile_list_newton_clock_step_kernel(
         idx3 = lists.tile([P, S // GROUP], U16, name="idx3")
 
         tab_sc = sb([P, T], U8, "tab_sc")
-        w2_sc_raw = sb([P, 2 * H], U8, "w2_sc_raw")
+        w2_sc_raw = sb([P, 2 * H], U8, "quads1")
         w3_sc = sb([P, 2 * N], U8, "w3_sc")
         v_sc1 = sb([P, S], U8, "v_sc1")
         nc.gpsimd.memset(words(tab_sc[:]), 0)
@@ -61,11 +61,10 @@ def tile_list_newton_clock_step_kernel(
         page = [sb([P, T], F32, "wide%d" % t) for t in range(PACK)]
         w1_raw = [sb([P, PACK * BANK], F32, "wide%d" % (4 + g)) for g in range(2)]
         tab = [sb([P, T], U32, "wide%d" % (6 + a)) for a in range(2)]
-        w2_raw = sb([P, 2 * 2 * H], U8, "w2_raw")
+        w2_raw = [sb([P, 2 * H], U8, tag) for tag in ("quads0", "quads3")]
         w3 = sb([P, 2 * N], U32, "w3")
         trim_sb = sb([P, N // P], F32, "trim")
-        page_pairs = [sb([P, PACK * BANK], BF16, "pairs%d" % c) for c in range(4)]
-        page_quads = [sb([P, PACK * BANK], BF16, "quads%d" % c) for c in range(4)]
+        page_cuts = [(0, 512), (512, 768), (768, 1024), (1024, 1536), (1536, 2048)]
         w1_quads = [sb([P, PACK * BANK], BF16, "w1_quads%d" % g) for g in range(2)]
 
         w2 = sb([P, 2 * 2 * H], U8, "w2")
@@ -95,11 +94,16 @@ def tile_list_newton_clock_step_kernel(
         w1_rows = w1.rearrange("(p t) r -> p t r", t=PACK)
 
         with tc.tile_pool(name="arrivals", bufs=1) as arrivals:
-            blocks = [arrivals.tile([P, S], F32, name="xs%d" % t, align_bytes=64) for t in range(PACK)]
+            cuts = [[(0, 256), (256, S)]] + [[(0, S)]] * (PACK - 1)
+            blocks = [
+                [arrivals.tile([P, hi - lo], F32, name="xs%d_%d" % (t, lo), align_bytes=64) for lo, hi in cuts[t]]
+                for t in range(PACK)
+            ]
 
             def load_plane(t):
                 nc.sync.dma_start(page[t][:], base_planes[t])
-                nc.sync.dma_start(blocks[t][:], xs_planes[t])
+                for block, (lo, hi) in zip(blocks[t], cuts[t]):
+                    nc.sync.dma_start(block[:], xs_planes[t][:, lo:hi])
 
             def load_table(a):
                 nc.sync.dma_start(words(tab[a][:]), words(tab_words[a].rearrange("p t i -> p (t i)")))
@@ -110,28 +114,30 @@ def tile_list_newton_clock_step_kernel(
                 )
 
             def place(t):
-                nc.vector.tensor_copy(page[t][:].indirect(idx2[:]), blocks[t][:])
-                for c in range(4):
-                    nc.scalar.copy(
-                        page_pairs[c][:].rearrange("p (u c e) -> p u c e", u=2, e=2)[:, t // 2, :, t % 2],
-                        page[t][:, c * BANK : (c + 1) * BANK],
-                    )
+                for block, (lo, hi) in zip(blocks[t], cuts[t]):
+                    nc.vector.tensor_copy(page[t][:].indirect(idx2[:, lo // GROUP : hi // GROUP]), block[:])
+                for c, (lo, hi) in enumerate(page_cuts):
+                    slots = page_quads[c][:].rearrange("p (c t) -> p c t", t=PACK)[:, :, t]
+                    if c < 2 or (t < 2 and c == 3):
+                        nc.gpsimd.tensor_scalar(slots, page[t][:, lo:hi], 1.0, 0.0, ALU.mult, ALU.add)
+                    else:
+                        nc.scalar.copy(slots, page[t][:, lo:hi])
 
             def round_w1(g):
-                nc.scalar.activation(
-                    w1_quads[g][:].rearrange("p (t m j) -> p m t j", t=PACK, j=PACK),
-                    w1_raw[g][:].rearrange("p (j m t) -> p m t j", j=PACK, t=PACK),
-                    ACT.Copy,
-                )
+                rounded = w1_quads[g][:].rearrange("p (t m j) -> p m t j", t=PACK, j=PACK)
+                raw = w1_raw[g][:].rearrange("p (j m t) -> p m t j", j=PACK, t=PACK)
+                if g == 0:
+                    nc.scalar.activation(rounded, raw, ACT.Copy)
+                else:
+                    nc.gpsimd.tensor_scalar(rounded, raw, 1.0, 0.0, ALU.mult, ALU.add)
 
             nc.sync.dma_start(idx[:], offs)
             for q in range(4):
                 nc.sync.dma_start(words(tab_sc[32 * q : 32 * q + 8, :]), words(tab_scales[:, 4 * q : 4 * q + 4, :]))
             nc.sync.dma_start(idx2[:], offs2)
             load_plane(0)
-            nc.sync.dma_start(
-                words(w2_raw[:]).rearrange("p (a c) -> p a c", a=2), words(w2_words).rearrange("a p c -> p a c")
-            )
+            for a in range(2):
+                nc.sync.dma_start(words(w2_raw[a][:]), words(w2_words[a]))
             for q in range(4):
                 nc.sync.dma_start(
                     words(w2_sc_raw[32 * q : 32 * q + 4, :]).rearrange("r (a c) -> r a c", a=2),
@@ -148,13 +154,14 @@ def tile_list_newton_clock_step_kernel(
             for x in range(4):
                 nc.gpsimd.tensor_copy(
                     w2[:, x * H : (x + 1) * H].rearrange("p (t m e) -> p t m e", t=PACK, e=2),
-                    w2_raw[:, x * H : (x + 1) * H].rearrange("p (m t e) -> p t m e", t=PACK, e=2),
+                    w2_raw[x // 2][:, x % 2 * H : (x % 2 + 1) * H].rearrange("p (m t e) -> p t m e", t=PACK, e=2),
                 )
             nc.gpsimd.tensor_copy(
                 w2_sc[:].rearrange("p (x t m) -> p x t m", t=PACK, m=P),
                 w2_sc_raw[:].rearrange("p (x m t) -> p x t m", t=PACK, m=P),
             )
 
+            page_quads = [sb([P, PACK * (hi - lo)], BF16, "quads%d" % c) for c, (lo, hi) in enumerate(page_cuts)]
             load_plane(2)
             load_w1(1)
             load_plane(3)
@@ -172,8 +179,8 @@ def tile_list_newton_clock_step_kernel(
                 nc.sync.dma_start(trim_sb[:], trim.rearrange("(c p) -> p c", p=P))
 
             place(0)
-            round_w1(0)
             place(1)
+            round_w1(0)
             for a in range(2):
                 pick_words(v_early[a], a, 0)
             for s in range(8):
@@ -183,49 +190,37 @@ def tile_list_newton_clock_step_kernel(
             place(3)
 
         picked = ctx.enter_context(tc.tile_pool(name="picked", bufs=1))
-        w1_codes = picked.tile([P, H], U32, name="w1_codes", align_bytes=64)
-        w1_sc = sb([P, H], U8, "w1_sc")
+        v_late = [picked.tile([P, BANK], U32, name="v_late%d" % a, align_bytes=64) for a in range(2)]
+        w1_codes = [picked.tile([P, BANK], U32, name="w1_codes0", align_bytes=64)]
+        w1_sc = [sb([P, BANK], U8, "w1_sc%d" % g) for g in range(2)]
         page_codes = sb([P, T], U32, "page_codes")
         page_sc = sb([P, T], U8, "page_sc")
 
-        def weave_page(c, weave):
-            weave(
-                page_quads[c][:].bitcast(F32).rearrange("p (c u) -> p c u", u=2),
-                page_pairs[c][:].bitcast(F32).rearrange("p (u c) -> p c u", u=2),
-            )
-
-        def quantise_page(c):
-            cols = slice(c * BANK, (c + 1) * BANK)
-            nc.vector.quantize_mx(page_codes[:, cols].bitcast(FP8X4), page_sc[:, cols], page_quads[c][:])
-
         def quantise_w1(g):
-            cols = slice(g * BANK, (g + 1) * BANK)
-            nc.vector.quantize_mx(w1_codes[:, cols].bitcast(FP8X4), w1_sc[:, cols], w1_quads[g][:])
+            nc.vector.quantize_mx(w1_codes[g][:].bitcast(FP8X4), w1_sc[g][:], w1_quads[g][:])
 
-        weave_page(3, nc.scalar.copy)
-        quantise_w1(0)
-        weave_page(0, nc.vector.tensor_copy)
-        quantise_w1(1)
-        for c in range(1, 3):
-            weave_page(c, nc.vector.tensor_copy)
-            quantise_page(c - 1)
-        quantise_page(2)
-        quantise_page(3)
-        v_late = [sb([P, BANK], U32, "quads%d" % (2 + a)) for a in range(2)]
         for a in range(2):
             pick_words(v_late[a], a, 1)
+        quantise_w1(0)
+        for c, (lo, hi) in enumerate(page_cuts):
+            nc.vector.quantize_mx(page_codes[:, lo:hi].bitcast(FP8X4), page_sc[:, lo:hi], page_quads[c][:])
+        w1_codes.append(sb([P, BANK], U32, "quads3"))
+        quantise_w1(1)
 
         neg_a = [sb([P, T], F32, "wide%d" % s) for s in range(8)]
 
         def gain(s, c):
-            rows = slice(s * P, (s + 1) * P)
+            rows = slice(s % PACK * P, (s % PACK + 1) * P)
             cols = slice(c * BANK, (c + 1) * BANK)
             acc = bank()
             nc.tensor.matmul_mx(
-                acc[:], lhsT=w1_codes[:, rows].bitcast(FP8X4), lhsT_scale=w1_sc[:, rows],
+                acc[:], lhsT=w1_codes[s // PACK][:, rows].bitcast(FP8X4), lhsT_scale=w1_sc[s // PACK][:, rows],
                 rhs=page_codes[:, cols].bitcast(FP8X4), rhs_scale=page_sc[:, cols], start=True, stop=True,
             )
-            nc.scalar.activation(neg_a[s][:, cols], acc[:], ACT.Copy, scale=-1.0)
+            if s == 0 and c == 3:
+                nc.vector.tensor_scalar(neg_a[s][:, cols], acc[:], -1.0, None, ALU.mult)
+            else:
+                nc.scalar.activation(neg_a[s][:, cols], acc[:], ACT.Copy, scale=-1.0)
 
         for s in range(8):
             for c in range(4):
@@ -345,7 +340,7 @@ def tile_list_newton_clock_step_kernel(
         def last_step(prod, i, weave):
             lo, hi = pieces[i]
             newton(z_second[i], lo, prod, lo, 3, lo, hi)
-            return weave_z(z_second[i], "quads%d" % (i + 1 if i >= 2 else i), weave)
+            return weave_z(z_second[i], "quads%d" % (0, 1, 2, 4)[i], weave)
 
         prods = [product_tile(*pieces[i]) for i in range(2)]
         for s in (6, 7):

@@ -53,9 +53,10 @@ def tile_list_newton_clock_step_kernel(
         tab_sc = sb([P, T], U8, "tab_sc")
         w2_sc_raw = sb([P, 2 * H], U8, "quads1")
         w3_sc = sb([P, 2 * N], U8, "w3_sc")
-        v_sc1 = sb([P, S], U8, "v_sc1")
-        nc.gpsimd.memset(words(tab_sc[:]), 0)
-        for plane in (w2_sc_raw, v_sc1, w3_sc):
+        v_planes = [sb([P, S], U8, "v_plane%d" % a) for a in range(2)]
+        nc.vector.memset(words(tab_sc[32:64, :]), 0)
+        nc.vector.memset(words(tab_sc[64:, :]), 0)
+        for plane in (w2_sc_raw, *v_planes, w3_sc):
             nc.vector.memset(words(plane[:]), 0)
 
         page = [sb([P, T], F32, "wide%d" % t) for t in range(PACK)]
@@ -84,7 +85,7 @@ def tile_list_newton_clock_step_kernel(
                 lo = a * H + s * P
                 nc.tensor.matmul_mx(
                     acc[:], lhsT=w2[:, 2 * lo : 2 * (lo + P)].bitcast(FP4X4), lhsT_scale=w2_sc[:, lo : lo + P],
-                    rhs=v[a][:].bitcast(FP8X4), rhs_scale=(v_sc, v_sc1)[a][:, cols], start=a == 0, stop=a == 1,
+                    rhs=v[a][:].bitcast(FP8X4), rhs_scale=v_planes[a][:, cols], start=a == 0, stop=a == 1,
                 )
             lo = (s % 2) * S + h * BANK
             nc.scalar.copy(b_pairs[s // 2][:, lo : lo + BANK], acc[:])
@@ -132,8 +133,7 @@ def tile_list_newton_clock_step_kernel(
                     nc.gpsimd.tensor_scalar(rounded, raw, 1.0, 0.0, ALU.mult, ALU.add)
 
             nc.sync.dma_start(idx[:], offs)
-            for q in range(4):
-                nc.sync.dma_start(words(tab_sc[32 * q : 32 * q + 8, :]), words(tab_scales[:, 4 * q : 4 * q + 4, :]))
+            nc.sync.dma_start(words(tab_sc[:32, :]), words(tab_scales.rearrange("a q t -> (a q) t")))
             nc.sync.dma_start(idx2[:], offs2)
             load_plane(0)
             for a in range(2):
@@ -147,10 +147,11 @@ def tile_list_newton_clock_step_kernel(
             load_w1(0)
 
             nc.vector.tensor_copy(v_sc[:], tab_sc[:].indirect(idx[:]))
-            for q in range(4):
-                nc.sync.dma_start(words(v_sc1[32 * q : 32 * q + 4, :]), words(v_sc[32 * q + 4 : 32 * q + 8, :]))
-            load_table(0)
-            load_table(1)
+            for a in range(2):
+                for q in range(4):
+                    row = 16 * a + 4 * q
+                    nc.sync.dma_start(words(v_planes[a][32 * q : 32 * q + 4, :]), words(v_sc[row : row + 4, :]))
+                load_table(a)
             for x in range(4):
                 nc.gpsimd.tensor_copy(
                     w2[:, x * H : (x + 1) * H].rearrange("p (t m e) -> p t m e", t=PACK, e=2),

@@ -276,7 +276,7 @@ def tile_list_newton_clock_step_kernel(
             )
 
         halves = [(0, BANK), (BANK, S)]
-        pieces = [(lo, lo + 256) for lo in range(0, S, 256)]
+        pieces = [(0, 256), (256, 512), (512, 768), (768, 896), (896, 1024)]
 
         def pick_pair(k):
             prods = [product_tile(lo, hi) for lo, hi in halves]
@@ -303,7 +303,7 @@ def tile_list_newton_clock_step_kernel(
             return accs
 
         def close_sums(accs, i):
-            for c in (0, 2, 1, 3):
+            for c in (0, 2, 1, 3) if i == len(pieces) - 1 else range(4):
                 project(accs[c], 1, c, *pieces[i])
 
         def staging(i):
@@ -330,18 +330,15 @@ def tile_list_newton_clock_step_kernel(
 
         def finish(accs, i):
             rows = staging(i)
-            for c in (0, 2, 1, 3):
-                add_trim(rows, accs, i, c, i >= 2 and c >= 2)
-            if i == len(pieces) - 1:
-                store(nc.scalar, rows, i, 0, 2)
-                store(nc.sync, rows, i, 2, 4)
-            else:
-                store(nc.sync, rows, i, 0, 4)
+            for c in range(4):
+                add_trim(rows, accs, i, c, i == len(pieces) - 1 and c >= 2)
+            store(nc.scalar if i == len(pieces) - 1 else nc.sync, rows, i, 0, 2)
+            store(nc.sync, rows, i, 2, 4)
 
         def last_step(prod, i, weave):
             lo, hi = pieces[i]
             newton(z_second[i], lo, prod, lo, 3, lo, hi)
-            return weave_z(z_second[i], "quads%d" % (0, 1, 2, 4)[i], weave)
+            return weave_z(z_second[i], "quads%d" % i, weave)
 
         prods = [product_tile(*pieces[i]) for i in range(2)]
         for s in (6, 7):
@@ -349,17 +346,17 @@ def tile_list_newton_clock_step_kernel(
                 pick_product(prods[i], s, *pieces[i])
         quads = [last_step(prods[i], i, nc.scalar.copy) for i in range(2)]
         quantise_z(quads_first, 0, 0, S)
-        sums = [multiply(quads[i], i) for i in range(2)]
-        prods = [product_tile(*pieces[2], "page_codes", 1), product_tile(*pieces[3], "quads0", 1)]
-        pick_product(prods[0], 6, *pieces[2])
-        pick_product(prods[0], 7, *pieces[2])
-        pick_product(prods[1], 6, *pieces[3])
-        finish(sums[0], 0)
-        quads2 = last_step(prods[0], 2, nc.scalar.copy)
-        finish(sums[1], 1)
-        pick_product(prods[1], 7, *pieces[3])
-        sums2 = multiply(quads2, 2)
-        quads3 = last_step(prods[1], 3, nc.vector.tensor_copy)
-        sums3 = multiply(quads3, 3)
-        finish(sums2, 2)
-        finish(sums3, 3)
+        finish(multiply(quads[0], 0), 0)
+        prod = product_tile(*pieces[2], "page_codes", 1)
+        pick_product(prod, 6, *pieces[2])
+        ready = quads[1]
+        for i in range(2, len(pieces)):
+            lo, hi = pieces[i]
+            pick_product(prod, 7, lo, hi)
+            finish(multiply(ready, i - 1), i - 1)
+            newton(z_second[i], lo, prod, lo, 3, lo, hi)
+            if i + 1 < len(pieces):
+                prod = product_tile(*pieces[i + 1], "quads%d" % (i - 2), 1)
+                pick_product(prod, 6, *pieces[i + 1])
+            ready = weave_z(z_second[i], "z_quads%d" % i, nc.vector.tensor_copy)
+        finish(multiply(ready, len(pieces) - 1), len(pieces) - 1)

@@ -20,8 +20,18 @@ S = 1024
 H = 1024
 N = 512
 BANK = 512
+BANKS = 8
 GROUP = 16
+SLICES = H // P
 FLOPS = 2 * (512 * H * T + 1024 * H * S + H * N * S)
+
+FIRST_BLOCK = 256
+PAGE_CUTS = [(0, 512), (512, 768), (768, 1024), (1024, 1536), (1536, 2048)]
+GPSIMD_CUTS = 2
+SHARED_CUT = 3
+HALVES = [(0, BANK), (BANK, S)]
+PIECES = [(0, 256), (256, 512), (512, 768), (768, 896), (896, 1024)]
+LAST = len(PIECES) - 1
 
 
 def tile_list_newton_clock_step_kernel(
@@ -39,7 +49,7 @@ def tile_list_newton_clock_step_kernel(
         banks_taken = []
 
         def bank():
-            tag = "bank%d" % (len(banks_taken) % 8)
+            tag = "bank%d" % (len(banks_taken) % BANKS)
             banks_taken.append(tag)
             return psum.tile([P, BANK], F32, name=tag, tag=tag)
 
@@ -53,26 +63,25 @@ def tile_list_newton_clock_step_kernel(
         tab_sc = sb([P, T], U8, "tab_sc")
         w2_sc_raw = sb([P, 2 * H], U8, "quads1")
         w3_sc = sb([P, 2 * N], U8, "w3_sc")
-        v_planes = [sb([P, S], U8, "v_plane%d" % a) for a in range(2)]
+        v_sc = [sb([P, S], U8, "v_sc%d" % a) for a in range(2)]
         nc.vector.memset(words(tab_sc[32:64, :]), 0)
         nc.vector.memset(words(tab_sc[64:, :]), 0)
-        for plane in (w2_sc_raw, *v_planes, w3_sc):
-            nc.vector.memset(words(plane[:]), 0)
+        for scale_tile in (w2_sc_raw, *v_sc, w3_sc):
+            nc.vector.memset(words(scale_tile[:]), 0)
 
         page = [sb([P, T], F32, "wide%d" % t) for t in range(PACK)]
         w1_raw = [sb([P, PACK * BANK], F32, "wide%d" % (4 + g)) for g in range(2)]
         tab = [sb([P, T], U32, "wide%d" % (6 + a)) for a in range(2)]
-        w2_raw = [sb([P, 2 * H], U8, tag) for tag in ("quads0", "quads3")]
+        w2_raw = [sb([P, 2 * H], U8, tag) for tag in ("quads0", "quads%d" % SHARED_CUT)]
         w3 = sb([P, 2 * N], U32, "w3")
         trim_sb = sb([P, N // P], F32, "trim")
-        page_cuts = [(0, 512), (512, 768), (768, 1024), (1024, 1536), (1536, 2048)]
         w1_quads = [sb([P, PACK * BANK], BF16, "w1_quads%d" % g) for g in range(2)]
 
         w2 = sb([P, 2 * 2 * H], U8, "w2")
         w2_sc = sb([P, 2 * H], U8, "w2_sc")
-        v_sc = sb([P, S], U8, "v_sc")
+        picked_sc_rows = sb([P, S], U8, "picked_sc_rows")
         v_early = [sb([P, BANK], U32, "v_early%d" % a) for a in range(2)]
-        b_pairs = [sb([P, 2 * S], F32, "b%d" % k) for k in range(4)]
+        b_pairs = [sb([P, 2 * S], F32, "b%d" % k) for k in range(SLICES // 2)]
 
         def pick_words(picked_words, a, h):
             at = h * BANK // GROUP
@@ -82,55 +91,60 @@ def tile_list_newton_clock_step_kernel(
             cols = slice(h * BANK, (h + 1) * BANK)
             acc = bank()
             for a in range(2):
-                lo = a * H + s * P
+                w_at = a * H + s * P
                 nc.tensor.matmul_mx(
-                    acc[:], lhsT=w2[:, 2 * lo : 2 * (lo + P)].bitcast(FP4X4), lhsT_scale=w2_sc[:, lo : lo + P],
-                    rhs=v[a][:].bitcast(FP8X4), rhs_scale=v_planes[a][:, cols], start=a == 0, stop=a == 1,
+                    acc[:], lhsT=w2[:, 2 * w_at : 2 * (w_at + P)].bitcast(FP4X4),
+                    lhsT_scale=w2_sc[:, w_at : w_at + P],
+                    rhs=v[a][:].bitcast(FP8X4), rhs_scale=v_sc[a][:, cols], start=a == 0, stop=a == 1,
                 )
-            lo = (s % 2) * S + h * BANK
-            nc.scalar.copy(b_pairs[s // 2][:, lo : lo + BANK], acc[:])
+            b_at = (s % 2) * S + h * BANK
+            nc.scalar.copy(b_pairs[s // 2][:, b_at : b_at + BANK], acc[:])
+
+        def round_on_gpsimd(rounded, raw):
+            nc.gpsimd.tensor_scalar(rounded, raw, 1.0, 0.0, ALU.mult, ALU.add)
 
         base_planes = base.rearrange("(p t) c -> t p c", t=PACK)
         xs_planes = xs.rearrange("(p t) j -> t p j", t=PACK)
         w1_rows = w1.rearrange("(p t) r -> p t r", t=PACK)
 
         with tc.tile_pool(name="arrivals", bufs=1) as arrivals:
-            cuts = [[(0, 256), (256, S)]] + [[(0, S)]] * (PACK - 1)
+            block_cuts = [[(0, FIRST_BLOCK), (FIRST_BLOCK, S)]] + [[(0, S)]] * (PACK - 1)
             blocks = [
-                [arrivals.tile([P, hi - lo], F32, name="xs%d_%d" % (t, lo), align_bytes=64) for lo, hi in cuts[t]]
+                [arrivals.tile([P, hi - lo], F32, name="xs%d_%d" % (t, lo), align_bytes=64) for lo, hi in block_cuts[t]]
                 for t in range(PACK)
             ]
 
             def load_plane(t):
                 nc.sync.dma_start(page[t][:], base_planes[t])
-                for block, (lo, hi) in zip(blocks[t], cuts[t]):
+                for block, (lo, hi) in zip(blocks[t], block_cuts[t]):
                     nc.sync.dma_start(block[:], xs_planes[t][:, lo:hi])
-
-            def load_table(a):
-                nc.sync.dma_start(words(tab[a][:]), words(tab_words[a].rearrange("p t i -> p (t i)")))
 
             def load_w1(g):
                 nc.sync.dma_start(
                     w1_raw[g][:].rearrange("p (t r) -> p t r", t=PACK), w1_rows[:, :, g * BANK : (g + 1) * BANK]
                 )
 
-            def place(t):
-                for block, (lo, hi) in zip(blocks[t], cuts[t]):
-                    nc.vector.tensor_copy(page[t][:].indirect(idx2[:, lo // GROUP : hi // GROUP]), block[:])
-                for c, (lo, hi) in enumerate(page_cuts):
-                    slots = page_quads[c][:].rearrange("p (c t) -> p c t", t=PACK)[:, :, t]
-                    if c < 2 or (t < 2 and c == 3):
-                        nc.gpsimd.tensor_scalar(slots, page[t][:, lo:hi], 1.0, 0.0, ALU.mult, ALU.add)
-                    else:
-                        nc.scalar.copy(slots, page[t][:, lo:hi])
+            def load_scales(scale_tile, scales):
+                for q in range(4):
+                    nc.sync.dma_start(
+                        words(scale_tile[32 * q : 32 * q + 4, :]).rearrange("r (a c) -> r a c", a=2),
+                        words(scales[:, 4 * q : 4 * q + 4, :]).rearrange("a r c -> r a c"),
+                    )
 
-            def round_w1(g):
-                rounded = w1_quads[g][:].rearrange("p (t m j) -> p m t j", t=PACK, j=PACK)
-                raw = w1_raw[g][:].rearrange("p (j m t) -> p m t j", j=PACK, t=PACK)
-                if g == 0:
-                    nc.scalar.activation(rounded, raw, ACT.Copy)
-                else:
-                    nc.gpsimd.tensor_scalar(rounded, raw, 1.0, 0.0, ALU.mult, ALU.add)
+            def place(t):
+                for block, (lo, hi) in zip(blocks[t], block_cuts[t]):
+                    nc.vector.tensor_copy(page[t][:].indirect(idx2[:, lo // GROUP : hi // GROUP]), block[:])
+                for c, (lo, hi) in enumerate(PAGE_CUTS):
+                    rounded = page_quads[c][:].rearrange("p (c t) -> p c t", t=PACK)[:, :, t]
+                    if c < GPSIMD_CUTS or (t < 2 and c == SHARED_CUT):
+                        round_on_gpsimd(rounded, page[t][:, lo:hi])
+                    else:
+                        nc.scalar.copy(rounded, page[t][:, lo:hi])
+
+            def w1_views(g, t0, t1):
+                rounded = w1_quads[g][:].rearrange("p (t m j) -> p m t j", t=PACK, j=PACK)[:, :, t0:t1, :]
+                raw = w1_raw[g][:].rearrange("p (j m t) -> p m t j", j=PACK, t=PACK)[:, :, t0:t1, :]
+                return rounded, raw
 
             nc.sync.dma_start(idx[:], offs)
             nc.sync.dma_start(words(tab_sc[:32, :]), words(tab_scales.rearrange("a q t -> (a q) t")))
@@ -138,31 +152,28 @@ def tile_list_newton_clock_step_kernel(
             load_plane(0)
             for a in range(2):
                 nc.sync.dma_start(words(w2_raw[a][:]), words(w2_words[a]))
-            for q in range(4):
-                nc.sync.dma_start(
-                    words(w2_sc_raw[32 * q : 32 * q + 4, :]).rearrange("r (a c) -> r a c", a=2),
-                    words(w2_scales[:, 4 * q : 4 * q + 4, :]).rearrange("a r c -> r a c"),
-                )
+            load_scales(w2_sc_raw, w2_scales)
             load_plane(1)
             load_w1(0)
 
-            nc.vector.tensor_copy(v_sc[:], tab_sc[:].indirect(idx[:]))
+            nc.vector.tensor_copy(picked_sc_rows[:], tab_sc[:].indirect(idx[:]))
             for a in range(2):
                 for q in range(4):
                     row = 16 * a + 4 * q
-                    nc.sync.dma_start(words(v_planes[a][32 * q : 32 * q + 4, :]), words(v_sc[row : row + 4, :]))
-                load_table(a)
+                    nc.sync.dma_start(words(v_sc[a][32 * q : 32 * q + 4, :]), words(picked_sc_rows[row : row + 4, :]))
+                nc.sync.dma_start(words(tab[a][:]), words(tab_words[a].rearrange("p t i -> p (t i)")))
+
             for x in range(4):
                 nc.gpsimd.tensor_copy(
-                    w2[:, x * H : (x + 1) * H].rearrange("p (t m e) -> p t m e", t=PACK, e=2),
-                    w2_raw[x // 2][:, x % 2 * H : (x % 2 + 1) * H].rearrange("p (m t e) -> p t m e", t=PACK, e=2),
+                    w2[:, x * H : (x + 1) * H].bitcast(U16).rearrange("p (t m) -> p t m", t=PACK),
+                    w2_raw[x // 2][:, x % 2 * H : (x % 2 + 1) * H].bitcast(U16).rearrange("p (m t) -> p t m", t=PACK),
                 )
             nc.gpsimd.tensor_copy(
                 w2_sc[:].rearrange("p (x t m) -> p x t m", t=PACK, m=P),
                 w2_sc_raw[:].rearrange("p (x m t) -> p x t m", t=PACK, m=P),
             )
 
-            page_quads = [sb([P, PACK * (hi - lo)], BF16, "quads%d" % c) for c, (lo, hi) in enumerate(page_cuts)]
+            page_quads = [sb([P, PACK * (hi - lo)], BF16, "quads%d" % c) for c, (lo, hi) in enumerate(PAGE_CUTS)]
             load_plane(2)
             load_w1(1)
             load_plane(3)
@@ -171,23 +182,20 @@ def tile_list_newton_clock_step_kernel(
                 words(w3[:]).rearrange("p (a c) -> p a c", a=2),
                 words(w3_words.rearrange("a p c i -> a p (c i)")).rearrange("a p c -> p a c"),
             )
-            for q in range(4):
-                nc.sync.dma_start(
-                    words(w3_sc[32 * q : 32 * q + 4, :]).rearrange("r (a c) -> r a c", a=2),
-                    words(w3_scales[:, 4 * q : 4 * q + 4, :]).rearrange("a r c -> r a c"),
-                )
+            load_scales(w3_sc, w3_scales)
             with nc.allow_non_contiguous_dma(reason="one trim value a partition"):
                 nc.sync.dma_start(trim_sb[:], trim.rearrange("(c p) -> p c", p=P))
 
             place(0)
             place(1)
-            round_w1(0)
+            round_on_gpsimd(*w1_views(0, 0, PACK))
             for a in range(2):
                 pick_words(v_early[a], a, 0)
-            for s in range(8):
+            for s in range(SLICES):
                 estimate(v_early, s, 0)
             place(2)
-            round_w1(1)
+            nc.scalar.activation(*w1_views(1, 0, 2), ACT.Copy)
+            round_on_gpsimd(*w1_views(1, 2, PACK))
             place(3)
 
         picked = ctx.enter_context(tc.tile_pool(name="picked", bufs=1))
@@ -203,12 +211,12 @@ def tile_list_newton_clock_step_kernel(
         for a in range(2):
             pick_words(v_late[a], a, 1)
         quantise_w1(0)
-        for c, (lo, hi) in enumerate(page_cuts):
+        for c, (lo, hi) in enumerate(PAGE_CUTS):
             nc.vector.quantize_mx(page_codes[:, lo:hi].bitcast(FP8X4), page_sc[:, lo:hi], page_quads[c][:])
-        w1_codes.append(sb([P, BANK], U32, "quads3"))
+        w1_codes.append(sb([P, BANK], U32, "quads%d" % SHARED_CUT))
         quantise_w1(1)
 
-        neg_a = [sb([P, T], F32, "wide%d" % s) for s in range(8)]
+        neg_a = [sb([P, T], F32, "wide%d" % s) for s in range(SLICES)]
 
         def gain(s, c):
             rows = slice(s % PACK * P, (s % PACK + 1) * P)
@@ -218,17 +226,18 @@ def tile_list_newton_clock_step_kernel(
                 acc[:], lhsT=w1_codes[s // PACK][:, rows].bitcast(FP8X4), lhsT_scale=w1_sc[s // PACK][:, rows],
                 rhs=page_codes[:, cols].bitcast(FP8X4), rhs_scale=page_sc[:, cols], start=True, stop=True,
             )
-            if s == 0 and c == 3:
+            if s == 0 and c == T // BANK - 1:
                 nc.vector.tensor_scalar(neg_a[s][:, cols], acc[:], -1.0, None, ALU.mult)
             else:
                 nc.scalar.activation(neg_a[s][:, cols], acc[:], ACT.Copy, scale=-1.0)
 
-        for s in range(8):
-            for c in range(4):
+        last_pair = (SLICES - 2, SLICES - 1)
+        for s in range(SLICES):
+            for c in range(T // BANK):
                 gain(s, c)
-            if s < 6:
+            if s not in last_pair:
                 estimate(v_late, s, 1)
-        for s in (6, 7):
+        for s in last_pair:
             estimate(v_late, s, 1)
 
         z_codes = [sb([P, S], U32, "z_codes%d" % g) for g in range(2)]
@@ -257,9 +266,9 @@ def tile_list_newton_clock_step_kernel(
                 ALU.mult,
             )
 
-        def weave_z(z_pairs, tag, weave):
+        def weave_z(z_pairs, tag, copy):
             quads = sb(list(z_pairs.shape), BF16, tag)
-            weave(
+            copy(
                 quads[:].bitcast(F32).rearrange("p (j u) -> p j u", u=2),
                 z_pairs[:].bitcast(F32).rearrange("p (u j) -> p j u", u=2),
             )
@@ -275,88 +284,67 @@ def tile_list_newton_clock_step_kernel(
                 rhs=z_codes[g][:, lo:hi].bitcast(FP8X4), rhs_scale=z_sc[g][:, lo:hi], start=g == 0, stop=g == 1,
             )
 
-        halves = [(0, BANK), (BANK, S)]
-        pieces = [(0, 256), (256, 512), (512, 768), (768, 896), (896, 1024)]
-
         def pick_pair(k):
-            prods = [product_tile(lo, hi) for lo, hi in halves]
+            prods = [product_tile(lo, hi) for lo, hi in HALVES]
             for s in (2 * k, 2 * k + 1):
-                for prod, (lo, hi) in zip(prods, halves):
+                for prod, (lo, hi) in zip(prods, HALVES):
                     pick_product(prod, s, lo, hi)
             return prods
 
         z_first = sb([P, PACK * S], BF16, "wide0")
         for k in range(2):
-            for prod, (lo, hi) in zip(pick_pair(k), halves):
+            for prod, (lo, hi) in zip(pick_pair(k), HALVES):
                 newton(z_first, 0, prod, lo, k, lo, hi)
         quads_first = weave_z(z_first, "page_codes", nc.scalar.copy)
 
-        z_second = [sb([P, PACK * (hi - lo)], BF16, "pairs%d" % i) for i, (lo, hi) in enumerate(pieces)]
-        prods = pick_pair(2)
-        for z_pairs, (lo, hi) in zip(z_second, pieces):
-            newton(z_pairs, lo, prods[lo // BANK], lo // BANK * BANK, 2, lo, hi)
+        z_second = [sb([P, PACK * (hi - lo)], BF16, "pairs%d" % i) for i, (lo, hi) in enumerate(PIECES)]
+        third_pair = pick_pair(2)
+        for z_pairs, (lo, hi) in zip(z_second, PIECES):
+            newton(z_pairs, lo, third_pair[lo // BANK], lo // BANK * BANK, 2, lo, hi)
 
-        def open_sums(i):
-            accs = [bank() for c in range(4)]
-            for c in range(4):
-                project(accs[c], 0, c, *pieces[i])
-            return accs
-
-        def close_sums(accs, i):
-            for c in (0, 2, 1, 3) if i == len(pieces) - 1 else range(4):
-                project(accs[c], 1, c, *pieces[i])
-
-        def staging(i):
-            lo, hi = pieces[i]
-            staged = sb([P, 4 * (hi - lo)], F32, "wide%d" % (2 + i))
-            return staged[:].rearrange("p (c j) -> p c j", c=4)
-
-        def add_trim(rows, accs, i, c, on_vector):
-            lo, hi = pieces[i]
-            if on_vector:
-                nc.vector.tensor_scalar(rows[:, c, :], accs[c][:, : hi - lo], trim_sb[:, c : c + 1], None, ALU.add)
-            else:
-                nc.scalar.activation(rows[:, c, :], accs[c][:, : hi - lo], ACT.Identity, bias=trim_sb[:, c : c + 1])
-
-        def store(queue, rows, i, c0, c1):
-            lo, hi = pieces[i]
-            queue.dma_start(out_rows[:, c0:c1, lo:hi], rows[:, c0:c1, :])
-
-        def multiply(quads, i):
-            accs = open_sums(i)
-            quantise_z(quads, 1, *pieces[i])
-            close_sums(accs, i)
-            return accs
-
-        def finish(accs, i):
-            rows = staging(i)
-            for c in range(4):
-                add_trim(rows, accs, i, c, i == len(pieces) - 1 and c >= 2)
-            store(nc.scalar if i == len(pieces) - 1 else nc.sync, rows, i, 0, 2)
-            store(nc.sync, rows, i, 2, 4)
-
-        def last_step(prod, i, weave):
-            lo, hi = pieces[i]
+        def last_newton(prod, i):
+            lo, hi = PIECES[i]
             newton(z_second[i], lo, prod, lo, 3, lo, hi)
-            return weave_z(z_second[i], "quads%d" % i, weave)
 
-        prods = [product_tile(*pieces[i]) for i in range(2)]
-        for s in (6, 7):
+        def finish(quads, i):
+            lo, hi = PIECES[i]
+            accs = [bank() for c in range(N // P)]
+            for c in range(N // P):
+                project(accs[c], 0, c, lo, hi)
+            quantise_z(quads, 1, lo, hi)
+            for c in (0, 2, 1, 3) if i == LAST else range(N // P):
+                project(accs[c], 1, c, lo, hi)
+            staged = sb([P, N // P * (hi - lo)], F32, "wide%d" % (2 + i))
+            rows = staged[:].rearrange("p (c j) -> p c j", c=N // P)
+            for c in range(N // P):
+                sums, offset = accs[c][:, : hi - lo], trim_sb[:, c : c + 1]
+                if i == LAST and c >= 2:
+                    nc.vector.tensor_scalar(rows[:, c, :], sums, offset, None, ALU.add)
+                else:
+                    nc.scalar.activation(rows[:, c, :], sums, ACT.Identity, bias=offset)
+            (nc.scalar if i == LAST else nc.sync).dma_start(out_rows[:, :2, lo:hi], rows[:, :2, :])
+            nc.sync.dma_start(out_rows[:, 2:, lo:hi], rows[:, 2:, :])
+
+        first_prods = [product_tile(*PIECES[i]) for i in range(2)]
+        for s in last_pair:
             for i in range(2):
-                pick_product(prods[i], s, *pieces[i])
-        quads = [last_step(prods[i], i, nc.scalar.copy) for i in range(2)]
+                pick_product(first_prods[i], s, *PIECES[i])
+        first_quads = []
+        for i in range(2):
+            last_newton(first_prods[i], i)
+            first_quads.append(weave_z(z_second[i], "quads%d" % i, nc.scalar.copy))
         quantise_z(quads_first, 0, 0, S)
-        finish(multiply(quads[0], 0), 0)
-        prod = product_tile(*pieces[2], "page_codes", 1)
-        pick_product(prod, 6, *pieces[2])
-        ready = quads[1]
-        for i in range(2, len(pieces)):
-            lo, hi = pieces[i]
-            pick_product(prod, 7, lo, hi)
-            finish(multiply(ready, i - 1), i - 1)
-            newton(z_second[i], lo, prod, lo, 3, lo, hi)
-            if i + 1 < len(pieces):
-                prod = product_tile(*pieces[i + 1], "quads%d" % (i - 2), 1)
-                pick_product(prod, 6, *pieces[i + 1])
-            ready = weave_z(z_second[i], "z_quads%d" % i, nc.vector.tensor_copy)
-        finish(multiply(ready, len(pieces) - 1), len(pieces) - 1)
+        finish(first_quads[0], 0)
+
+        prod = product_tile(*PIECES[2], "page_codes", 1)
+        pick_product(prod, last_pair[0], *PIECES[2])
+        woven = first_quads[1]
+        for i in range(2, len(PIECES)):
+            pick_product(prod, last_pair[1], *PIECES[i])
+            finish(woven, i - 1)
+            last_newton(prod, i)
+            if i < LAST:
+                prod = product_tile(*PIECES[i + 1], "quads%d" % (i - 2), 1)
+                pick_product(prod, last_pair[0], *PIECES[i + 1])
+            woven = weave_z(z_second[i], "z_quads%d" % i, nc.vector.tensor_copy)
+        finish(woven, LAST)

@@ -26,6 +26,7 @@ SLICES = H // P
 FLOPS = 2 * (512 * H * T + 1024 * H * S + H * N * S)
 
 FIRST_BLOCK = 256
+LAST_BLOCK = 256
 PAGE_CUTS = [(0, 512), (512, 768), (768, 1024), (1024, 1536), (1536, 2048)]
 GPSIMD_CUTS = 2
 SHARED_CUT = 3
@@ -108,16 +109,19 @@ def tile_list_newton_clock_step_kernel(
         w1_rows = w1.rearrange("(p t) r -> p t r", t=PACK)
 
         with tc.tile_pool(name="arrivals", bufs=1) as arrivals:
-            block_cuts = [[(0, FIRST_BLOCK), (FIRST_BLOCK, S)]] + [[(0, S)]] * (PACK - 1)
+            block_cuts = [[(0, FIRST_BLOCK), (FIRST_BLOCK, S)], [(0, S)], [(0, S)], [(0, S - LAST_BLOCK), (S - LAST_BLOCK, S)]]
             blocks = [
                 [arrivals.tile([P, hi - lo], F32, name="xs%d_%d" % (t, lo), align_bytes=64) for lo, hi in block_cuts[t]]
                 for t in range(PACK)
             ]
 
+            def load_block(t, i):
+                lo, hi = block_cuts[t][i]
+                nc.sync.dma_start(blocks[t][i][:], xs_planes[t][:, lo:hi])
+
             def load_plane(t):
                 nc.sync.dma_start(page[t][:], base_planes[t])
-                for block, (lo, hi) in zip(blocks[t], block_cuts[t]):
-                    nc.sync.dma_start(block[:], xs_planes[t][:, lo:hi])
+                load_block(t, 0)
 
             def load_w1(g):
                 nc.sync.dma_start(
@@ -150,18 +154,18 @@ def tile_list_newton_clock_step_kernel(
             nc.sync.dma_start(words(tab_sc[:32, :]), words(tab_scales.rearrange("a q t -> (a q) t")))
             nc.sync.dma_start(idx2[:], offs2)
             load_plane(0)
+            load_block(0, 1)
+            load_plane(1)
             for a in range(2):
                 nc.sync.dma_start(words(w2_raw[a][:]), words(w2_words[a]))
             load_scales(w2_sc_raw, w2_scales)
-            load_plane(1)
-            load_w1(0)
 
             nc.vector.tensor_copy(picked_sc_rows[:], tab_sc[:].indirect(idx[:]))
             for a in range(2):
+                nc.sync.dma_start(words(tab[a][:]), words(tab_words[a].rearrange("p t i -> p (t i)")))
                 for q in range(4):
                     row = 16 * a + 4 * q
                     nc.sync.dma_start(words(v_sc[a][32 * q : 32 * q + 4, :]), words(picked_sc_rows[row : row + 4, :]))
-                nc.sync.dma_start(words(tab[a][:]), words(tab_words[a].rearrange("p t i -> p (t i)")))
 
             for x in range(4):
                 nc.gpsimd.tensor_copy(
@@ -175,8 +179,10 @@ def tile_list_newton_clock_step_kernel(
 
             page_quads = [sb([P, PACK * (hi - lo)], BF16, "quads%d" % c) for c, (lo, hi) in enumerate(PAGE_CUTS)]
             load_plane(2)
-            load_w1(1)
+            load_w1(0)
             load_plane(3)
+            load_w1(1)
+            load_block(3, 1)
             nc.sync.dma_start(idx3[:], offs3)
             nc.sync.dma_start(
                 words(w3[:]).rearrange("p (a c) -> p a c", a=2),

@@ -25,11 +25,10 @@ GROUP = 16
 SLICES = H // P
 FLOPS = 2 * (512 * H * T + 1024 * H * S + H * N * S)
 
-FIRST_BLOCK = 256
-LAST_BLOCK = 256
-PAGE_CUTS = [(0, 512), (512, 768), (768, 1024), (1024, 1536), (1536, 2048)]
-GPSIMD_CUTS = 2
-SHARED_CUT = 3
+SMALL_BLOCK = 256
+PLANE_ORDER = (2, 0, 1, 3)
+GPSIMD_COLUMNS = (2048, 704)
+BANK_ORDER = (0, 1, 2, 3)
 HALVES = [(0, BANK), (BANK, S)]
 PIECES = [(0, 256), (256, 512), (512, 768), (768, 896), (896, 1024)]
 LAST = len(PIECES) - 1
@@ -73,7 +72,7 @@ def tile_list_newton_clock_step_kernel(
         page = [sb([P, T], F32, "wide%d" % t) for t in range(PACK)]
         w1_raw = [sb([P, PACK * BANK], F32, "wide%d" % (4 + g)) for g in range(2)]
         tab = [sb([P, T], U32, "wide%d" % (6 + a)) for a in range(2)]
-        w2_raw = [sb([P, 2 * H], U8, tag) for tag in ("quads0", "quads%d" % SHARED_CUT)]
+        w2_raw = sb([P, 2 * 2 * H], U8, "quads0")
         w3 = sb([P, 2 * N], U32, "w3")
         trim_sb = sb([P, N // P], F32, "trim")
         w1_quads = [sb([P, PACK * BANK], BF16, "w1_quads%d" % g) for g in range(2)]
@@ -81,14 +80,14 @@ def tile_list_newton_clock_step_kernel(
         w2 = sb([P, 2 * 2 * H], U8, "w2")
         w2_sc = sb([P, 2 * H], U8, "w2_sc")
         picked_sc_rows = sb([P, S], U8, "picked_sc_rows")
-        v_early = [sb([P, BANK], U32, "v_early%d" % a) for a in range(2)]
+        v = [[sb([P, BANK], U32, "v_early%d" % a)] for a in range(2)]
         b_pairs = [sb([P, 2 * S], F32, "b%d" % k) for k in range(SLICES // 2)]
 
         def pick_words(picked_words, a, h):
             at = h * BANK // GROUP
             nc.vector.tensor_copy(picked_words[:], tab[a][:].indirect(idx[:, at : at + BANK // GROUP]))
 
-        def estimate(v, s, h):
+        def estimate(s, h):
             cols = slice(h * BANK, (h + 1) * BANK)
             acc = bank()
             for a in range(2):
@@ -96,7 +95,7 @@ def tile_list_newton_clock_step_kernel(
                 nc.tensor.matmul_mx(
                     acc[:], lhsT=w2[:, 2 * w_at : 2 * (w_at + P)].bitcast(FP4X4),
                     lhsT_scale=w2_sc[:, w_at : w_at + P],
-                    rhs=v[a][:].bitcast(FP8X4), rhs_scale=v_sc[a][:, cols], start=a == 0, stop=a == 1,
+                    rhs=v[a][h][:].bitcast(FP8X4), rhs_scale=v_sc[a][:, cols], start=a == 0, stop=a == 1,
                 )
             b_at = (s % 2) * S + h * BANK
             nc.scalar.copy(b_pairs[s // 2][:, b_at : b_at + BANK], acc[:])
@@ -109,7 +108,7 @@ def tile_list_newton_clock_step_kernel(
         w1_rows = w1.rearrange("(p t) r -> p t r", t=PACK)
 
         with tc.tile_pool(name="arrivals", bufs=1) as arrivals:
-            block_cuts = [[(0, FIRST_BLOCK), (FIRST_BLOCK, S)], [(0, S)], [(0, S)], [(0, S - LAST_BLOCK), (S - LAST_BLOCK, S)]]
+            block_cuts = [[(0, S)], [(0, S)], [(0, SMALL_BLOCK), (SMALL_BLOCK, S)], [(0, S)]]
             blocks = [
                 [arrivals.tile([P, hi - lo], F32, name="xs%d_%d" % (t, lo), align_bytes=64) for lo, hi in block_cuts[t]]
                 for t in range(PACK)
@@ -138,12 +137,15 @@ def tile_list_newton_clock_step_kernel(
             def place(t):
                 for block, (lo, hi) in zip(blocks[t], block_cuts[t]):
                     nc.vector.tensor_copy(page[t][:].indirect(idx2[:, lo // GROUP : hi // GROUP]), block[:])
-                for c, (lo, hi) in enumerate(PAGE_CUTS):
+                split = GPSIMD_COLUMNS[t // 2]
+                for c in range(T // BANK):
+                    at = c * BANK
                     rounded = page_quads[c][:].rearrange("p (c t) -> p c t", t=PACK)[:, :, t]
-                    if c < GPSIMD_CUTS or (t < 2 and c == SHARED_CUT):
-                        round_on_gpsimd(rounded, page[t][:, lo:hi])
-                    else:
-                        nc.scalar.copy(rounded, page[t][:, lo:hi])
+                    mid = min(max(split - at, 0), BANK)
+                    if mid > 0:
+                        round_on_gpsimd(rounded[:, :mid], page[t][:, at : at + mid])
+                    if mid < BANK:
+                        nc.scalar.copy(rounded[:, mid:], page[t][:, at + mid : at + BANK])
 
             def w1_views(g, t0, t1):
                 rounded = w1_quads[g][:].rearrange("p (t m j) -> p m t j", t=PACK, j=PACK)[:, :, t0:t1, :]
@@ -153,12 +155,11 @@ def tile_list_newton_clock_step_kernel(
             nc.sync.dma_start(idx[:], offs)
             nc.sync.dma_start(words(tab_sc[:32, :]), words(tab_scales.rearrange("a q t -> (a q) t")))
             nc.sync.dma_start(idx2[:], offs2)
-            load_plane(0)
-            load_block(0, 1)
-            load_plane(1)
-            for a in range(2):
-                nc.sync.dma_start(words(w2_raw[a][:]), words(w2_words[a]))
+            load_plane(PLANE_ORDER[0])
+            load_block(PLANE_ORDER[0], 1)
+            nc.sync.dma_start(words(w2_raw[:]).rearrange("p (a c) -> p a c", a=2), words(w2_words).rearrange("a p c -> p a c"))
             load_scales(w2_sc_raw, w2_scales)
+            load_plane(PLANE_ORDER[1])
 
             nc.vector.tensor_copy(picked_sc_rows[:], tab_sc[:].indirect(idx[:]))
             for a in range(2):
@@ -170,19 +171,18 @@ def tile_list_newton_clock_step_kernel(
             for x in range(4):
                 nc.gpsimd.tensor_copy(
                     w2[:, x * H : (x + 1) * H].bitcast(U16).rearrange("p (t m) -> p t m", t=PACK),
-                    w2_raw[x // 2][:, x % 2 * H : (x % 2 + 1) * H].bitcast(U16).rearrange("p (m t) -> p t m", t=PACK),
+                    w2_raw[:, x * H : (x + 1) * H].bitcast(U16).rearrange("p (m t) -> p t m", t=PACK),
                 )
             nc.gpsimd.tensor_copy(
                 w2_sc[:].rearrange("p (x t m) -> p x t m", t=PACK, m=P),
                 w2_sc_raw[:].rearrange("p (x m t) -> p x t m", t=PACK, m=P),
             )
 
-            page_quads = [sb([P, PACK * (hi - lo)], BF16, "quads%d" % c) for c, (lo, hi) in enumerate(PAGE_CUTS)]
-            load_plane(2)
+            page_quads = [sb([P, PACK * BANK], BF16, "quads%d" % c) for c in range(T // BANK)]
+            load_plane(PLANE_ORDER[2])
             load_w1(0)
-            load_plane(3)
             load_w1(1)
-            load_block(3, 1)
+            load_plane(PLANE_ORDER[3])
             nc.sync.dma_start(idx3[:], offs3)
             nc.sync.dma_start(
                 words(w3[:]).rearrange("p (a c) -> p a c", a=2),
@@ -192,20 +192,20 @@ def tile_list_newton_clock_step_kernel(
             with nc.allow_non_contiguous_dma(reason="one trim value a partition"):
                 nc.sync.dma_start(trim_sb[:], trim.rearrange("(c p) -> p c", p=P))
 
-            place(0)
-            place(1)
-            round_on_gpsimd(*w1_views(0, 0, PACK))
+            place(PLANE_ORDER[0])
+            place(PLANE_ORDER[1])
             for a in range(2):
-                pick_words(v_early[a], a, 0)
+                pick_words(v[a][0], a, 0)
             for s in range(SLICES):
-                estimate(v_early, s, 0)
-            place(2)
-            nc.scalar.activation(*w1_views(1, 0, 2), ACT.Copy)
-            round_on_gpsimd(*w1_views(1, 2, PACK))
-            place(3)
+                estimate(s, 0)
+            for g in range(2):
+                nc.scalar.activation(*w1_views(g, 0, PACK), ACT.Copy)
+            place(PLANE_ORDER[2])
+            place(PLANE_ORDER[3])
 
         picked = ctx.enter_context(tc.tile_pool(name="picked", bufs=1))
-        v_late = [picked.tile([P, BANK], U32, name="v_late%d" % a, align_bytes=64) for a in range(2)]
+        for a in range(2):
+            v[a].append(picked.tile([P, BANK], U32, name="v_late%d" % a, align_bytes=64))
         w1_codes = [picked.tile([P, BANK], U32, name="w1_codes0", align_bytes=64)]
         w1_sc = [sb([P, BANK], U8, "w1_sc%d" % g) for g in range(2)]
         page_codes = sb([P, T], U32, "page_codes")
@@ -215,11 +215,12 @@ def tile_list_newton_clock_step_kernel(
             nc.vector.quantize_mx(w1_codes[g][:].bitcast(FP8X4), w1_sc[g][:], w1_quads[g][:])
 
         for a in range(2):
-            pick_words(v_late[a], a, 1)
+            pick_words(v[a][1], a, 1)
         quantise_w1(0)
-        for c, (lo, hi) in enumerate(PAGE_CUTS):
-            nc.vector.quantize_mx(page_codes[:, lo:hi].bitcast(FP8X4), page_sc[:, lo:hi], page_quads[c][:])
-        w1_codes.append(sb([P, BANK], U32, "quads%d" % SHARED_CUT))
+        for c in BANK_ORDER:
+            cols = slice(c * BANK, (c + 1) * BANK)
+            nc.vector.quantize_mx(page_codes[:, cols].bitcast(FP8X4), page_sc[:, cols], page_quads[c][:])
+        w1_codes.append(sb([P, BANK], U32, "quads%d" % BANK_ORDER[-2]))
         quantise_w1(1)
 
         neg_a = [sb([P, T], F32, "wide%d" % s) for s in range(SLICES)]
@@ -232,19 +233,19 @@ def tile_list_newton_clock_step_kernel(
                 acc[:], lhsT=w1_codes[s // PACK][:, rows].bitcast(FP8X4), lhsT_scale=w1_sc[s // PACK][:, rows],
                 rhs=page_codes[:, cols].bitcast(FP8X4), rhs_scale=page_sc[:, cols], start=True, stop=True,
             )
-            if s == 0 and c == T // BANK - 1:
+            if s == 0 and c == BANK_ORDER[-1]:
                 nc.vector.tensor_scalar(neg_a[s][:, cols], acc[:], -1.0, None, ALU.mult)
             else:
                 nc.scalar.activation(neg_a[s][:, cols], acc[:], ACT.Copy, scale=-1.0)
 
         last_pair = (SLICES - 2, SLICES - 1)
         for s in range(SLICES):
-            for c in range(T // BANK):
+            for c in BANK_ORDER:
                 gain(s, c)
             if s not in last_pair:
-                estimate(v_late, s, 1)
+                estimate(s, 1)
         for s in last_pair:
-            estimate(v_late, s, 1)
+            estimate(s, 1)
 
         z_codes = [sb([P, S], U32, "z_codes%d" % g) for g in range(2)]
         z_sc = [sb([P, S], U8, "z_sc%d" % g) for g in range(2)]

@@ -70,7 +70,7 @@ def tile_list_newton_clock_step_kernel(
             nc.vector.memset(words(scale_tile[:]), 0)
 
         page = [sb([P, T], F32, "wide%d" % t) for t in range(PACK)]
-        w1_raw = [sb([P, PACK * BANK], F32, "wide%d" % (4 + g)) for g in range(2)]
+        w1_raw = sb([P, PACK * H], F32, "w1_raw")
         tab = [sb([P, T], U32, "wide%d" % (6 + a)) for a in range(2)]
         w2_raw = sb([P, 2 * 2 * H], U8, "quads0")
         w3 = sb([P, 2 * N], U32, "w3")
@@ -105,7 +105,6 @@ def tile_list_newton_clock_step_kernel(
 
         base_planes = base.rearrange("(p t) c -> t p c", t=PACK)
         xs_planes = xs.rearrange("(p t) j -> t p j", t=PACK)
-        w1_rows = w1.rearrange("(p t) r -> p t r", t=PACK)
 
         with tc.tile_pool(name="arrivals", bufs=1) as arrivals:
             block_cuts = [[(0, S)], [(0, S)], [(0, SMALL_BLOCK), (SMALL_BLOCK, S)], [(0, S)]]
@@ -121,11 +120,6 @@ def tile_list_newton_clock_step_kernel(
             def load_plane(t):
                 nc.sync.dma_start(page[t][:], base_planes[t])
                 load_block(t, 0)
-
-            def load_w1(g):
-                nc.sync.dma_start(
-                    w1_raw[g][:].rearrange("p (t r) -> p t r", t=PACK), w1_rows[:, :, g * BANK : (g + 1) * BANK]
-                )
 
             def load_scales(scale_tile, scales):
                 for q in range(4):
@@ -149,7 +143,7 @@ def tile_list_newton_clock_step_kernel(
 
             def w1_views(g, t0, t1):
                 rounded = w1_quads[g][:].rearrange("p (t m j) -> p m t j", t=PACK, j=PACK)[:, :, t0:t1, :]
-                raw = w1_raw[g][:].rearrange("p (j m t) -> p m t j", j=PACK, t=PACK)[:, :, t0:t1, :]
+                raw = w1_raw[:].rearrange("p (j g m t) -> p g m t j", j=PACK, g=2, t=PACK)[:, g, :, t0:t1, :]
                 return rounded, raw
 
             nc.sync.dma_start(idx[:], offs)
@@ -180,8 +174,7 @@ def tile_list_newton_clock_step_kernel(
 
             page_quads = [sb([P, PACK * BANK], BF16, "quads%d" % c) for c in range(T // BANK)]
             load_plane(PLANE_ORDER[2])
-            load_w1(0)
-            load_w1(1)
+            nc.sync.dma_start(w1_raw[:], w1.rearrange("(p j) r -> p (j r)", j=PACK))
             load_plane(PLANE_ORDER[3])
             nc.sync.dma_start(idx3[:], offs3)
             nc.sync.dma_start(
@@ -254,18 +247,19 @@ def tile_list_newton_clock_step_kernel(
         def product_tile(lo, hi, tag="prod", bufs=4):
             return sb([P, 2 * (hi - lo)], F32, tag, bufs=bufs)
 
-        def pick_product(prod, s, lo, hi):
+        def pick_product(prod, s, lo, hi, prod_first_col=None):
             at = (s % 2) * S
+            prod_at = (s % 2) * prod.shape[1] // 2 + (0 if prod_first_col is None else lo - prod_first_col)
             nc.vector.tensor_tensor(
-                prod[:, (s % 2) * (hi - lo) : (s % 2 + 1) * (hi - lo)],
+                prod[:, prod_at : prod_at + hi - lo],
                 neg_a[s][:].indirect(idx3[:, lo // GROUP : hi // GROUP]),
                 b_pairs[s // 2][:, at + lo : at + hi],
                 ALU.mult,
             )
 
-        def newton(z_pairs, z_first_col, prod, prod_first_col, k, lo, hi):
+        def newton(z_pairs, prod, prod_first_col, k, lo, hi):
             nc.vector.scalar_tensor_tensor(
-                z_pairs[:].rearrange("p (u j e) -> p u j e", u=2, e=2)[:, k % 2, lo - z_first_col : hi - z_first_col, :],
+                z_pairs[:].rearrange("p (u j e) -> p u j e", u=2, e=2)[:, k % 2, lo:hi, :],
                 prod[:].rearrange("p (e j) -> p j e", e=2)[:, lo - prod_first_col : hi - prod_first_col, :],
                 2.0,
                 b_pairs[k][:].rearrange("p (e j) -> p j e", e=2)[:, lo:hi, :],
@@ -273,11 +267,11 @@ def tile_list_newton_clock_step_kernel(
                 ALU.mult,
             )
 
-        def weave_z(z_pairs, tag, copy):
-            quads = sb(list(z_pairs.shape), BF16, tag)
+        def weave_z(z_pairs, lo, hi, tag, copy):
+            quads = sb([P, PACK * (hi - lo)], BF16, tag)
             copy(
                 quads[:].bitcast(F32).rearrange("p (j u) -> p j u", u=2),
-                z_pairs[:].bitcast(F32).rearrange("p (u j) -> p j u", u=2),
+                z_pairs[:].bitcast(F32).rearrange("p (u j) -> p j u", u=2)[:, lo:hi, :],
             )
             return quads
 
@@ -301,17 +295,16 @@ def tile_list_newton_clock_step_kernel(
         z_first = sb([P, PACK * S], BF16, "wide0")
         for k in range(2):
             for prod, (lo, hi) in zip(pick_pair(k), HALVES):
-                newton(z_first, 0, prod, lo, k, lo, hi)
-        quads_first = weave_z(z_first, "page_codes", nc.scalar.copy)
+                newton(z_first, prod, lo, k, lo, hi)
+        quads_first = weave_z(z_first, 0, S, "page_codes", nc.scalar.copy)
 
-        z_second = [sb([P, PACK * (hi - lo)], BF16, "pairs%d" % i) for i, (lo, hi) in enumerate(PIECES)]
-        third_pair = pick_pair(2)
-        for z_pairs, (lo, hi) in zip(z_second, PIECES):
-            newton(z_pairs, lo, third_pair[lo // BANK], lo // BANK * BANK, 2, lo, hi)
+        z_second = sb([P, PACK * S], BF16, "z_second")
+        for prod, (lo, hi) in zip(pick_pair(2), HALVES):
+            newton(z_second, prod, lo, 2, lo, hi)
 
-        def last_newton(prod, i):
+        def last_newton(prod, i, prod_first_col=None):
             lo, hi = PIECES[i]
-            newton(z_second[i], lo, prod, lo, 3, lo, hi)
+            newton(z_second, prod, lo if prod_first_col is None else prod_first_col, 3, lo, hi)
 
         def finish(quads, i):
             lo, hi = PIECES[i]
@@ -329,29 +322,42 @@ def tile_list_newton_clock_step_kernel(
                     nc.vector.tensor_scalar(rows[:, c, :], sums, offset, None, ALU.add)
                 else:
                     nc.scalar.activation(rows[:, c, :], sums, ACT.Identity, bias=offset)
-            (nc.scalar if i == LAST else nc.sync).dma_start(out_rows[:, :2, lo:hi], rows[:, :2, :])
-            nc.sync.dma_start(out_rows[:, 2:, lo:hi], rows[:, 2:, :])
+            if i == LAST:
+                for c in (0, 2, 1, 3):
+                    (nc.scalar if c == 1 else nc.sync).dma_start(out_rows[:, c, lo:hi], rows[:, c, :])
+            else:
+                nc.sync.dma_start(out_rows[:, :2, lo:hi], rows[:, :2, :])
+                nc.sync.dma_start(out_rows[:, 2:, lo:hi], rows[:, 2:, :])
 
-        first_prods = [product_tile(*PIECES[i]) for i in range(2)]
-        for s in last_pair:
-            for i in range(2):
-                pick_product(first_prods[i], s, *PIECES[i])
+        first_prod = product_tile(*HALVES[0])
+        pick_product(first_prod, last_pair[0], *HALVES[0])
+        for i in range(2):
+            pick_product(first_prod, last_pair[1], *PIECES[i], 0)
         first_quads = []
         for i in range(2):
-            last_newton(first_prods[i], i)
-            first_quads.append(weave_z(z_second[i], "quads%d" % i, nc.scalar.copy))
+            last_newton(first_prod, i, 0)
+            first_quads.append(weave_z(z_second, *PIECES[i], "quads%d" % i, nc.scalar.copy))
         quantise_z(quads_first, 0, 0, S)
         finish(first_quads[0], 0)
 
-        prod = product_tile(*PIECES[2], "page_codes", 1)
-        pick_product(prod, last_pair[0], *PIECES[2])
-        woven = first_quads[1]
-        for i in range(2, len(PIECES)):
-            pick_product(prod, last_pair[1], *PIECES[i])
-            finish(woven, i - 1)
-            last_newton(prod, i)
-            if i < LAST:
-                prod = product_tile(*PIECES[i + 1], "quads%d" % (i - 2), 1)
-                pick_product(prod, last_pair[0], *PIECES[i + 1])
-            woven = weave_z(z_second[i], "z_quads%d" % i, nc.vector.tensor_copy)
-        finish(woven, LAST)
+        def weave_piece(i):
+            return weave_z(z_second, *PIECES[i], "z_quads%d" % i, nc.vector.tensor_copy)
+
+        prod2 = product_tile(*PIECES[2], "page_codes", 1)
+        for s in last_pair:
+            pick_product(prod2, s, *PIECES[2])
+        finish(first_quads[1], 1)
+        last_newton(prod2, 2)
+        prod3 = product_tile(*PIECES[3], "quads0", 1)
+        pick_product(prod3, last_pair[0], *PIECES[3])
+        woven2 = weave_piece(2)
+        pick_product(prod3, last_pair[1], *PIECES[3])
+        finish(woven2, 2)
+        prod4 = product_tile(*PIECES[4], "z_quads2", 1)
+        pick_product(prod4, last_pair[0], *PIECES[4])
+        last_newton(prod3, 3)
+        pick_product(prod4, last_pair[1], *PIECES[4])
+        woven3 = weave_piece(3)
+        last_newton(prod4, 4)
+        finish(woven3, 3)
+        finish(weave_piece(4), 4)

@@ -302,6 +302,26 @@ def tile_list_newton_clock_step_kernel(
         for prod, (lo, hi) in zip(pick_pair(2), HALVES):
             newton(z_second, prod, lo, 2, lo, hi)
 
+        late_quads = {}
+        for i in range(2, len(PIECES)):
+            lo, hi = PIECES[i]
+            late_quads[i] = sb([P, PACK * (hi - lo)], BF16, "z_quads%d" % i)
+            nc.scalar.copy(
+                late_quads[i][:].bitcast(F32).rearrange("p (j u) -> p j u", u=2)[:, :, 0],
+                z_second[:].bitcast(F32)[:, lo:hi],
+            )
+
+        def newton_into_quads(prod, i):
+            lo, hi = PIECES[i]
+            nc.vector.scalar_tensor_tensor(
+                late_quads[i][:].rearrange("p (j u e) -> p j u e", u=2, e=2)[:, :, 1, :],
+                prod[:].rearrange("p (e j) -> p j e", e=2),
+                2.0,
+                b_pairs[3][:].rearrange("p (e j) -> p j e", e=2)[:, lo:hi, :],
+                ALU.add,
+                ALU.mult,
+            )
+
         def last_newton(prod, i, prod_first_col=None):
             lo, hi = PIECES[i]
             newton(z_second, prod, lo if prod_first_col is None else prod_first_col, 3, lo, hi)
@@ -312,7 +332,7 @@ def tile_list_newton_clock_step_kernel(
             for c in range(N // P):
                 project(accs[c], 0, c, lo, hi)
             quantise_z(quads, 1, lo, hi)
-            for c in (0, 2, 1, 3) if i == LAST else range(N // P):
+            for c in (2, 0, 3, 1) if i == LAST else range(N // P):
                 project(accs[c], 1, c, lo, hi)
             staged = sb([P, N // P * (hi - lo)], F32, "wide%d" % (2 + i))
             rows = staged[:].rearrange("p (c j) -> p c j", c=N // P)
@@ -323,7 +343,7 @@ def tile_list_newton_clock_step_kernel(
                 else:
                     nc.scalar.activation(rows[:, c, :], sums, ACT.Identity, bias=offset)
             if i == LAST:
-                for c in (0, 2, 1, 3):
+                for c in (2, 0, 3, 1):
                     (nc.scalar if c == 1 else nc.sync).dma_start(out_rows[:, c, lo:hi], rows[:, c, :])
             else:
                 nc.sync.dma_start(out_rows[:, :2, lo:hi], rows[:, :2, :])
@@ -340,24 +360,19 @@ def tile_list_newton_clock_step_kernel(
         quantise_z(quads_first, 0, 0, S)
         finish(first_quads[0], 0)
 
-        def weave_piece(i):
-            return weave_z(z_second, *PIECES[i], "z_quads%d" % i, nc.vector.tensor_copy)
-
         prod2 = product_tile(*PIECES[2], "page_codes", 1)
         for s in last_pair:
             pick_product(prod2, s, *PIECES[2])
         finish(first_quads[1], 1)
-        last_newton(prod2, 2)
+        newton_into_quads(prod2, 2)
         prod3 = product_tile(*PIECES[3], "quads0", 1)
         pick_product(prod3, last_pair[0], *PIECES[3])
-        woven2 = weave_piece(2)
+        finish(late_quads[2], 2)
         pick_product(prod3, last_pair[1], *PIECES[3])
-        finish(woven2, 2)
         prod4 = product_tile(*PIECES[4], "z_quads2", 1)
         pick_product(prod4, last_pair[0], *PIECES[4])
-        last_newton(prod3, 3)
+        newton_into_quads(prod3, 3)
         pick_product(prod4, last_pair[1], *PIECES[4])
-        woven3 = weave_piece(3)
-        last_newton(prod4, 4)
-        finish(woven3, 3)
-        finish(weave_piece(4), 4)
+        finish(late_quads[3], 3)
+        newton_into_quads(prod4, 4)
+        finish(late_quads[4], 4)

@@ -27,7 +27,7 @@ FLOPS = 2 * (512 * H * T + 1024 * H * S + H * N * S)
 
 SMALL_BLOCK = 256
 PLANE_ORDER = (2, 0, 1, 3)
-GPSIMD_COLUMNS = (2048, 704)
+GPSIMD_COLUMNS = (2048, 512)
 BANK_ORDER = (0, 1, 2, 3)
 HALVES = [(0, BANK), (BANK, S)]
 PIECES = [(0, 256), (256, 512), (512, 768), (768, 896), (896, 1024)]

@@ -128,22 +128,22 @@ def tile_list_newton_clock_step_kernel(
                         words(scales[:, 4 * q : 4 * q + 4, :]).rearrange("a r c -> r a c"),
                     )
 
+            def slot(quads, t):
+                return quads[:].rearrange("p (c t) -> p c t", t=PACK)[:, :, t]
+
             def place(t):
                 for block, (lo, hi) in zip(blocks[t], block_cuts[t]):
                     nc.vector.tensor_copy(page[t][:].indirect(idx2[:, lo // GROUP : hi // GROUP]), block[:])
-                split = GPSIMD_COLUMNS[t // 2]
-                for c in range(T // BANK):
-                    at = c * BANK
-                    rounded = page_quads[c][:].rearrange("p (c t) -> p c t", t=PACK)[:, :, t]
-                    mid = min(max(split - at, 0), BANK)
-                    if mid > 0:
-                        round_on_gpsimd(rounded[:, :mid], page[t][:, at : at + mid])
-                    if mid < BANK:
-                        nc.scalar.copy(rounded[:, mid:], page[t][:, at + mid : at + BANK])
+                if t < 2:
+                    round_on_gpsimd(slot(quads_rest, t), page[t][:, BANK:])
+                else:
+                    for at in range(0, T - BANK, BANK):
+                        nc.scalar.copy(slot(quads_rest, t)[:, at : at + BANK], page[t][:, BANK + at : 2 * BANK + at])
+                round_on_gpsimd(slot(quads_head, t), page[t][:, :BANK])
 
             def w1_views(g, t0, t1):
-                rounded = w1_quads[g][:].rearrange("p (t m j) -> p m t j", t=PACK, j=PACK)[:, :, t0:t1, :]
-                raw = w1_raw[:].rearrange("p (j g m t) -> p g m t j", j=PACK, g=2, t=PACK)[:, g, :, t0:t1, :]
+                rounded = w1_quads[g][:].rearrange("p (t m j) -> p m j t", t=PACK, j=PACK)[:, :, :, t0:t1]
+                raw = w1_raw[:].rearrange("p (j g m t) -> p g m j t", j=PACK, g=2, t=PACK)[:, g, :, :, t0:t1]
                 return rounded, raw
 
             nc.sync.dma_start(idx[:], offs)
@@ -172,7 +172,8 @@ def tile_list_newton_clock_step_kernel(
                 w2_sc_raw[:].rearrange("p (x m t) -> p x t m", t=PACK, m=P),
             )
 
-            page_quads = [sb([P, PACK * BANK], BF16, "quads%d" % c) for c in range(T // BANK)]
+            quads_head = sb([P, PACK * BANK], BF16, "quads0")
+            quads_rest = sb([P, PACK * (T - BANK)], BF16, "quads1")
             load_plane(PLANE_ORDER[2])
             nc.sync.dma_start(w1_raw[:], w1.rearrange("(p j) r -> p (j r)", j=PACK))
             load_plane(PLANE_ORDER[3])
@@ -212,8 +213,8 @@ def tile_list_newton_clock_step_kernel(
         quantise_w1(0)
         for c in BANK_ORDER:
             cols = slice(c * BANK, (c + 1) * BANK)
-            nc.vector.quantize_mx(page_codes[:, cols].bitcast(FP8X4), page_sc[:, cols], page_quads[c][:])
-        w1_codes.append(sb([P, BANK], U32, "quads%d" % BANK_ORDER[-2]))
+            nc.vector.quantize_mx(page_codes[:, cols].bitcast(FP8X4), page_sc[:, cols], quads_rest[:, (c - 1) * PACK * BANK : c * PACK * BANK] if c else quads_head[:])
+        w1_codes.append(sb([P, BANK], U32, "quads1"))
         quantise_w1(1)
 
         neg_a = [sb([P, T], F32, "wide%d" % s) for s in range(SLICES)]

@@ -29,6 +29,8 @@ SMALL_BLOCK = 256
 PLANE_ORDER = (2, 0, 1, 3)
 GPSIMD_COLUMNS = (2048, 512)
 BANK_ORDER = (0, 1, 2, 3)
+EARLY_BANKS = 3
+EARLY_SLICES = 6
 HALVES = [(0, BANK), (BANK, S)]
 PIECES = [(0, 256), (256, 512), (512, 768), (768, 896), (896, 1024)]
 LAST = len(PIECES) - 1
@@ -48,9 +50,10 @@ def tile_list_newton_clock_step_kernel(
 
         banks_taken = []
 
-        def bank():
-            tag = "bank%d" % (len(banks_taken) % BANKS)
-            banks_taken.append(tag)
+        def bank(number=None):
+            tag = "bank%d" % (len(banks_taken) % BANKS if number is None else number)
+            if number is None:
+                banks_taken.append(tag)
             return psum.tile([P, BANK], F32, name=tag, tag=tag)
 
         def words(ap):
@@ -89,7 +92,7 @@ def tile_list_newton_clock_step_kernel(
 
         def estimate(s, h):
             cols = slice(h * BANK, (h + 1) * BANK)
-            acc = bank()
+            acc = bank(s % EARLY_BANKS if h == 0 and s < EARLY_SLICES else None)
             for a in range(2):
                 w_at = a * H + s * P
                 nc.tensor.matmul_mx(
@@ -157,10 +160,11 @@ def tile_list_newton_clock_step_kernel(
 
             nc.vector.tensor_copy(picked_sc_rows[:], tab_sc[:].indirect(idx[:]))
             for a in range(2):
-                nc.sync.dma_start(words(tab[a][:]), words(tab_words[a].rearrange("p t i -> p (t i)")))
                 for q in range(4):
                     row = 16 * a + 4 * q
                     nc.sync.dma_start(words(v_sc[a][32 * q : 32 * q + 4, :]), words(picked_sc_rows[row : row + 4, :]))
+                if a == 0:
+                    load_plane(PLANE_ORDER[2])
 
             for x in range(4):
                 nc.gpsimd.tensor_copy(
@@ -174,8 +178,9 @@ def tile_list_newton_clock_step_kernel(
 
             quads_head = sb([P, PACK * BANK], BF16, "quads0")
             quads_rest = sb([P, PACK * (T - BANK)], BF16, "quads1")
-            load_plane(PLANE_ORDER[2])
             nc.sync.dma_start(w1_raw[:], w1.rearrange("(p j) r -> p (j r)", j=PACK))
+            for a in range(2):
+                nc.sync.dma_start(words(tab[a][:]), words(tab_words[a].rearrange("p t i -> p (t i)")))
             load_plane(PLANE_ORDER[3])
             nc.sync.dma_start(idx3[:], offs3)
             nc.sync.dma_start(
@@ -186,45 +191,48 @@ def tile_list_newton_clock_step_kernel(
             with nc.allow_non_contiguous_dma(reason="one trim value a partition"):
                 nc.sync.dma_start(trim_sb[:], trim.rearrange("(c p) -> p c", p=P))
 
-            place(PLANE_ORDER[0])
-            place(PLANE_ORDER[1])
-            for a in range(2):
-                pick_words(v[a][0], a, 0)
-            for s in range(SLICES):
-                estimate(s, 0)
+            for t in PLANE_ORDER[:3]:
+                place(t)
             for g in range(2):
                 nc.scalar.activation(*w1_views(g, 0, PACK), ACT.Copy)
-            place(PLANE_ORDER[2])
+            for a in range(2):
+                pick_words(v[a][0], a, 0)
+            for s in range(EARLY_SLICES):
+                estimate(s, 0)
             place(PLANE_ORDER[3])
 
         picked = ctx.enter_context(tc.tile_pool(name="picked", bufs=1))
         for a in range(2):
             v[a].append(picked.tile([P, BANK], U32, name="v_late%d" % a, align_bytes=64))
-        w1_codes = [picked.tile([P, BANK], U32, name="w1_codes0", align_bytes=64)]
-        w1_sc = [sb([P, BANK], U8, "w1_sc%d" % g) for g in range(2)]
+        w1_codes = {0: picked.tile([P, P], U32, name="w1_codes0", align_bytes=64)[:]}
+        w1_sc = sb([P, H], U8, "w1_sc")
         page_codes = sb([P, T], U32, "page_codes")
         page_sc = sb([P, T], U8, "page_sc")
 
-        def quantise_w1(g):
-            nc.vector.quantize_mx(w1_codes[g][:].bitcast(FP8X4), w1_sc[g][:], w1_quads[g][:])
+        def quantise_w1(codes, s0, s1):
+            source = w1_quads[s0 // PACK][:, s0 % PACK * BANK : ((s1 - 1) % PACK + 1) * BANK]
+            nc.vector.quantize_mx(codes.bitcast(FP8X4), w1_sc[:, s0 * P : s1 * P], source)
+            for s in range(s0, s1):
+                w1_codes[s] = codes[:, (s - s0) * P : (s - s0 + 1) * P]
 
         for a in range(2):
             pick_words(v[a][1], a, 1)
-        quantise_w1(0)
+        quantise_w1(w1_codes[0], 0, 1)
         for c in BANK_ORDER:
             cols = slice(c * BANK, (c + 1) * BANK)
             nc.vector.quantize_mx(page_codes[:, cols].bitcast(FP8X4), page_sc[:, cols], quads_rest[:, (c - 1) * PACK * BANK : c * PACK * BANK] if c else quads_head[:])
-        w1_codes.append(sb([P, BANK], U32, "quads1"))
-        quantise_w1(1)
+        quantise_w1(sb([P, 2 * P], U32, "quads0")[:], 2, 4)
+        held_codes = sb([P, 5 * P], U32, "quads1")
+        quantise_w1(held_codes[:, :P], 1, 2)
+        quantise_w1(held_codes[:, P:], 4, 8)
 
         neg_a = [sb([P, T], F32, "wide%d" % s) for s in range(SLICES)]
 
         def gain(s, c):
-            rows = slice(s % PACK * P, (s % PACK + 1) * P)
             cols = slice(c * BANK, (c + 1) * BANK)
             acc = bank()
             nc.tensor.matmul_mx(
-                acc[:], lhsT=w1_codes[s // PACK][:, rows].bitcast(FP8X4), lhsT_scale=w1_sc[s // PACK][:, rows],
+                acc[:], lhsT=w1_codes[s].bitcast(FP8X4), lhsT_scale=w1_sc[:, s * P : (s + 1) * P],
                 rhs=page_codes[:, cols].bitcast(FP8X4), rhs_scale=page_sc[:, cols], start=True, stop=True,
             )
             if s == 0 and c == BANK_ORDER[-1]:
@@ -234,6 +242,8 @@ def tile_list_newton_clock_step_kernel(
 
         last_pair = (SLICES - 2, SLICES - 1)
         for s in range(SLICES):
+            if s >= EARLY_SLICES:
+                estimate(s, 0)
             for c in BANK_ORDER:
                 gain(s, c)
             if s not in last_pair:

@@ -31,6 +31,7 @@ GPSIMD_COLUMNS = (2048, 512)
 BANK_ORDER = (0, 1, 2, 3)
 EARLY_BANKS = 3
 EARLY_SLICES = 6
+EXTRA = 128
 HALVES = [(0, BANK), (BANK, S)]
 PIECES = [(0, 256), (256, 512), (512, 768), (768, 896), (896, 1024)]
 LAST = len(PIECES) - 1
@@ -92,7 +93,7 @@ def tile_list_newton_clock_step_kernel(
 
         def estimate(s, h):
             cols = slice(h * BANK, (h + 1) * BANK)
-            acc = bank(s % EARLY_BANKS if h == 0 and s < EARLY_SLICES else None)
+            acc = bank(s % EARLY_BANKS if h == 0 and s < EARLY_SLICES else 3 if s == 1 else None)
             for a in range(2):
                 w_at = a * H + s * P
                 nc.tensor.matmul_mx(
@@ -140,9 +141,11 @@ def tile_list_newton_clock_step_kernel(
                 if t < 2:
                     round_on_gpsimd(slot(quads_rest, t), page[t][:, BANK:])
                 else:
-                    for at in range(0, T - BANK, BANK):
-                        nc.scalar.copy(slot(quads_rest, t)[:, at : at + BANK], page[t][:, BANK + at : 2 * BANK + at])
+                    for lo, hi in ((EXTRA, BANK), (BANK, 2 * BANK), (2 * BANK, 3 * BANK)):
+                        nc.scalar.copy(slot(quads_rest, t)[:, lo:hi], page[t][:, BANK + lo : BANK + hi])
                 round_on_gpsimd(slot(quads_head, t), page[t][:, :BANK])
+                if t >= 2:
+                    round_on_gpsimd(slot(quads_rest, t)[:, :EXTRA], page[t][:, BANK : BANK + EXTRA])
 
             def w1_views(g, t0, t1):
                 rounded = w1_quads[g][:].rearrange("p (t m j) -> p m j t", t=PACK, j=PACK)[:, :, :, t0:t1]
@@ -221,10 +224,10 @@ def tile_list_newton_clock_step_kernel(
         for c in BANK_ORDER:
             cols = slice(c * BANK, (c + 1) * BANK)
             nc.vector.quantize_mx(page_codes[:, cols].bitcast(FP8X4), page_sc[:, cols], quads_rest[:, (c - 1) * PACK * BANK : c * PACK * BANK] if c else quads_head[:])
-        quantise_w1(sb([P, 2 * P], U32, "quads0")[:], 2, 4)
-        held_codes = sb([P, 5 * P], U32, "quads1")
-        quantise_w1(held_codes[:, :P], 1, 2)
-        quantise_w1(held_codes[:, P:], 4, 8)
+        quantise_w1(sb([P, P], U32, "quads0")[:], 3, 4)
+        held_codes = sb([P, 6 * P], U32, "quads1")
+        quantise_w1(held_codes[:, : 2 * P], 1, 3)
+        quantise_w1(held_codes[:, 2 * P :], 4, 8)
 
         neg_a = [sb([P, T], F32, "wide%d" % s) for s in range(SLICES)]
 

@@ -31,7 +31,8 @@ GPSIMD_COLUMNS = (2048, 512)
 BANK_ORDER = (0, 1, 2, 3)
 EARLY_BANKS = 3
 EARLY_SLICES = 6
-EXTRA = 128
+TAIL = 256
+REST_CUTS = [(512, 1024), (1024, 1536), (1536, 1792)]
 HALVES = [(0, BANK), (BANK, S)]
 PIECES = [(0, 256), (256, 512), (512, 768), (768, 896), (896, 1024)]
 LAST = len(PIECES) - 1
@@ -74,7 +75,7 @@ def tile_list_newton_clock_step_kernel(
             nc.vector.memset(words(scale_tile[:]), 0)
 
         page = [sb([P, T], F32, "wide%d" % t) for t in range(PACK)]
-        w1_raw = sb([P, PACK * H], F32, "w1_raw")
+        w1_raw = [sb([P, PACK * BANK], F32, tag) for tag in ("v_early0", "wide5")]
         tab = [sb([P, T], U32, "wide%d" % (6 + a)) for a in range(2)]
         w2_raw = sb([P, 2 * 2 * H], U8, "quads0")
         w3 = sb([P, 2 * N], U32, "w3")
@@ -84,7 +85,7 @@ def tile_list_newton_clock_step_kernel(
         w2 = sb([P, 2 * 2 * H], U8, "w2")
         w2_sc = sb([P, 2 * H], U8, "w2_sc")
         picked_sc_rows = sb([P, S], U8, "picked_sc_rows")
-        v = [[sb([P, BANK], U32, "v_early%d" % a)] for a in range(2)]
+        v = [[None], [sb([P, BANK], U32, "v_early1")]]
         b_pairs = [sb([P, 2 * S], F32, "b%d" % k) for k in range(SLICES // 2)]
 
         def pick_words(picked_words, a, h):
@@ -93,7 +94,7 @@ def tile_list_newton_clock_step_kernel(
 
         def estimate(s, h):
             cols = slice(h * BANK, (h + 1) * BANK)
-            acc = bank(s % EARLY_BANKS if h == 0 and s < EARLY_SLICES else 3 if s == 1 else None)
+            acc = bank(s % EARLY_BANKS if h == 0 and s < EARLY_SLICES else 4 if s == 1 else None)
             for a in range(2):
                 w_at = a * H + s * P
                 nc.tensor.matmul_mx(
@@ -125,6 +126,12 @@ def tile_list_newton_clock_step_kernel(
                 nc.sync.dma_start(page[t][:], base_planes[t])
                 load_block(t, 0)
 
+            def load_w1(g):
+                nc.sync.dma_start(
+                    w1_raw[g][:].rearrange("p (j r) -> p j r", j=PACK),
+                    w1.rearrange("(p j) r -> p j r", j=PACK)[:, :, g * BANK : (g + 1) * BANK],
+                )
+
             def load_scales(scale_tile, scales):
                 for q in range(4):
                     nc.sync.dma_start(
@@ -138,18 +145,20 @@ def tile_list_newton_clock_step_kernel(
             def place(t):
                 for block, (lo, hi) in zip(blocks[t], block_cuts[t]):
                     nc.vector.tensor_copy(page[t][:].indirect(idx2[:, lo // GROUP : hi // GROUP]), block[:])
-                if t < 2:
-                    round_on_gpsimd(slot(quads_rest, t), page[t][:, BANK:])
+                if t == PLANE_ORDER[3]:
+                    nc.vector.tensor_copy(slot(quads_tail, t), page[t][:, T - TAIL :])
                 else:
-                    for lo, hi in ((EXTRA, BANK), (BANK, 2 * BANK), (2 * BANK, 3 * BANK)):
-                        nc.scalar.copy(slot(quads_rest, t)[:, lo:hi], page[t][:, BANK + lo : BANK + hi])
+                    nc.scalar.copy(slot(quads_tail, t), page[t][:, T - TAIL :])
+                if t < 2:
+                    round_on_gpsimd(slot(quads_rest, t), page[t][:, BANK : T - TAIL])
+                else:
+                    for lo, hi in REST_CUTS:
+                        nc.scalar.copy(slot(quads_rest, t)[:, lo - BANK : hi - BANK], page[t][:, lo:hi])
                 round_on_gpsimd(slot(quads_head, t), page[t][:, :BANK])
-                if t >= 2:
-                    round_on_gpsimd(slot(quads_rest, t)[:, :EXTRA], page[t][:, BANK : BANK + EXTRA])
 
             def w1_views(g, t0, t1):
                 rounded = w1_quads[g][:].rearrange("p (t m j) -> p m j t", t=PACK, j=PACK)[:, :, :, t0:t1]
-                raw = w1_raw[:].rearrange("p (j g m t) -> p g m j t", j=PACK, g=2, t=PACK)[:, g, :, :, t0:t1]
+                raw = w1_raw[g][:].rearrange("p (j m t) -> p m j t", j=PACK, t=PACK)[:, :, :, t0:t1]
                 return rounded, raw
 
             nc.sync.dma_start(idx[:], offs)
@@ -167,6 +176,7 @@ def tile_list_newton_clock_step_kernel(
                     row = 16 * a + 4 * q
                     nc.sync.dma_start(words(v_sc[a][32 * q : 32 * q + 4, :]), words(picked_sc_rows[row : row + 4, :]))
                 if a == 0:
+                    load_w1(0)
                     load_plane(PLANE_ORDER[2])
 
             for x in range(4):
@@ -180,8 +190,9 @@ def tile_list_newton_clock_step_kernel(
             )
 
             quads_head = sb([P, PACK * BANK], BF16, "quads0")
-            quads_rest = sb([P, PACK * (T - BANK)], BF16, "quads1")
-            nc.sync.dma_start(w1_raw[:], w1.rearrange("(p j) r -> p (j r)", j=PACK))
+            quads_rest = sb([P, PACK * (T - BANK - TAIL)], BF16, "quads1")
+            quads_tail = sb([P, PACK * TAIL], BF16, "quads_tail")
+            load_w1(1)
             for a in range(2):
                 nc.sync.dma_start(words(tab[a][:]), words(tab_words[a].rearrange("p t i -> p (t i)")))
             load_plane(PLANE_ORDER[3])
@@ -194,10 +205,12 @@ def tile_list_newton_clock_step_kernel(
             with nc.allow_non_contiguous_dma(reason="one trim value a partition"):
                 nc.sync.dma_start(trim_sb[:], trim.rearrange("(c p) -> p c", p=P))
 
-            for t in PLANE_ORDER[:3]:
+            for t in PLANE_ORDER[:2]:
                 place(t)
-            for g in range(2):
-                nc.scalar.activation(*w1_views(g, 0, PACK), ACT.Copy)
+            nc.scalar.activation(*w1_views(0, 0, PACK), ACT.Copy)
+            place(PLANE_ORDER[2])
+            nc.scalar.activation(*w1_views(1, 0, PACK), ACT.Copy)
+            v[0][0] = sb([P, BANK], U32, "v_early0")
             for a in range(2):
                 pick_words(v[a][0], a, 0)
             for s in range(EARLY_SLICES):
@@ -221,34 +234,34 @@ def tile_list_newton_clock_step_kernel(
         for a in range(2):
             pick_words(v[a][1], a, 1)
         quantise_w1(w1_codes[0], 0, 1)
-        for c in BANK_ORDER:
-            cols = slice(c * BANK, (c + 1) * BANK)
-            nc.vector.quantize_mx(page_codes[:, cols].bitcast(FP8X4), page_sc[:, cols], quads_rest[:, (c - 1) * PACK * BANK : c * PACK * BANK] if c else quads_head[:])
-        quantise_w1(sb([P, P], U32, "quads0")[:], 3, 4)
-        held_codes = sb([P, 6 * P], U32, "quads1")
-        quantise_w1(held_codes[:, : 2 * P], 1, 3)
-        quantise_w1(held_codes[:, 2 * P :], 4, 8)
+        def quantise_page(quads, lo, hi):
+            nc.vector.quantize_mx(page_codes[:, lo:hi].bitcast(FP8X4), page_sc[:, lo:hi], quads)
+
+        quantise_page(quads_head[:], 0, BANK)
+        quantise_page(quads_tail[:], T - TAIL, T)
+        for lo, hi in REST_CUTS:
+            quantise_page(quads_rest[:, PACK * (lo - BANK) : PACK * (hi - BANK)], lo, hi)
+        held_codes = sb([P, 7 * P], U32, "quads1")
+        for s0, s1 in ((1, 2), (2, 4), (4, 8)):
+            quantise_w1(held_codes[:, (s0 - 1) * P : (s1 - 1) * P], s0, s1)
 
         neg_a = [sb([P, T], F32, "wide%d" % s) for s in range(SLICES)]
 
-        def gain(s, c):
-            cols = slice(c * BANK, (c + 1) * BANK)
-            acc = bank()
+        def gain(s, lo, hi):
+            cols = slice(lo, hi)
+            acc = bank()[:, : hi - lo]
             nc.tensor.matmul_mx(
-                acc[:], lhsT=w1_codes[s].bitcast(FP8X4), lhsT_scale=w1_sc[:, s * P : (s + 1) * P],
+                acc, lhsT=w1_codes[s].bitcast(FP8X4), lhsT_scale=w1_sc[:, s * P : (s + 1) * P],
                 rhs=page_codes[:, cols].bitcast(FP8X4), rhs_scale=page_sc[:, cols], start=True, stop=True,
             )
-            if s == 0 and c == BANK_ORDER[-1]:
-                nc.vector.tensor_scalar(neg_a[s][:, cols], acc[:], -1.0, None, ALU.mult)
-            else:
-                nc.scalar.activation(neg_a[s][:, cols], acc[:], ACT.Copy, scale=-1.0)
+            nc.scalar.activation(neg_a[s][:, cols], acc, ACT.Copy, scale=-1.0)
 
         last_pair = (SLICES - 2, SLICES - 1)
         for s in range(SLICES):
             if s >= EARLY_SLICES:
                 estimate(s, 0)
-            for c in BANK_ORDER:
-                gain(s, c)
+            for lo, hi in [(0, BANK), (T - TAIL, T)] + REST_CUTS if s == 0 else [(at, at + BANK) for at in range(0, T, BANK)]:
+                gain(s, lo, hi)
             if s not in last_pair:
                 estimate(s, 1)
         for s in last_pair:

@@ -162,9 +162,9 @@ def tile_list_newton_clock_step_kernel(
                 return rounded, raw
 
             nc.sync.dma_start(idx[:], offs)
-            nc.sync.dma_start(words(tab_sc[:32, :]), words(tab_scales.rearrange("a q t -> (a q) t")))
-            nc.sync.dma_start(idx2[:], offs2)
+            nc.scalar.dma_start(words(tab_sc[:32, :]), words(tab_scales.rearrange("a q t -> (a q) t")))
             load_plane(PLANE_ORDER[0])
+            nc.sync.dma_start(idx2[:], offs2)
             load_block(PLANE_ORDER[0], 1)
             nc.sync.dma_start(words(w2_raw[:]).rearrange("p (a c) -> p a c", a=2), words(w2_words).rearrange("a p c -> p a c"))
             load_scales(w2_sc_raw, w2_scales)
@@ -271,7 +271,7 @@ def tile_list_newton_clock_step_kernel(
         z_sc = [sb([P, S], U8, "z_sc%d" % g) for g in range(2)]
         out_rows = out.rearrange("(c p) j -> p c j", p=P)
 
-        def product_tile(lo, hi, tag="prod", bufs=4):
+        def product_tile(lo, hi, tag="prod", bufs=2):
             return sb([P, 2 * (hi - lo)], F32, tag, bufs=bufs)
 
         def pick_product(prod, s, lo, hi, prod_first_col=None):
@@ -313,21 +313,24 @@ def tile_list_newton_clock_step_kernel(
             )
 
         def pick_pair(k):
-            prods = [product_tile(lo, hi) for lo, hi in HALVES]
-            for s in (2 * k, 2 * k + 1):
-                for prod, (lo, hi) in zip(prods, HALVES):
-                    pick_product(prod, s, lo, hi)
-            return prods
+            prod = product_tile(0, S)
+            for lo, hi in HALVES if k == 0 else [(0, S)]:
+                pick_product(prod, 2 * k, lo, hi, 0)
+            for lo, hi in HALVES:
+                pick_product(prod, 2 * k + 1, lo, hi, 0)
+            return prod
 
         z_first = sb([P, PACK * S], BF16, "wide0")
         for k in range(2):
-            for prod, (lo, hi) in zip(pick_pair(k), HALVES):
-                newton(z_first, prod, lo, k, lo, hi)
+            prod = pick_pair(k)
+            for lo, hi in HALVES:
+                newton(z_first, prod, 0, k, lo, hi)
         quads_first = weave_z(z_first, 0, S, "page_codes", nc.scalar.copy)
 
         z_second = sb([P, PACK * S], BF16, "z_second")
-        for prod, (lo, hi) in zip(pick_pair(2), HALVES):
-            newton(z_second, prod, lo, 2, lo, hi)
+        prod = pick_pair(2)
+        for lo, hi in HALVES:
+            newton(z_second, prod, 0, 2, lo, hi)
 
         late_quads = {}
         for i in range(2, len(PIECES)):

@@ -32,6 +32,7 @@ BANK_ORDER = (0, 1, 2, 3)
 EARLY_BANKS = 3
 EARLY_SLICES = 6
 TAIL = 256
+SKEW = 2
 REST_CUTS = [(512, 1024), (1024, 1536), (1536, 1792)]
 HALVES = [(0, BANK), (BANK, S)]
 PIECES = [(0, 256), (256, 512), (512, 768), (768, 896), (896, 1024)]
@@ -86,7 +87,7 @@ def tile_list_newton_clock_step_kernel(
         w2_sc = sb([P, 2 * H], U8, "w2_sc")
         picked_sc_rows = sb([P, S], U8, "picked_sc_rows")
         v = [[None], [sb([P, BANK], U32, "v_early1")]]
-        b_pairs = [sb([P, 2 * S], F32, "b%d" % k) for k in range(SLICES // 2)]
+        b_pairs = [sb([P, 2 * (S + SKEW)], F32, "b%d" % k) for k in range(SLICES // 2)]
 
         def pick_words(picked_words, a, h):
             at = h * BANK // GROUP
@@ -102,7 +103,7 @@ def tile_list_newton_clock_step_kernel(
                     lhsT_scale=w2_sc[:, w_at : w_at + P],
                     rhs=v[a][h][:].bitcast(FP8X4), rhs_scale=v_sc[a][:, cols], start=a == 0, stop=a == 1,
                 )
-            b_at = (s % 2) * S + h * BANK
+            b_at = (s % 2) * (S + SKEW) + h * BANK
             nc.scalar.copy(b_pairs[s // 2][:, b_at : b_at + BANK], acc[:])
 
         def round_on_gpsimd(rounded, raw):
@@ -162,9 +163,9 @@ def tile_list_newton_clock_step_kernel(
                 return rounded, raw
 
             nc.sync.dma_start(idx[:], offs)
-            nc.scalar.dma_start(words(tab_sc[:32, :]), words(tab_scales.rearrange("a q t -> (a q) t")))
-            load_plane(PLANE_ORDER[0])
+            nc.sync.dma_start(words(tab_sc[:32, :]), words(tab_scales.rearrange("a q t -> (a q) t")))
             nc.sync.dma_start(idx2[:], offs2)
+            load_plane(PLANE_ORDER[0])
             load_block(PLANE_ORDER[0], 1)
             nc.sync.dma_start(words(w2_raw[:]).rearrange("p (a c) -> p a c", a=2), words(w2_words).rearrange("a p c -> p a c"))
             load_scales(w2_sc_raw, w2_scales)
@@ -272,10 +273,10 @@ def tile_list_newton_clock_step_kernel(
         out_rows = out.rearrange("(c p) j -> p c j", p=P)
 
         def product_tile(lo, hi, tag="prod", bufs=2):
-            return sb([P, 2 * (hi - lo)], F32, tag, bufs=bufs)
+            return sb([P, 2 * (hi - lo + SKEW)], F32, tag, bufs=bufs)
 
         def pick_product(prod, s, lo, hi, prod_first_col=None):
-            at = (s % 2) * S
+            at = (s % 2) * (S + SKEW)
             prod_at = (s % 2) * prod.shape[1] // 2 + (0 if prod_first_col is None else lo - prod_first_col)
             nc.vector.tensor_tensor(
                 prod[:, prod_at : prod_at + hi - lo],
@@ -345,7 +346,7 @@ def tile_list_newton_clock_step_kernel(
             lo, hi = PIECES[i]
             nc.vector.scalar_tensor_tensor(
                 late_quads[i][:].rearrange("p (j u e) -> p j u e", u=2, e=2)[:, :, 1, :],
-                prod[:].rearrange("p (e j) -> p j e", e=2),
+                prod[:].rearrange("p (e j) -> p j e", e=2)[:, : hi - lo, :],
                 2.0,
                 b_pairs[3][:].rearrange("p (e j) -> p j e", e=2)[:, lo:hi, :],
                 ALU.add,

@@ -30,9 +30,12 @@ PLANE_ORDER = (2, 0, 1, 3)
 GPSIMD_COLUMNS = (2048, 512)
 BANK_ORDER = (0, 1, 2, 3)
 EARLY_BANKS = 3
-EARLY_SLICES = 6
+EARLY_SLICES = 8
 TAIL = 256
 SKEW = 2
+QUARTER = 256
+GPSIMD_ENTRIES = (96, 160, 160)
+UNKEPT = ((BANK, S), (0, QUARTER), (0, QUARTER))
 REST_CUTS = [(512, 1024), (1024, 1536), (1536, 1792)]
 HALVES = [(0, BANK), (BANK, S)]
 PIECES = [(0, 256), (256, 512), (512, 768), (768, 896), (896, 1024)]
@@ -51,12 +54,8 @@ def tile_list_newton_clock_step_kernel(
         def sb(shape, dtype, tag, bufs=1):
             return held.tile(shape, dtype, name=tag, tag=tag, bufs=bufs, align_bytes=64)
 
-        banks_taken = []
-
-        def bank(number=None):
-            tag = "bank%d" % (len(banks_taken) % BANKS if number is None else number)
-            if number is None:
-                banks_taken.append(tag)
+        def bank(number):
+            tag = "bank%d" % number
             return psum.tile([P, BANK], F32, name=tag, tag=tag)
 
         def words(ap):
@@ -93,18 +92,33 @@ def tile_list_newton_clock_step_kernel(
             at = h * BANK // GROUP
             nc.vector.tensor_copy(picked_words[:], tab[a][:].indirect(idx[:, at : at + BANK // GROUP]))
 
-        def estimate(s, h):
-            cols = slice(h * BANK, (h + 1) * BANK)
-            acc = bank(s % EARLY_BANKS if h == 0 and s < EARLY_SLICES else 4 if s == 1 else None)
+        def sum_b(acc, s, lo, hi):
             for a in range(2):
                 w_at = a * H + s * P
                 nc.tensor.matmul_mx(
-                    acc[:], lhsT=w2[:, 2 * w_at : 2 * (w_at + P)].bitcast(FP4X4),
+                    acc, lhsT=w2[:, 2 * w_at : 2 * (w_at + P)].bitcast(FP4X4),
                     lhsT_scale=w2_sc[:, w_at : w_at + P],
-                    rhs=v[a][h][:].bitcast(FP8X4), rhs_scale=v_sc[a][:, cols], start=a == 0, stop=a == 1,
+                    rhs=v[a][lo // BANK][:, lo % BANK : (hi - 1) % BANK + 1].bitcast(FP8X4),
+                    rhs_scale=v_sc[a][:, lo:hi], start=a == 0, stop=a == 1,
                 )
+
+        def estimate(s, h, number):
+            acc = bank(number)
+            sum_b(acc[:], s, h * BANK, (h + 1) * BANK)
             b_at = (s % 2) * (S + SKEW) + h * BANK
             nc.scalar.copy(b_pairs[s // 2][:, b_at : b_at + BANK], acc[:])
+
+        def pair_bank(k, lo, number):
+            acc = bank(number)
+            for e in range(2):
+                sum_b(acc[:, e * QUARTER : (e + 1) * QUARTER], 2 * k + e, lo, lo + QUARTER)
+            return acc
+
+        def copy_pair_bank(acc, k, lo):
+            nc.scalar.copy(
+                b_pairs[k][:].rearrange("p (e j) -> p e j", e=2)[:, :, lo : lo + QUARTER],
+                acc[:].rearrange("p (e j) -> p e j", e=2),
+            )
 
         def round_on_gpsimd(rounded, raw):
             nc.gpsimd.tensor_scalar(rounded, raw, 1.0, 0.0, ALU.mult, ALU.add)
@@ -215,7 +229,7 @@ def tile_list_newton_clock_step_kernel(
             for a in range(2):
                 pick_words(v[a][0], a, 0)
             for s in range(EARLY_SLICES):
-                estimate(s, 0)
+                estimate(s, 0, s % EARLY_BANKS)
             place(PLANE_ORDER[3])
 
         picked = ctx.enter_context(tc.tile_pool(name="picked", bufs=1))
@@ -248,9 +262,9 @@ def tile_list_newton_clock_step_kernel(
 
         neg_a = [sb([P, T], F32, "wide%d" % s) for s in range(SLICES)]
 
-        def gain(s, lo, hi):
+        def gain(s, lo, hi, number):
             cols = slice(lo, hi)
-            acc = bank()[:, : hi - lo]
+            acc = bank(number)[:, : hi - lo]
             nc.tensor.matmul_mx(
                 acc, lhsT=w1_codes[s].bitcast(FP8X4), lhsT_scale=w1_sc[:, s * P : (s + 1) * P],
                 rhs=page_codes[:, cols].bitcast(FP8X4), rhs_scale=page_sc[:, cols], start=True, stop=True,
@@ -258,15 +272,26 @@ def tile_list_newton_clock_step_kernel(
             nc.scalar.activation(neg_a[s][:, cols], acc, ACT.Copy, scale=-1.0)
 
         last_pair = (SLICES - 2, SLICES - 1)
-        for s in range(SLICES):
-            if s >= EARLY_SLICES:
-                estimate(s, 0)
-            for lo, hi in [(0, BANK), (T - TAIL, T)] + REST_CUTS if s == 0 else [(at, at + BANK) for at in range(0, T, BANK)]:
-                gain(s, lo, hi)
-            if s not in last_pair:
-                estimate(s, 1)
-        for s in last_pair:
-            estimate(s, 1)
+        ranges = [(at, at + BANK) for at in range(0, T, BANK)]
+
+        def gains(s, numbers):
+            for (lo, hi), number in zip([(0, BANK), (T - TAIL, T)] + REST_CUTS if s == 0 else ranges, numbers):
+                gain(s, lo, hi, number)
+
+        def late_pair(k, numbers):
+            for q, number in zip((2, 3), numbers):
+                kept[k][q] = pair_bank(k, q * QUARTER, number)
+                copy_pair_bank(kept[k][q], k, q * QUARTER)
+
+        kept = [{}, {}, {}]
+        gains(0, (0, 1, 2, 3, 4))
+        estimate(0, 1, 5)
+        gains(1, (6, 7, 0, 1))
+        estimate(1, 1, 4)
+        kept[0][0] = pair_bank(0, 0, 1)
+        kept[0][1] = pair_bank(0, QUARTER, 4)
+        gains(2, (2, 3, 5, 6))
+        late_pair(1, (7, 0))
 
         z_codes = [sb([P, S], U32, "z_codes%d" % g) for g in range(2)]
         z_sc = [sb([P, S], U8, "z_sc%d" % g) for g in range(2)]
@@ -306,6 +331,37 @@ def tile_list_newton_clock_step_kernel(
         def quantise_z(quads, g, lo, hi):
             nc.vector.quantize_mx(z_codes[g][:, lo:hi].bitcast(FP8X4), z_sc[g][:, lo:hi], quads[:])
 
+        def newton_kept(z_pairs, prod, k, q):
+            lo, hi = q * QUARTER, (q + 1) * QUARTER
+            nc.vector.scalar_tensor_tensor(
+                z_pairs[:].rearrange("p (u j e) -> p u j e", u=2, e=2)[:, k % 2, lo:hi, :],
+                prod[:].rearrange("p (e j) -> p j e", e=2)[:, lo:hi, :],
+                2.0,
+                kept[k][q][:].rearrange("p (e j) -> p j e", e=2),
+                ALU.add,
+                ALU.mult,
+            )
+
+        def newton_on_gpsimd(z_pairs, prod, k):
+            n = GPSIMD_ENTRIES[k]
+            cols = slice(UNKEPT[k][0], UNKEPT[k][0] + n)
+            factor = sb([P, 2 * n], F32, "wide%d" % (2 * k + 1))
+            pairs = factor[:].rearrange("p (j e) -> p j e", e=2)
+            nc.gpsimd.tensor_scalar(pairs, prod[:].rearrange("p (e j) -> p j e", e=2)[:, cols, :], 1.0, 2.0, ALU.mult, ALU.add)
+            nc.gpsimd.tensor_tensor(
+                z_pairs[:].rearrange("p (u j e) -> p u j e", u=2, e=2)[:, k % 2, cols, :],
+                pairs,
+                b_pairs[k][:].rearrange("p (e j) -> p j e", e=2)[:, cols, :],
+                ALU.mult,
+            )
+
+        def newton_pair(z_pairs, k):
+            prod = pick_pair(k)
+            newton_on_gpsimd(z_pairs, prod, k)
+            for q in sorted(kept[k]):
+                newton_kept(z_pairs, prod, k, q)
+            newton(z_pairs, prod, 0, k, UNKEPT[k][0] + GPSIMD_ENTRIES[k], UNKEPT[k][1])
+
         def project(acc, g, c, lo, hi):
             at = g * N + c * P
             nc.tensor.matmul_mx(
@@ -322,25 +378,22 @@ def tile_list_newton_clock_step_kernel(
             return prod
 
         z_first = sb([P, PACK * S], BF16, "wide0")
-        for k in range(2):
-            prod = pick_pair(k)
-            for lo, hi in HALVES:
-                newton(z_first, prod, 0, k, lo, hi)
+        newton_pair(z_first, 0)
+        gains(3, (2, 3, 1, 4))
+        kept[1][1] = pair_bank(1, QUARTER, 5)
+        gains(4, (6, 2, 3, 1))
+        late_pair(2, (4, 6))
+        newton_pair(z_first, 1)
+        gains(5, (2, 3, 1, 5))
+        kept[2][1] = pair_bank(2, QUARTER, 7)
+        gains(6, (2, 0, 3, 1))
+        gains(7, (5, 2, 0, 3))
+        for s, number in zip(last_pair, (1, 5)):
+            estimate(s, 1, number)
         quads_first = weave_z(z_first, 0, S, "page_codes", nc.scalar.copy)
 
         z_second = sb([P, PACK * S], BF16, "z_second")
-        prod = pick_pair(2)
-        for lo, hi in HALVES:
-            newton(z_second, prod, 0, 2, lo, hi)
-
-        late_quads = {}
-        for i in range(2, len(PIECES)):
-            lo, hi = PIECES[i]
-            late_quads[i] = sb([P, PACK * (hi - lo)], BF16, "z_quads%d" % i)
-            nc.scalar.copy(
-                late_quads[i][:].bitcast(F32).rearrange("p (j u) -> p j u", u=2)[:, :, 0],
-                z_second[:].bitcast(F32)[:, lo:hi],
-            )
+        newton_pair(z_second, 2)
 
         def newton_into_quads(prod, i):
             lo, hi = PIECES[i]
@@ -359,7 +412,7 @@ def tile_list_newton_clock_step_kernel(
 
         def finish(quads, i):
             lo, hi = PIECES[i]
-            accs = [bank() for c in range(N // P)]
+            accs = [bank(number) for number in ((2, 0, 3, 1), (4, 6, 7, 5))[i % 2]]
             for c in range(N // P):
                 project(accs[c], 0, c, lo, hi)
             quantise_z(quads, 1, lo, hi)
@@ -388,6 +441,14 @@ def tile_list_newton_clock_step_kernel(
         for i in range(2):
             last_newton(first_prod, i, 0)
             first_quads.append(weave_z(z_second, *PIECES[i], "quads%d" % i, nc.scalar.copy))
+        late_quads = {}
+        for i in range(2, len(PIECES)):
+            lo, hi = PIECES[i]
+            late_quads[i] = sb([P, PACK * (hi - lo)], BF16, "z_quads%d" % i)
+            nc.scalar.copy(
+                late_quads[i][:].bitcast(F32).rearrange("p (j u) -> p j u", u=2)[:, :, 0],
+                z_second[:].bitcast(F32)[:, lo:hi],
+            )
         quantise_z(quads_first, 0, 0, S)
         finish(first_quads[0], 0)
 

@@ -34,8 +34,8 @@ EARLY_SLICES = 8
 TAIL = 256
 SKEW = 2
 QUARTER = 256
-GPSIMD_ENTRIES = (96, 160, 160)
-UNKEPT = ((BANK, S), (0, QUARTER), (0, QUARTER))
+GPSIMD_ENTRIES = 144
+KEPT = [(128, 256), (256, 512), (512, 768), (768, 1024)]
 REST_CUTS = [(512, 1024), (1024, 1536), (1536, 1792)]
 HALVES = [(0, BANK), (BANK, S)]
 PIECES = [(0, 256), (256, 512), (512, 768), (768, 896), (896, 1024)]
@@ -108,17 +108,19 @@ def tile_list_newton_clock_step_kernel(
             b_at = (s % 2) * (S + SKEW) + h * BANK
             nc.scalar.copy(b_pairs[s // 2][:, b_at : b_at + BANK], acc[:])
 
-        def pair_bank(k, lo, number):
-            acc = bank(number)
+        def pair_bank(k, lo, hi, number):
+            acc = bank(number)[:, : 2 * (hi - lo)]
             for e in range(2):
-                sum_b(acc[:, e * QUARTER : (e + 1) * QUARTER], 2 * k + e, lo, lo + QUARTER)
-            return acc
+                sum_b(acc[:, e * (hi - lo) : (e + 1) * (hi - lo)], 2 * k + e, lo, hi)
+            kept[k, lo] = acc
 
-        def copy_pair_bank(acc, k, lo):
+        def copy_pair_bank(k, lo, hi):
             nc.scalar.copy(
-                b_pairs[k][:].rearrange("p (e j) -> p e j", e=2)[:, :, lo : lo + QUARTER],
-                acc[:].rearrange("p (e j) -> p e j", e=2),
+                b_pairs[k][:].rearrange("p (e j) -> p e j", e=2)[:, :, lo:hi],
+                kept[k, lo].rearrange("p (e j) -> p e j", e=2),
             )
+
+        kept = {}
 
         def round_on_gpsimd(rounded, raw):
             nc.gpsimd.tensor_scalar(rounded, raw, 1.0, 0.0, ALU.mult, ALU.add)
@@ -279,19 +281,24 @@ def tile_list_newton_clock_step_kernel(
                 gain(s, lo, hi, number)
 
         def late_pair(k, numbers):
-            for q, number in zip((2, 3), numbers):
-                kept[k][q] = pair_bank(k, q * QUARTER, number)
-                copy_pair_bank(kept[k][q], k, q * QUARTER)
+            for (lo, hi), number in zip(KEPT[2:], numbers):
+                pair_bank(k, lo, hi, number)
+                copy_pair_bank(k, lo, hi)
 
-        kept = [{}, {}, {}]
+        def early_pair_again(k, numbers):
+            for (lo, hi), number in zip(KEPT[:2], numbers):
+                pair_bank(k, lo, hi, number)
+
         gains(0, (0, 1, 2, 3, 4))
         estimate(0, 1, 5)
         gains(1, (6, 7, 0, 1))
         estimate(1, 1, 4)
-        kept[0][0] = pair_bank(0, 0, 1)
-        kept[0][1] = pair_bank(0, QUARTER, 4)
         gains(2, (2, 3, 5, 6))
         late_pair(1, (7, 0))
+        gains(3, (1, 4, 2, 3))
+        gains(4, (5, 6, 1, 4))
+        early_pair_again(1, (2, 3))
+        late_pair(2, (5, 6))
 
         z_codes = [sb([P, S], U32, "z_codes%d" % g) for g in range(2)]
         z_sc = [sb([P, S], U8, "z_sc%d" % g) for g in range(2)]
@@ -331,36 +338,34 @@ def tile_list_newton_clock_step_kernel(
         def quantise_z(quads, g, lo, hi):
             nc.vector.quantize_mx(z_codes[g][:, lo:hi].bitcast(FP8X4), z_sc[g][:, lo:hi], quads[:])
 
-        def newton_kept(z_pairs, prod, k, q):
-            lo, hi = q * QUARTER, (q + 1) * QUARTER
+        def newton_kept(z_pairs, prod, k, lo, hi):
+            first = max(lo, GPSIMD_ENTRIES)
             nc.vector.scalar_tensor_tensor(
-                z_pairs[:].rearrange("p (u j e) -> p u j e", u=2, e=2)[:, k % 2, lo:hi, :],
-                prod[:].rearrange("p (e j) -> p j e", e=2)[:, lo:hi, :],
+                z_pairs[:].rearrange("p (u j e) -> p u j e", u=2, e=2)[:, k % 2, first:hi, :],
+                prod[:].rearrange("p (e j) -> p j e", e=2)[:, first:hi, :],
                 2.0,
-                kept[k][q][:].rearrange("p (e j) -> p j e", e=2),
+                kept[k, lo].rearrange("p (e j) -> p j e", e=2)[:, first - lo :, :],
                 ALU.add,
                 ALU.mult,
             )
 
         def newton_on_gpsimd(z_pairs, prod, k):
-            n = GPSIMD_ENTRIES[k]
-            cols = slice(UNKEPT[k][0], UNKEPT[k][0] + n)
-            factor = sb([P, 2 * n], F32, "wide%d" % (2 * k + 1))
+            n = GPSIMD_ENTRIES
+            factor = sb([P, 2 * n], F32, "factor")
             pairs = factor[:].rearrange("p (j e) -> p j e", e=2)
-            nc.gpsimd.tensor_scalar(pairs, prod[:].rearrange("p (e j) -> p j e", e=2)[:, cols, :], 1.0, 2.0, ALU.mult, ALU.add)
+            nc.gpsimd.tensor_scalar(pairs, prod[:].rearrange("p (e j) -> p j e", e=2)[:, :n, :], 1.0, 2.0, ALU.mult, ALU.add)
             nc.gpsimd.tensor_tensor(
-                z_pairs[:].rearrange("p (u j e) -> p u j e", u=2, e=2)[:, k % 2, cols, :],
+                z_pairs[:].rearrange("p (u j e) -> p u j e", u=2, e=2)[:, k % 2, :n, :],
                 pairs,
-                b_pairs[k][:].rearrange("p (e j) -> p j e", e=2)[:, cols, :],
+                b_pairs[k][:].rearrange("p (e j) -> p j e", e=2)[:, :n, :],
                 ALU.mult,
             )
 
         def newton_pair(z_pairs, k):
             prod = pick_pair(k)
             newton_on_gpsimd(z_pairs, prod, k)
-            for q in sorted(kept[k]):
-                newton_kept(z_pairs, prod, k, q)
-            newton(z_pairs, prod, 0, k, UNKEPT[k][0] + GPSIMD_ENTRIES[k], UNKEPT[k][1])
+            for lo, hi in KEPT:
+                newton_kept(z_pairs, prod, k, lo, hi)
 
         def project(acc, g, c, lo, hi):
             at = g * N + c * P
@@ -378,17 +383,15 @@ def tile_list_newton_clock_step_kernel(
             return prod
 
         z_first = sb([P, PACK * S], BF16, "wide0")
-        newton_pair(z_first, 0)
-        gains(3, (2, 3, 1, 4))
-        kept[1][1] = pair_bank(1, QUARTER, 5)
-        gains(4, (6, 2, 3, 1))
-        late_pair(2, (4, 6))
+        prod = pick_pair(0)
+        for lo, hi in HALVES:
+            newton(z_first, prod, 0, 0, lo, hi)
         newton_pair(z_first, 1)
-        gains(5, (2, 3, 1, 5))
-        kept[2][1] = pair_bank(2, QUARTER, 7)
-        gains(6, (2, 0, 3, 1))
-        gains(7, (5, 2, 0, 3))
-        for s, number in zip(last_pair, (1, 5)):
+        gains(5, (1, 4, 2, 3))
+        early_pair_again(2, (7, 0))
+        for s in last_pair:
+            gains(s, (1, 4, 2, 3))
+        for s, number in zip(last_pair, (1, 4)):
             estimate(s, 1, number)
         quads_first = weave_z(z_first, 0, S, "page_codes", nc.scalar.copy)
 
@@ -412,7 +415,7 @@ def tile_list_newton_clock_step_kernel(
 
         def finish(quads, i):
             lo, hi = PIECES[i]
-            accs = [bank(number) for number in ((2, 0, 3, 1), (4, 6, 7, 5))[i % 2]]
+            accs = [bank(number) for number in ((2, 3, 1, 4), (5, 6, 7, 0))[i % 2]]
             for c in range(N // P):
                 project(accs[c], 0, c, lo, hi)
             quantise_z(quads, 1, lo, hi)

@@ -34,7 +34,7 @@ EARLY_SLICES = 8
 TAIL = 256
 SKEW = 2
 QUARTER = 256
-GPSIMD_ENTRIES = 144
+GPSIMD_ENTRIES = 184
 KEPT = [(128, 256), (256, 512), (512, 768), (768, 1024)]
 REST_CUTS = [(512, 1024), (1024, 1536), (1536, 1792)]
 HALVES = [(0, BANK), (BANK, S)]

@@ -34,7 +34,7 @@ EARLY_SLICES = 8
 TAIL = 256
 SKEW = 2
 QUARTER = 256
-GPSIMD_ENTRIES = 184
+GPSIMD_ENTRIES = (152, 184, 184)
 KEPT = [(128, 256), (256, 512), (512, 768), (768, 1024)]
 REST_CUTS = [(512, 1024), (1024, 1536), (1536, 1792)]
 HALVES = [(0, BANK), (BANK, S)]
@@ -92,26 +92,27 @@ def tile_list_newton_clock_step_kernel(
             at = h * BANK // GROUP
             nc.vector.tensor_copy(picked_words[:], tab[a][:].indirect(idx[:, at : at + BANK // GROUP]))
 
-        def sum_b(acc, s, lo, hi):
-            for a in range(2):
-                w_at = a * H + s * P
-                nc.tensor.matmul_mx(
-                    acc, lhsT=w2[:, 2 * w_at : 2 * (w_at + P)].bitcast(FP4X4),
-                    lhsT_scale=w2_sc[:, w_at : w_at + P],
-                    rhs=v[a][lo // BANK][:, lo % BANK : (hi - 1) % BANK + 1].bitcast(FP8X4),
-                    rhs_scale=v_sc[a][:, lo:hi], start=a == 0, stop=a == 1,
-                )
+        def b_pass(acc, s, a, lo, hi, start, stop):
+            w_at = a * H + s * P
+            nc.tensor.matmul_mx(
+                acc, lhsT=w2[:, 2 * w_at : 2 * (w_at + P)].bitcast(FP4X4),
+                lhsT_scale=w2_sc[:, w_at : w_at + P],
+                rhs=v[a][lo // BANK][:, lo % BANK : (hi - 1) % BANK + 1].bitcast(FP8X4),
+                rhs_scale=v_sc[a][:, lo:hi], start=start, stop=stop,
+            )
 
         def estimate(s, h, number):
             acc = bank(number)
-            sum_b(acc[:], s, h * BANK, (h + 1) * BANK)
+            for a in range(2):
+                b_pass(acc[:], s, a, h * BANK, (h + 1) * BANK, a == 0, a == 1)
             b_at = (s % 2) * (S + SKEW) + h * BANK
             nc.scalar.copy(b_pairs[s // 2][:, b_at : b_at + BANK], acc[:])
 
         def pair_bank(k, lo, hi, number):
             acc = bank(number)[:, : 2 * (hi - lo)]
-            for e in range(2):
-                sum_b(acc[:, e * (hi - lo) : (e + 1) * (hi - lo)], 2 * k + e, lo, hi)
+            for a in range(2):
+                for e in range(2):
+                    b_pass(acc[:, e * (hi - lo) : (e + 1) * (hi - lo)], 2 * k + e, a, lo, hi, a + e == 0, a + e == 2)
             kept[k, lo] = acc
 
         def copy_pair_bank(k, lo, hi):
@@ -289,16 +290,16 @@ def tile_list_newton_clock_step_kernel(
             for (lo, hi), number in zip(KEPT[:2], numbers):
                 pair_bank(k, lo, hi, number)
 
+        pair_bank(0, *KEPT[2], 5)
+        copy_pair_bank(0, *KEPT[2])
         gains(0, (0, 1, 2, 3, 4))
-        estimate(0, 1, 5)
-        gains(1, (6, 7, 0, 1))
-        estimate(1, 1, 4)
-        gains(2, (2, 3, 5, 6))
-        late_pair(1, (7, 0))
-        gains(3, (1, 4, 2, 3))
-        gains(4, (5, 6, 1, 4))
-        early_pair_again(1, (2, 3))
-        late_pair(2, (5, 6))
+        pair_bank(0, *KEPT[3], 0)
+        nc.scalar.copy(b_pairs[0][:, KEPT[3][0] : S], kept[0, KEPT[3][0]][:, :QUARTER])
+        gains(1, (7, 6, 1, 2))
+        nc.scalar.copy(b_pairs[0][:, S + SKEW + KEPT[3][0] : 2 * S + SKEW], kept[0, KEPT[3][0]][:, QUARTER:])
+        pair_bank(0, *KEPT[1], 4)
+        gains(2, (3, 7, 6, 1))
+        late_pair(1, (2, 3))
 
         z_codes = [sb([P, S], U32, "z_codes%d" % g) for g in range(2)]
         z_sc = [sb([P, S], U8, "z_sc%d" % g) for g in range(2)]
@@ -339,7 +340,7 @@ def tile_list_newton_clock_step_kernel(
             nc.vector.quantize_mx(z_codes[g][:, lo:hi].bitcast(FP8X4), z_sc[g][:, lo:hi], quads[:])
 
         def newton_kept(z_pairs, prod, k, lo, hi):
-            first = max(lo, GPSIMD_ENTRIES)
+            first = max(lo, GPSIMD_ENTRIES[k])
             nc.vector.scalar_tensor_tensor(
                 z_pairs[:].rearrange("p (u j e) -> p u j e", u=2, e=2)[:, k % 2, first:hi, :],
                 prod[:].rearrange("p (e j) -> p j e", e=2)[:, first:hi, :],
@@ -350,7 +351,7 @@ def tile_list_newton_clock_step_kernel(
             )
 
         def newton_on_gpsimd(z_pairs, prod, k):
-            n = GPSIMD_ENTRIES
+            n = GPSIMD_ENTRIES[k]
             factor = sb([P, 2 * n], F32, "factor")
             pairs = factor[:].rearrange("p (j e) -> p j e", e=2)
             nc.gpsimd.tensor_scalar(pairs, prod[:].rearrange("p (e j) -> p j e", e=2)[:, :n, :], 1.0, 2.0, ALU.mult, ALU.add)
@@ -364,8 +365,10 @@ def tile_list_newton_clock_step_kernel(
         def newton_pair(z_pairs, k):
             prod = pick_pair(k)
             newton_on_gpsimd(z_pairs, prod, k)
-            for lo, hi in KEPT:
+            for lo, hi in KEPT[1:] if k == 0 else KEPT:
                 newton_kept(z_pairs, prod, k, lo, hi)
+            if k == 0:
+                newton(z_pairs, prod, 0, k, GPSIMD_ENTRIES[k], QUARTER)
 
         def project(acc, g, c, lo, hi):
             at = g * N + c * P
@@ -376,22 +379,25 @@ def tile_list_newton_clock_step_kernel(
 
         def pick_pair(k):
             prod = product_tile(0, S)
-            for lo, hi in HALVES if k == 0 else [(0, S)]:
+            first_cuts = [(0, KEPT[3][0]), KEPT[3]]
+            for lo, hi in first_cuts if k == 0 else [(0, S)]:
                 pick_product(prod, 2 * k, lo, hi, 0)
-            for lo, hi in HALVES:
+            for lo, hi in first_cuts if k == 0 else HALVES:
                 pick_product(prod, 2 * k + 1, lo, hi, 0)
             return prod
 
         z_first = sb([P, PACK * S], BF16, "wide0")
-        prod = pick_pair(0)
-        for lo, hi in HALVES:
-            newton(z_first, prod, 0, 0, lo, hi)
+        newton_pair(z_first, 0)
+        gains(3, (7, 4, 5, 0))
+        gains(4, (6, 1, 7, 4))
+        early_pair_again(1, (5, 0))
+        late_pair(2, (6, 1))
         newton_pair(z_first, 1)
-        gains(5, (1, 4, 2, 3))
-        early_pair_again(2, (7, 0))
+        gains(5, (7, 4, 5, 0))
+        early_pair_again(2, (2, 3))
         for s in last_pair:
-            gains(s, (1, 4, 2, 3))
-        for s, number in zip(last_pair, (1, 4)):
+            gains(s, (7, 4, 5, 0))
+        for s, number in zip(last_pair, (7, 4)):
             estimate(s, 1, number)
         quads_first = weave_z(z_first, 0, S, "page_codes", nc.scalar.copy)
 
@@ -415,7 +421,7 @@ def tile_list_newton_clock_step_kernel(
 
         def finish(quads, i):
             lo, hi = PIECES[i]
-            accs = [bank(number) for number in ((2, 3, 1, 4), (5, 6, 7, 0))[i % 2]]
+            accs = [bank(number) for number in ((5, 0, 7, 4), (6, 1, 2, 3))[i % 2]]
             for c in range(N // P):
                 project(accs[c], 0, c, lo, hi)
             quantise_z(quads, 1, lo, hi)

@@ -71,8 +71,7 @@ def tile_list_newton_clock_step_kernel(
         v_sc = [sb([P, S], U8, "v_sc%d" % a) for a in range(2)]
         nc.vector.memset(words(tab_sc[32:64, :]), 0)
         nc.vector.memset(words(tab_sc[64:, :]), 0)
-        for scale_tile in (w2_sc_raw, *v_sc, w3_sc):
-            nc.vector.memset(words(scale_tile[:]), 0)
+        nc.vector.memset(words(w2_sc_raw[:]), 0)
 
         page = [sb([P, T], F32, "wide%d" % t) for t in range(PACK)]
         w1_raw = [sb([P, PACK * BANK], F32, tag) for tag in ("v_early0", "wide5")]

@@ -34,7 +34,7 @@ EARLY_SLICES = 8
 TAIL = 256
 SKEW = 2
 QUARTER = 256
-GPSIMD_ENTRIES = (152, 184, 184)
+GPSIMD_ENTRIES = (168, 200, 200)
 KEPT = [(128, 256), (256, 512), (512, 768), (768, 1024)]
 REST_CUTS = [(512, 1024), (1024, 1536), (1536, 1792)]
 HALVES = [(0, BANK), (BANK, S)]
@@ -262,7 +262,7 @@ def tile_list_newton_clock_step_kernel(
         for s0, s1 in ((1, 2), (2, 4), (4, 8)):
             quantise_w1(held_codes[:, (s0 - 1) * P : (s1 - 1) * P], s0, s1)
 
-        neg_a = [sb([P, T], F32, "wide%d" % s) for s in range(SLICES)]
+        a_rows = [sb([P, T], F32, "wide%d" % s) for s in range(SLICES)]
 
         def gain(s, lo, hi, number):
             cols = slice(lo, hi)
@@ -271,7 +271,7 @@ def tile_list_newton_clock_step_kernel(
                 acc, lhsT=w1_codes[s].bitcast(FP8X4), lhsT_scale=w1_sc[:, s * P : (s + 1) * P],
                 rhs=page_codes[:, cols].bitcast(FP8X4), rhs_scale=page_sc[:, cols], start=True, stop=True,
             )
-            nc.scalar.activation(neg_a[s][:, cols], acc, ACT.Copy, scale=-1.0)
+            nc.scalar.copy(a_rows[s][:, cols], acc)
 
         last_pair = (SLICES - 2, SLICES - 1)
         ranges = [(at, at + BANK) for at in range(0, T, BANK)]
@@ -312,7 +312,7 @@ def tile_list_newton_clock_step_kernel(
             prod_at = (s % 2) * prod.shape[1] // 2 + (0 if prod_first_col is None else lo - prod_first_col)
             nc.vector.tensor_tensor(
                 prod[:, prod_at : prod_at + hi - lo],
-                neg_a[s][:].indirect(idx3[:, lo // GROUP : hi // GROUP]),
+                a_rows[s][:].indirect(idx3[:, lo // GROUP : hi // GROUP]),
                 b_pairs[s // 2][:, at + lo : at + hi],
                 ALU.mult,
             )
@@ -321,7 +321,7 @@ def tile_list_newton_clock_step_kernel(
             nc.vector.scalar_tensor_tensor(
                 z_pairs[:].rearrange("p (u j e) -> p u j e", u=2, e=2)[:, k % 2, lo:hi, :],
                 prod[:].rearrange("p (e j) -> p j e", e=2)[:, lo - prod_first_col : hi - prod_first_col, :],
-                2.0,
+                -2.0,
                 b_pairs[k][:].rearrange("p (e j) -> p j e", e=2)[:, lo:hi, :],
                 ALU.add,
                 ALU.mult,
@@ -343,7 +343,7 @@ def tile_list_newton_clock_step_kernel(
             nc.vector.scalar_tensor_tensor(
                 z_pairs[:].rearrange("p (u j e) -> p u j e", u=2, e=2)[:, k % 2, first:hi, :],
                 prod[:].rearrange("p (e j) -> p j e", e=2)[:, first:hi, :],
-                2.0,
+                -2.0,
                 kept[k, lo].rearrange("p (e j) -> p j e", e=2)[:, first - lo :, :],
                 ALU.add,
                 ALU.mult,
@@ -353,7 +353,7 @@ def tile_list_newton_clock_step_kernel(
             n = GPSIMD_ENTRIES[k]
             factor = sb([P, 2 * n], F32, "factor")
             pairs = factor[:].rearrange("p (j e) -> p j e", e=2)
-            nc.gpsimd.tensor_scalar(pairs, prod[:].rearrange("p (e j) -> p j e", e=2)[:, :n, :], 1.0, 2.0, ALU.mult, ALU.add)
+            nc.gpsimd.tensor_scalar(pairs, prod[:].rearrange("p (e j) -> p j e", e=2)[:, :n, :], 1.0, -2.0, ALU.mult, ALU.add)
             nc.gpsimd.tensor_tensor(
                 z_pairs[:].rearrange("p (u j e) -> p u j e", u=2, e=2)[:, k % 2, :n, :],
                 pairs,
@@ -408,7 +408,7 @@ def tile_list_newton_clock_step_kernel(
             nc.vector.scalar_tensor_tensor(
                 late_quads[i][:].rearrange("p (j u e) -> p j u e", u=2, e=2)[:, :, 1, :],
                 prod[:].rearrange("p (e j) -> p j e", e=2)[:, : hi - lo, :],
-                2.0,
+                -2.0,
                 b_pairs[3][:].rearrange("p (e j) -> p j e", e=2)[:, lo:hi, :],
                 ALU.add,
                 ALU.mult,
@@ -431,9 +431,9 @@ def tile_list_newton_clock_step_kernel(
             for c in range(N // P):
                 sums, offset = accs[c][:, : hi - lo], trim_sb[:, c : c + 1]
                 if i == LAST and c >= 2:
-                    nc.vector.tensor_scalar(rows[:, c, :], sums, offset, None, ALU.add)
+                    nc.vector.tensor_scalar(rows[:, c, :], sums, -1.0, offset, ALU.mult, ALU.add)
                 else:
-                    nc.scalar.activation(rows[:, c, :], sums, ACT.Identity, bias=offset)
+                    nc.scalar.activation(rows[:, c, :], sums, ACT.Identity, bias=offset, scale=-1.0)
             if i == LAST:
                 for c in (2, 0, 3, 1):
                     (nc.scalar if c == 1 else nc.sync).dma_start(out_rows[:, c, lo:hi], rows[:, c, :])

@@ -396,9 +396,8 @@ def tile_list_newton_clock_step_kernel(
         early_pair_again(2, (2, 3))
         for s in last_pair:
             gains(s, (7, 4, 5, 0))
-        for s, number in zip(last_pair, (7, 4)):
-            estimate(s, 1, number)
         quads_first = weave_z(z_first, 0, S, "page_codes", nc.scalar.copy)
+        estimate(last_pair[0], 1, 7)
 
         z_second = sb([P, PACK * S], BF16, "z_second")
         newton_pair(z_second, 2)
@@ -449,6 +448,8 @@ def tile_list_newton_clock_step_kernel(
         for i in range(2):
             last_newton(first_prod, i, 0)
             first_quads.append(weave_z(z_second, *PIECES[i], "quads%d" % i, nc.scalar.copy))
+            if i == 0:
+                estimate(last_pair[1], 1, 4)
         late_quads = {}
         for i in range(2, len(PIECES)):
             lo, hi = PIECES[i]

@@ -34,7 +34,7 @@ EARLY_SLICES = 8
 TAIL = 256
 SKEW = 2
 QUARTER = 256
-GPSIMD_ENTRIES = (168, 200, 200)
+GPSIMD_ENTRIES = (184, 224, 224)
 KEPT = [(128, 256), (256, 512), (512, 768), (768, 1024)]
 REST_CUTS = [(512, 1024), (1024, 1536), (1536, 1792)]
 HALVES = [(0, BANK), (BANK, S)]
@@ -352,12 +352,12 @@ def tile_list_newton_clock_step_kernel(
         def newton_on_gpsimd(z_pairs, prod, k):
             n = GPSIMD_ENTRIES[k]
             factor = sb([P, 2 * n], F32, "factor")
-            pairs = factor[:].rearrange("p (j e) -> p j e", e=2)
-            nc.gpsimd.tensor_scalar(pairs, prod[:].rearrange("p (e j) -> p j e", e=2)[:, :n, :], 1.0, -2.0, ALU.mult, ALU.add)
+            rows = factor[:].rearrange("p (e j) -> p e j", e=2)
+            nc.gpsimd.tensor_scalar(rows, prod[:].rearrange("p (e j) -> p e j", e=2)[:, :, :n], 1.0, -2.0, ALU.mult, ALU.add)
             nc.gpsimd.tensor_tensor(
-                z_pairs[:].rearrange("p (u j e) -> p u j e", u=2, e=2)[:, k % 2, :n, :],
-                pairs,
-                b_pairs[k][:].rearrange("p (e j) -> p j e", e=2)[:, :n, :],
+                z_pairs[:].rearrange("p (u j e) -> p u e j", u=2, e=2)[:, k % 2, :, :n],
+                rows,
+                b_pairs[k][:].rearrange("p (e j) -> p e j", e=2)[:, :, :n],
                 ALU.mult,
             )
 

from contextlib import ExitStack

import concourse.mybir as mybir

F32 = mybir.dt.float32
BF16 = mybir.dt.bfloat16
I32 = mybir.dt.int32
U32 = mybir.dt.uint32
U16 = mybir.dt.uint16
U8 = mybir.dt.uint8
FP8X4 = mybir.dt.float8_e4m3fn_x4
FP4X4 = mybir.dt.float4_e2m1fn_x4
ALU = mybir.AluOpType
ACT = mybir.ActivationFunctionType

P = 128
PACK = 4
T = 2048
S = 1024
H = 1024
N = 512
BANK = 512
BANKS = 8
GROUP = 16
SLICES = H // P
FLOPS = 2 * (512 * H * T + 1024 * H * S + H * N * S)

SMALL_BLOCK = 256
PLANE_ORDER = (2, 0, 1, 3)
GPSIMD_COLUMNS = (2048, 512)
BANK_ORDER = (0, 1, 2, 3)
EARLY_BANKS = 3
EARLY_SLICES = 8
TAIL = 256
SKEW = 2
QUARTER = 256
GPSIMD_ENTRIES = (184, 224, 224)
KEPT = [(128, 256), (256, 512), (512, 768), (768, 1024)]
REST_CUTS = [(512, 1024), (1024, 1536), (1536, 1792)]
HALVES = [(0, BANK), (BANK, S)]
PIECES = [(0, 256), (256, 512), (512, 768), (768, 896), (896, 1024)]
LAST = len(PIECES) - 1


def tile_list_newton_clock_step_kernel(
    tc, tab_words, tab_scales, offs, offs2, offs3, base, xs, w1, w2_words, w2_scales, w3_words, w3_scales, trim, out
):
    nc = tc.nc
    with ExitStack() as ctx:
        lists = ctx.enter_context(tc.tile_pool(name="lists", bufs=1))
        held = ctx.enter_context(tc.tile_pool(name="held", bufs=1))
        psum = ctx.enter_context(tc.psum_pool(name="psum", bufs=1))

        def sb(shape, dtype, tag, bufs=1):
            return held.tile(shape, dtype, name=tag, tag=tag, bufs=bufs, align_bytes=64)

        def bank(number):
            tag = "bank%d" % number
            return psum.tile([P, BANK], F32, name=tag, tag=tag)

        def words(ap):
            return ap.bitcast(I32)

        idx = lists.tile([P, S // GROUP], U16, name="idx")
        idx2 = lists.tile([P, S // GROUP], U16, name="idx2")
        idx3 = lists.tile([P, S // GROUP], U16, name="idx3")

        tab_sc = sb([P, T], U8, "tab_sc")
        w2_sc_raw = sb([P, 2 * H], U8, "quads1")
        w3_sc = sb([P, 2 * N], U8, "w3_sc")
        v_sc = [sb([P, S], U8, "v_sc%d" % a) for a in range(2)]
        nc.vector.memset(words(tab_sc[32:64, :]), 0)
        nc.vector.memset(words(tab_sc[64:, :]), 0)
        nc.vector.memset(words(w2_sc_raw[:]), 0)

        page = [sb([P, T], F32, "wide%d" % t) for t in range(PACK)]
        w1_raw = [sb([P, PACK * BANK], F32, tag) for tag in ("v_early0", "wide5")]
        tab = [sb([P, T], U32, "wide%d" % (6 + a)) for a in range(2)]
        w2_raw = sb([P, 2 * 2 * H], U8, "quads0")
        w3 = sb([P, 2 * N], U32, "w3")
        trim_sb = sb([P, N // P], F32, "trim")
        w1_quads = [sb([P, PACK * BANK], BF16, "w1_quads%d" % g) for g in range(2)]

        w2 = sb([P, 2 * 2 * H], U8, "w2")
        w2_sc = sb([P, 2 * H], U8, "w2_sc")
        picked_sc_rows = sb([P, S], U8, "picked_sc_rows")
        v = [[None], [sb([P, BANK], U32, "v_early1")]]
        b_pairs = [sb([P, 2 * (S + SKEW)], F32, "b%d" % k) for k in range(SLICES // 2)]

        def pick_words(picked_words, a, h):
            at = h * BANK // GROUP
            nc.vector.tensor_copy(picked_words[:], tab[a][:].indirect(idx[:, at : at + BANK // GROUP]))

        def b_pass(acc, s, a, lo, hi, start, stop):
            w_at = a * H + s * P
            nc.tensor.matmul_mx(
                acc, lhsT=w2[:, 2 * w_at : 2 * (w_at + P)].bitcast(FP4X4),
                lhsT_scale=w2_sc[:, w_at : w_at + P],
                rhs=v[a][lo // BANK][:, lo % BANK : (hi - 1) % BANK + 1].bitcast(FP8X4),
                rhs_scale=v_sc[a][:, lo:hi], start=start, stop=stop,
            )

        def estimate(s, h, number):
            acc = bank(number)
            for a in range(2):
                b_pass(acc[:], s, a, h * BANK, (h + 1) * BANK, a == 0, a == 1)
            b_at = (s % 2) * (S + SKEW) + h * BANK
            nc.scalar.copy(b_pairs[s // 2][:, b_at : b_at + BANK], acc[:])

        def pair_bank(k, lo, hi, number):
            acc = bank(number)[:, : 2 * (hi - lo)]
            for a in range(2):
                for e in range(2):
                    b_pass(acc[:, e * (hi - lo) : (e + 1) * (hi - lo)], 2 * k + e, a, lo, hi, a + e == 0, a + e == 2)
            kept[k, lo] = acc

        def copy_pair_bank(k, lo, hi):
            nc.scalar.copy(
                b_pairs[k][:].rearrange("p (e j) -> p e j", e=2)[:, :, lo:hi],
                kept[k, lo].rearrange("p (e j) -> p e j", e=2),
            )

        kept = {}

        def round_on_gpsimd(rounded, raw):
            nc.gpsimd.tensor_scalar(rounded, raw, 1.0, 0.0, ALU.mult, ALU.add)

        base_planes = base.rearrange("(p t) c -> t p c", t=PACK)
        xs_planes = xs.rearrange("(p t) j -> t p j", t=PACK)

        with tc.tile_pool(name="arrivals", bufs=1) as arrivals:
            block_cuts = [[(0, S)], [(0, S)], [(0, SMALL_BLOCK), (SMALL_BLOCK, S)], [(0, S)]]
            blocks = [
                [arrivals.tile([P, hi - lo], F32, name="xs%d_%d" % (t, lo), align_bytes=64) for lo, hi in block_cuts[t]]
                for t in range(PACK)
            ]

            def load_block(t, i):
                lo, hi = block_cuts[t][i]
                nc.sync.dma_start(blocks[t][i][:], xs_planes[t][:, lo:hi])

            def load_plane(t):
                nc.sync.dma_start(page[t][:], base_planes[t])
                load_block(t, 0)

            def load_w1(g):
                nc.sync.dma_start(
                    w1_raw[g][:].rearrange("p (j r) -> p j r", j=PACK),
                    w1.rearrange("(p j) r -> p j r", j=PACK)[:, :, g * BANK : (g + 1) * BANK],
                )

            def load_scales(scale_tile, scales):
                for q in range(4):
                    nc.sync.dma_start(
                        words(scale_tile[32 * q : 32 * q + 4, :]).rearrange("r (a c) -> r a c", a=2),
                        words(scales[:, 4 * q : 4 * q + 4, :]).rearrange("a r c -> r a c"),
                    )

            def slot(quads, t):
                return quads[:].rearrange("p (c t) -> p c t", t=PACK)[:, :, t]

            def place(t):
                for block, (lo, hi) in zip(blocks[t], block_cuts[t]):
                    nc.vector.tensor_copy(page[t][:].indirect(idx2[:, lo // GROUP : hi // GROUP]), block[:])
                if t == PLANE_ORDER[3]:
                    nc.vector.tensor_copy(slot(quads_tail, t), page[t][:, T - TAIL :])
                else:
                    nc.scalar.copy(slot(quads_tail, t), page[t][:, T - TAIL :])
                if t < 2:
                    round_on_gpsimd(slot(quads_rest, t), page[t][:, BANK : T - TAIL])
                else:
                    for lo, hi in REST_CUTS:
                        nc.scalar.copy(slot(quads_rest, t)[:, lo - BANK : hi - BANK], page[t][:, lo:hi])
                round_on_gpsimd(slot(quads_head, t), page[t][:, :BANK])

            def w1_views(g, t0, t1):
                rounded = w1_quads[g][:].rearrange("p (t m j) -> p m j t", t=PACK, j=PACK)[:, :, :, t0:t1]
                raw = w1_raw[g][:].rearrange("p (j m t) -> p m j t", j=PACK, t=PACK)[:, :, :, t0:t1]
                return rounded, raw

            nc.sync.dma_start(idx[:], offs)
            nc.sync.dma_start(words(tab_sc[:32, :]), words(tab_scales.rearrange("a q t -> (a q) t")))
            nc.sync.dma_start(idx2[:], offs2)
            load_plane(PLANE_ORDER[0])
            load_block(PLANE_ORDER[0], 1)
            nc.sync.dma_start(words(w2_raw[:]).rearrange("p (a c) -> p a c", a=2), words(w2_words).rearrange("a p c -> p a c"))
            load_scales(w2_sc_raw, w2_scales)
            load_plane(PLANE_ORDER[1])

            nc.vector.tensor_copy(picked_sc_rows[:], tab_sc[:].indirect(idx[:]))
            for a in range(2):
                for q in range(4):
                    row = 16 * a + 4 * q
                    nc.sync.dma_start(words(v_sc[a][32 * q : 32 * q + 4, :]), words(picked_sc_rows[row : row + 4, :]))
                if a == 0:
                    load_w1(0)
                    load_plane(PLANE_ORDER[2])

            for x in range(4):
                nc.gpsimd.tensor_copy(
                    w2[:, x * H : (x + 1) * H].bitcast(U16).rearrange("p (t m) -> p t m", t=PACK),
                    w2_raw[:, x * H : (x + 1) * H].bitcast(U16).rearrange("p (m t) -> p t m", t=PACK),
                )
            nc.gpsimd.tensor_copy(
                w2_sc[:].rearrange("p (x t m) -> p x t m", t=PACK, m=P),
                w2_sc_raw[:].rearrange("p (x m t) -> p x t m", t=PACK, m=P),
            )

            quads_head = sb([P, PACK * BANK], BF16, "quads0")
            quads_rest = sb([P, PACK * (T - BANK - TAIL)], BF16, "quads1")
            quads_tail = sb([P, PACK * TAIL], BF16, "quads_tail")
            load_w1(1)
            for a in range(2):
                nc.sync.dma_start(words(tab[a][:]), words(tab_words[a].rearrange("p t i -> p (t i)")))
            load_plane(PLANE_ORDER[3])
            nc.sync.dma_start(idx3[:], offs3)
            nc.sync.dma_start(
                words(w3[:]).rearrange("p (a c) -> p a c", a=2),
                words(w3_words.rearrange("a p c i -> a p (c i)")).rearrange("a p c -> p a c"),
            )
            load_scales(w3_sc, w3_scales)
            with nc.allow_non_contiguous_dma(reason="one trim value a partition"):
                nc.sync.dma_start(trim_sb[:], trim.rearrange("(c p) -> p c", p=P))

            for t in PLANE_ORDER[:2]:
                place(t)
            nc.scalar.activation(*w1_views(0, 0, PACK), ACT.Copy)
            place(PLANE_ORDER[2])
            nc.scalar.activation(*w1_views(1, 0, PACK), ACT.Copy)
            v[0][0] = sb([P, BANK], U32, "v_early0")
            for a in range(2):
                pick_words(v[a][0], a, 0)
            for s in range(EARLY_SLICES):
                estimate(s, 0, s % EARLY_BANKS)
            place(PLANE_ORDER[3])

        picked = ctx.enter_context(tc.tile_pool(name="picked", bufs=1))
        for a in range(2):
            v[a].append(picked.tile([P, BANK], U32, name="v_late%d" % a, align_bytes=64))
        w1_codes = {0: picked.tile([P, P], U32, name="w1_codes0", align_bytes=64)[:]}
        w1_sc = sb([P, H], U8, "w1_sc")
        page_codes = sb([P, T], U32, "page_codes")
        page_sc = sb([P, T], U8, "page_sc")

        def quantise_w1(codes, s0, s1):
            source = w1_quads[s0 // PACK][:, s0 % PACK * BANK : ((s1 - 1) % PACK + 1) * BANK]
            nc.vector.quantize_mx(codes.bitcast(FP8X4), w1_sc[:, s0 * P : s1 * P], source)
            for s in range(s0, s1):
                w1_codes[s] = codes[:, (s - s0) * P : (s - s0 + 1) * P]

        for a in range(2):
            pick_words(v[a][1], a, 1)
        quantise_w1(w1_codes[0], 0, 1)
        def quantise_page(quads, lo, hi):
            nc.vector.quantize_mx(page_codes[:, lo:hi].bitcast(FP8X4), page_sc[:, lo:hi], quads)

        quantise_page(quads_head[:], 0, BANK)
        quantise_page(quads_tail[:], T - TAIL, T)
        for lo, hi in REST_CUTS:
            quantise_page(quads_rest[:, PACK * (lo - BANK) : PACK * (hi - BANK)], lo, hi)
        held_codes = sb([P, 7 * P], U32, "quads1")
        for s0, s1 in ((1, 2), (2, 4), (4, 8)):
            quantise_w1(held_codes[:, (s0 - 1) * P : (s1 - 1) * P], s0, s1)

        a_rows = [sb([P, T], F32, "wide%d" % s) for s in range(SLICES)]

        def gain(s, lo, hi, number):
            cols = slice(lo, hi)
            acc = bank(number)[:, : hi - lo]
            nc.tensor.matmul_mx(
                acc, lhsT=w1_codes[s].bitcast(FP8X4), lhsT_scale=w1_sc[:, s * P : (s + 1) * P],
                rhs=page_codes[:, cols].bitcast(FP8X4), rhs_scale=page_sc[:, cols], start=True, stop=True,
            )
            nc.scalar.copy(a_rows[s][:, cols], acc)

        last_pair = (SLICES - 2, SLICES - 1)
        ranges = [(at, at + BANK) for at in range(0, T, BANK)]

        def gains(s, numbers):
            for (lo, hi), number in zip([(0, BANK), (T - TAIL, T)] + REST_CUTS if s == 0 else ranges, numbers):
                gain(s, lo, hi, number)

        def late_pair(k, numbers):
            for (lo, hi), number in zip(KEPT[2:], numbers):
                pair_bank(k, lo, hi, number)
                copy_pair_bank(k, lo, hi)

        def early_pair_again(k, numbers):
            for (lo, hi), number in zip(KEPT[:2], numbers):
                pair_bank(k, lo, hi, number)

        pair_bank(0, *KEPT[2], 5)
        copy_pair_bank(0, *KEPT[2])
        gains(0, (0, 1, 2, 3, 4))
        pair_bank(0, *KEPT[3], 0)
        nc.scalar.copy(b_pairs[0][:, KEPT[3][0] : S], kept[0, KEPT[3][0]][:, :QUARTER])
        gains(1, (7, 6, 1, 2))
        nc.scalar.copy(b_pairs[0][:, S + SKEW + KEPT[3][0] : 2 * S + SKEW], kept[0, KEPT[3][0]][:, QUARTER:])
        pair_bank(0, *KEPT[1], 4)
        gains(2, (3, 7, 6, 1))
        late_pair(1, (2, 3))

        z_codes = [sb([P, S], U32, "z_codes%d" % g) for g in range(2)]
        z_sc = [sb([P, S], U8, "z_sc%d" % g) for g in range(2)]
        out_rows = out.rearrange("(c p) j -> p c j", p=P)

        def product_tile(lo, hi, tag="prod", bufs=2):
            return sb([P, 2 * (hi - lo + SKEW)], F32, tag, bufs=bufs)

        def pick_product(prod, s, lo, hi, prod_first_col=None):
            at = (s % 2) * (S + SKEW)
            prod_at = (s % 2) * prod.shape[1] // 2 + (0 if prod_first_col is None else lo - prod_first_col)
            nc.vector.tensor_tensor(
                prod[:, prod_at : prod_at + hi - lo],
                a_rows[s][:].indirect(idx3[:, lo // GROUP : hi // GROUP]),
                b_pairs[s // 2][:, at + lo : at + hi],
                ALU.mult,
            )

        def newton(z_pairs, prod, prod_first_col, k, lo, hi):
            nc.vector.scalar_tensor_tensor(
                z_pairs[:].rearrange("p (u j e) -> p u j e", u=2, e=2)[:, k % 2, lo:hi, :],
                prod[:].rearrange("p (e j) -> p j e", e=2)[:, lo - prod_first_col : hi - prod_first_col, :],
                -2.0,
                b_pairs[k][:].rearrange("p (e j) -> p j e", e=2)[:, lo:hi, :],
                ALU.add,
                ALU.mult,
            )

        def weave_z(z_pairs, lo, hi, tag, copy):
            quads = sb([P, PACK * (hi - lo)], BF16, tag)
            copy(
                quads[:].bitcast(F32).rearrange("p (j u) -> p j u", u=2),
                z_pairs[:].bitcast(F32).rearrange("p (u j) -> p j u", u=2)[:, lo:hi, :],
            )
            return quads

        def quantise_z(quads, g, lo, hi):
            nc.vector.quantize_mx(z_codes[g][:, lo:hi].bitcast(FP8X4), z_sc[g][:, lo:hi], quads[:])

        def newton_kept(z_pairs, prod, k, lo, hi):
            first = max(lo, GPSIMD_ENTRIES[k])
            nc.vector.scalar_tensor_tensor(
                z_pairs[:].rearrange("p (u j e) -> p u j e", u=2, e=2)[:, k % 2, first:hi, :],
                prod[:].rearrange("p (e j) -> p j e", e=2)[:, first:hi, :],
                -2.0,
                kept[k, lo].rearrange("p (e j) -> p j e", e=2)[:, first - lo :, :],
                ALU.add,
                ALU.mult,
            )

        def newton_on_gpsimd(z_pairs, prod, k):
            n = GPSIMD_ENTRIES[k]
            factor = sb([P, 2 * n], F32, "factor")
            rows = factor[:].rearrange("p (e j) -> p e j", e=2)
            nc.gpsimd.tensor_scalar(rows, prod[:].rearrange("p (e j) -> p e j", e=2)[:, :, :n], 1.0, -2.0, ALU.mult, ALU.add)
            nc.gpsimd.tensor_tensor(
                z_pairs[:].rearrange("p (u j e) -> p u e j", u=2, e=2)[:, k % 2, :, :n],
                rows,
                b_pairs[k][:].rearrange("p (e j) -> p e j", e=2)[:, :, :n],
                ALU.mult,
            )

        def newton_pair(z_pairs, k):
            prod = pick_pair(k)
            newton_on_gpsimd(z_pairs, prod, k)
            for lo, hi in KEPT[1:] if k == 0 else KEPT:
                newton_kept(z_pairs, prod, k, lo, hi)
            if k == 0:
                newton(z_pairs, prod, 0, k, GPSIMD_ENTRIES[k], QUARTER)

        def project(acc, g, c, lo, hi):
            at = g * N + c * P
            nc.tensor.matmul_mx(
                acc[:, : hi - lo], lhsT=w3[:, at : at + P].bitcast(FP8X4), lhsT_scale=w3_sc[:, at : at + P],
                rhs=z_codes[g][:, lo:hi].bitcast(FP8X4), rhs_scale=z_sc[g][:, lo:hi], start=g == 0, stop=g == 1,
            )

        def pick_pair(k):
            prod = product_tile(0, S)
            first_cuts = [(0, KEPT[3][0]), KEPT[3]]
            for lo, hi in first_cuts if k == 0 else [(0, S)]:
                pick_product(prod, 2 * k, lo, hi, 0)
            for lo, hi in first_cuts if k == 0 else HALVES:
                pick_product(prod, 2 * k + 1, lo, hi, 0)
            return prod

        z_first = sb([P, PACK * S], BF16, "wide0")
        newton_pair(z_first, 0)
        gains(3, (7, 4, 5, 0))
        gains(4, (6, 1, 7, 4))
        early_pair_again(1, (5, 0))
        late_pair(2, (6, 1))
        newton_pair(z_first, 1)
        gains(5, (7, 4, 5, 0))
        early_pair_again(2, (2, 3))
        for s in last_pair:
            gains(s, (7, 4, 5, 0))
        quads_first = weave_z(z_first, 0, S, "page_codes", nc.scalar.copy)
        estimate(last_pair[0], 1, 7)

        z_second = sb([P, PACK * S], BF16, "z_second")
        newton_pair(z_second, 2)

        def newton_into_quads(prod, i):
            lo, hi = PIECES[i]
            nc.vector.scalar_tensor_tensor(
                late_quads[i][:].rearrange("p (j u e) -> p j u e", u=2, e=2)[:, :, 1, :],
                prod[:].rearrange("p (e j) -> p j e", e=2)[:, : hi - lo, :],
                -2.0,
                b_pairs[3][:].rearrange("p (e j) -> p j e", e=2)[:, lo:hi, :],
                ALU.add,
                ALU.mult,
            )

        def last_newton(prod, i, prod_first_col=None):
            lo, hi = PIECES[i]
            newton(z_second, prod, lo if prod_first_col is None else prod_first_col, 3, lo, hi)

        def finish(quads, i):
            lo, hi = PIECES[i]
            accs = [bank(number) for number in ((5, 0, 7, 4), (6, 1, 2, 3))[i % 2]]
            for c in range(N // P):
                project(accs[c], 0, c, lo, hi)
            quantise_z(quads, 1, lo, hi)
            for c in (2, 0, 3, 1) if i == LAST else range(N // P):
                project(accs[c], 1, c, lo, hi)
            staged = sb([P, N // P * (hi - lo)], F32, "wide%d" % (2 + i))
            rows = staged[:].rearrange("p (c j) -> p c j", c=N // P)
            for c in range(N // P):
                sums, offset = accs[c][:, : hi - lo], trim_sb[:, c : c + 1]
                if i == LAST and c >= 2:
                    nc.vector.tensor_scalar(rows[:, c, :], sums, -1.0, offset, ALU.mult, ALU.add)
                else:
                    nc.scalar.activation(rows[:, c, :], sums, ACT.Identity, bias=offset, scale=-1.0)
            if i == LAST:
                for c in (2, 0, 3, 1):
                    (nc.scalar if c == 1 else nc.sync).dma_start(out_rows[:, c, lo:hi], rows[:, c, :])
            else:
                nc.sync.dma_start(out_rows[:, :2, lo:hi], rows[:, :2, :])
                nc.sync.dma_start(out_rows[:, 2:, lo:hi], rows[:, 2:, :])

        first_prod = product_tile(*HALVES[0])
        pick_product(first_prod, last_pair[0], *HALVES[0])
        for i in range(2):
            pick_product(first_prod, last_pair[1], *PIECES[i], 0)
        first_quads = []
        for i in range(2):
            last_newton(first_prod, i, 0)
            first_quads.append(weave_z(z_second, *PIECES[i], "quads%d" % i, nc.scalar.copy))
            if i == 0:
                estimate(last_pair[1], 1, 4)
        late_quads = {}
        for i in range(2, len(PIECES)):
            lo, hi = PIECES[i]
            late_quads[i] = sb([P, PACK * (hi - lo)], BF16, "z_quads%d" % i)
            nc.scalar.copy(
                late_quads[i][:].bitcast(F32).rearrange("p (j u) -> p j u", u=2)[:, :, 0],
                z_second[:].bitcast(F32)[:, lo:hi],
            )
        quantise_z(quads_first, 0, 0, S)
        finish(first_quads[0], 0)

        prod2 = product_tile(*PIECES[2], "page_codes", 1)
        for s in last_pair:
            pick_product(prod2, s, *PIECES[2])
        finish(first_quads[1], 1)
        newton_into_quads(prod2, 2)
        prod3 = product_tile(*PIECES[3], "quads0", 1)
        pick_product(prod3, last_pair[0], *PIECES[3])
        finish(late_quads[2], 2)
        pick_product(prod3, last_pair[1], *PIECES[3])
        prod4 = product_tile(*PIECES[4], "z_quads2", 1)
        pick_product(prod4, last_pair[0], *PIECES[4])
        newton_into_quads(prod3, 3)
        pick_product(prod4, last_pair[1], *PIECES[4])
        finish(late_quads[3], 3)
        newton_into_quads(prod4, 4)
        finish(late_quads[4], 4)
